import numpy as np, ml_dtypes
CORES = [40,41,42,43,44,45,46,47]
N = 8
BF = ml_dtypes.bfloat16
M, Q, CAP, V = 2048, 256, 96, 15
R = 2 ** 20; H = R - 2 ** 13
def shave(lo, hi, u, k):
    return [lo[i] + int((hi[i] - lo[i]) * k * u[3 + i]) for i in range(3)] + [hi[i] - int((hi[i] - lo[i]) * k * u[6 + i]) for i in range(3)]
def scene(rng, h, deep, uneven):
    U = rng.random((M, 12)).tolist(); u = U[0]; side = [int(h * (1 + 0.5 * u[i])) for i in range(3)]
    lo = [int(u[3 + i] * (2 * h - side[i])) - h for i in range(3)]; hi = [lo[i] + side[i] for i in range(3)]
    box = [lo + hi] * M; skip = [M] * M; todo = [(1, M, lo, hi, M, V - 1)]
    while todo:
        a, b, lo, hi, out, v = todo.pop(); u = U[a]; s = b - a
        if s <= 4 or (s <= v and (deep or u[0] < 0.3)):
            for n in range(a, b):
                w = U[n]; box[n] = shave(lo, hi, w, 0.25)
                k = n + 1 if deep or w[2] < 0.5 else n + 1 + int(w[11] * (b - n)); skip[n] = k if k < b else out
            if out > b:
                i = int(u[1] * 3); box[b - 1][3 + i] = box[b - 1][i] - 1
            continue
        c = 5 * 2 ** (v - 5) - 1; x = max(2, s - 1 - c); z = min(s - 3, c)
        m = a + 1 + (V - 2 if deep and a == 1 else x + int(u[9] * (z - x + 1)))
        i = int(u[1] * 3); cut = lo[i] + int((hi[i] - lo[i]) * (0.25 + 0.5 * u[10]))
        l2 = lo[:]; l2[i] = min(cut + 1, hi[i]); h2 = hi[:]; h2[i] = cut
        yes, no = ((lo, h2), (l2, hi)) if u[2] < 0.5 else ((l2, hi), (lo, h2))
        box[a] = shave(yes[0], yes[1], u, 0.125); skip[a] = m
        todo += [(a + 1, m) + yes + (out, v - 1), (m, b) + no + (out, v - 1)]
    w = 2 ** rng.integers(0, 17, M) if uneven else rng.integers(1, 2 ** 16 + 1, M)
    return np.concatenate([np.array(box, np.int64).T, np.array([skip], np.int64), (w * (2 * rng.integers(0, 2, M) - 1))[None]])
def scenes(rng, h, deep=False, uneven=False):
    t = np.zeros((N, 8, 16, M), np.int64)
    for r in range(N):
        for g in range(8):
            t[r, g, :8] = scene(rng, int(h[g]), deep, uneven)
    return t
def points(rng, h):
    h = np.asarray(h, np.int64).reshape(1, 8, 1, 1); return rng.integers(-h, h + 1, (N, 8, 3, Q))
def inbox(t, p):
    return ((t[:, :3, :1] <= p) & (p <= t[:, 3:6, :1])).all(-2)
def far(rng, n):
    return rng.integers(R - 2 ** 12, R + 1, (3, n))
def made(rng, t, p, s=0):
    for r in range(N):
        for q in [(r + s + i) % N for i in range(N)]:
            if q == r: continue
            k = inbox(t[q], p[r])
            for g in range(8):
                i = rng.permutation(np.flatnonzero(k[g]))[CAP:]
                if len(i): p[r, g][:, i] = far(rng, len(i))
    return {"nodes": t.reshape(N, 128, M).astype(np.int32), "pts": p.reshape(N, 24, Q).astype(np.int32)}
def setup_inputs(rng):
    return made(rng, scenes(rng, [H] * 8), points(rng, [H] * 8))
def setup_inputs_faces(rng):
    t = scenes(rng, [H] * 8); p = np.zeros((N, 8, 3, Q), np.int64)
    for g in range(8):
        q = rng.integers(0, N, (N, 1, Q)); n = rng.integers(0, M, (N, 1, Q)) * (rng.random((N, 1, Q)) > 0.25)
        p[:, g] = t[q, g, np.arange(3)[:, None] + 3 * rng.integers(0, 2, (N, 3, Q)), n] + rng.integers(-1, 2, (N, 3, Q))
    return made(rng, t, p)
def setup_inputs_full(rng):
    t = scenes(rng, [H] * 8); p = points(rng, [H] * 8); s = int(rng.integers(1, N))
    for r in range(N):
        b = t[(r + s) % N, :, :6, :1]; p[r] = b[:, :3] + np.floor(rng.random((8, 3, Q)) * (b[:, 3:] - b[:, :3] + 1)).astype(np.int64)
    return made(rng, t, p, s)
def setup_inputs_few(rng):
    t = scenes(rng, [H] * 8); p = points(rng, [H] * 8); o = rng.permutation(N); b, c = o[:2]; e = o[2:]; t[e, :, 3, 0] = t[e, :, 0, 0] - 1
    w = t[c, :, :6, :1]; p[c] = w[:, :3] + np.floor(rng.random((8, 3, Q)) * (w[:, 3:] - w[:, :3] + 1)).astype(np.int64)
    for g in range(8):
        p[b, g] = far(rng, Q); v = t[b, g, :3, 0] + np.floor(rng.random(3) * (t[b, g, 3:6, 0] - t[b, g, :3, 0] + 1)).astype(np.int64)
        p[b, g, :, :4] = v[:, None]; p[b, g, :, Q - 4:] = v[:, None]
    return made(rng, t, p)
def setup_inputs_deep(rng):
    return made(rng, scenes(rng, [H] * 8, deep=True), points(rng, [H] * 8))
def setup_inputs_spread(rng):
    h = 2 ** rng.integers(5, 20, 8); p = points(rng, h)
    return made(rng, scenes(rng, h, uneven=True), p >> (rng.integers(0, 6, (N, 8, 1, Q)) * (rng.random((N, 8, 1, Q)) < 0.25)))
def walk(t, p):
    nd = t.transpose(0, 2, 1); x = p.transpose(0, 1, 3, 2); c = np.zeros((N, 8, Q), np.int64); s = np.zeros_like(c); v = np.zeros_like(c)
    while (c < M).any():
        live = c < M; b = nd[np.arange(8)[:, None], np.minimum(c, M - 1)]
        hit = live & (b[..., :3] <= x).all(-1) & (x <= b[..., 3:6]).all(-1)
        s += hit * b[..., 7]; v += live; c = np.where(live, np.where(hit, c + 1, b[..., 6]), c)
    return s, v
def check_inputs(d):
    t = d["nodes"].astype(np.int64).reshape(N, 8, 16, M); p = d["pts"].astype(np.int64).reshape(N, 8, 3, Q); k = t[:, :, 6]; bad = []
    if (k <= np.arange(M)).any() or (k > M).any() or (k[:, :, 0] != M).any(): return ["skips"]
    if np.abs(t[:, :, :6]).max() > R or np.abs(p).max() > R: bad.append("coordinates")
    if np.abs(t[:, :, 7]).max() > 2 ** 16: bad.append("weights")
    if t[:, :, 8:].any(): bad.append("rows of zeros")
    n = np.stack([np.sum(inbox(t[q], p), axis=-1) for q in range(N)])
    n[np.arange(N), np.arange(N)] = 0
    if n.max() > CAP: bad.append("points in another rank's first box")
    if max(walk(t[q], p)[1].max() for q in range(N)) > V: bad.append("visits")
    return bad
def reference(nodes, pts):
    t = nodes.astype(np.int64).reshape(N, 8, 16, M); p = pts.astype(np.int64).reshape(N, 8, 3, Q); y = np.zeros((N, 8, Q), np.int64)
    for q in range(N):
        y += walk(t[q], p)[0]
    return {"y": y.astype(np.float32)}

@@ -1,0 +1,459 @@
+from concourse.bass import DstId, RemoteDMATransfer
+from concourse.mybir import AluOpType, ActivationFunctionType
+
+N = 8
+M = 2048
+MW = 2056
+STEPS = 14
+BATCH = [(0, 320), (320, 320), (640, 288)]
+ALU = AluOpType
+COPY = ActivationFunctionType.Copy
+RELU = ActivationFunctionType.Relu
+
+SCRATCH = {}
+for _n, _w, _t in (
+        [(n, 1, "float32") for n in ("KF AF U2 V32 UV BASE PEN0 PEN1 TG0 TG1 R1 R2 R3 SG P16 VM V4 V1 W1 W2 W3").split()]
+        + [(n, 1, "int32") for n in "IK AI UI VI BI GI HI16".split()]
+        + [(n, 128, "int32") for n in "SKi Wi".split()]
+        + [(n, 128, "float32") for n in "CJ IRf IDf Wb MS ST Q1 GT".split()]
+        + [(n, 128, "bfloat16") for n in "TRI ONE AX0 SKh SKl Wh Wl HB NB".split()]
+        + [(n, 128, "float16") for n in "IDh L00 L01 L10 L11 SC SX GQ GX".split()]
+        + [(n, 256, "float32") for n in "A0 A1 A2 Y0 Y1 Y2 Y3".split()]
+        + [("SO", 128, "uint16"), ("GO", 128, "uint16"), ("G8", 8, "float32"), ("CM", 8, "bfloat16"),
+           ("C1", 32, "bfloat16"), ("C2", 32, "bfloat16"), ("JT", 16, "float32"), ("N0", 8, "int32"),
+           ("BXi", 8, "int32"), ("BX", 8, "float32"), ("Pi", 256, "int32"), ("PL", 928, "float32"),
+           ("TW", MW, "float32"), ("AX", MW, "bfloat16"), ("F0", 2048, "bfloat16"), ("CP", 7 * 256, "float32"),
+           ("HIT", 1152, "float16"), ("LOT", 1152, "float16"), ("EE", 144, "float32"), ("SS", 72, "float32"),
+           ("SA", 672, "float32"), ("ZZ", 144, "float32"), ("RW0", 288, "float32")]
+        + [("RW%d" % d, 128, "float32") for d in range(1, 8)]):
+    SCRATCH[_n] = ("sbuf", [128, _w], _t)
+for _b in range(3):
+    for _n, _w, _t in (("D1_", 320, "bfloat16"), ("D2_", 320, "bfloat16"), ("OF", 32, "uint16"), ("NX", 32, "float16"),
+                       ("TT", 24, "float32"), ("XT", 32, "float16"), ("WT", 32, "float32")):
+        SCRATCH["%s%d" % (_n, _b)] = ("sbuf", [128, _w], _t)
+PSUM = ["PF", "PR", "PQ", "PS0", "PS1", "PS2", "EX", "AC"]
+for _n in PSUM:
+    SCRATCH[_n] = ("psum", [128, 512], "float32")
+
+DMASEMS = ["dN0", "dP", "dSW", "dT0", "dT1", "dAX", "dY"]
+SEMAPHORES = (["cV", "cA", "cP", "cG", "box", "ls"] + DMASEMS
+              + ["pt%d" % d for d in range(1, 8)] + ["rt%d" % d for d in range(1, 8)])
+
+
+def rank_program(g, core, T, topo):
+    rank = T.rank_of(core)
+    if rank is None:
+        return
+    cores = T.cores
+    queue = {"V": g.vector, "A": g.scalar, "P": g.tensor, "G": g, "S": g.sync}
+    total = {"ls": 0}
+    seen = {}
+    wr, rd = {}, {}
+
+    def await_(q, handles):
+        need = {}
+        for (_, sem, val) in handles:
+            if sem in DMASEMS:
+                val = total[sem]
+            need[sem] = max(need.get(sem, 0), val)
+        for sem in sorted(need):
+            if seen.get((q, sem), 0) < need[sem]:
+                queue[q].wait_ge(T.sem[sem], need[sem])
+                seen[(q, sem)] = need[sem]
+
+    def deps(q, reads, writes):
+        hs = []
+        for t in reads:
+            hs += wr.get(t, [])
+            if t in PSUM:
+                hs += [h for h in rd.get(t, []) if h[0] != q]
+        for t in writes:
+            hs += [h for h in wr.get(t, []) + rd.get(t, []) if h[0] != q]
+        await_(q, hs)
+
+    def note(h, reads, writes, add=False):
+        for t in reads:
+            rd.setdefault(t, []).append(h)
+        for t in writes:
+            if add:
+                wr.setdefault(t, []).append(h)
+            else:
+                wr[t] = [h]
+                rd[t] = []
+
+    def op(q, method, reads, writes, *args, add=False, **kw):
+        deps(q, reads, writes)
+        sem = "c" + q
+        total[sem] = total.get(sem, 0) + 1
+        h = (q, sem, total[sem])
+        method(*args, **kw).then_inc(T.sem[sem], 1)
+        note(h, reads, writes, add)
+
+    def dma(q, sem, out, in_, reads, writes):
+        deps(q, reads, writes)
+        total[sem] = total.get(sem, 0) + 16
+        queue[q].dma_start(out, in_).then_inc(T.sem[sem], 16)
+        note((None, sem, total[sem]), reads, writes)
+
+    v, a, p = g.vector, g.scalar, g.tensor
+
+    def ts(reads, writes, out, in0, s1, s2, *ops):
+        op("V", v.tensor_scalar, reads, writes, out, in0, s1, s2, *ops)
+
+    def tt(reads, writes, out, in0, in1, o):
+        op("V", v.tensor_tensor, reads, writes, out, in0, in1, o)
+
+    def vc(reads, writes, out, in_):
+        op("V", v.tensor_copy, reads, writes, out, in_)
+
+    def turn(x, y, out, in_):
+        op("V", v.transpose, [x], [y], out, in_)
+
+    def fill(tag, ap, c):
+        op("V", v.memset, [], [tag], ap, c)
+
+    def mm(reads, writes, out, lhsT, rhs, start, stop):
+        op("P", p.matmul, reads, writes, out, lhsT, rhs, start, stop)
+
+    def act(reads, writes, out, in_, func, **kw):
+        op("A", a.activation, reads, writes, out, in_, func, **kw)
+
+    dma("S", "dN0", T.N0[:], T.nodes[:, 0:8], [], ["N0"])
+    fill("Pz", T.Pi[:], 0)
+    op("G", g.iota, [], ["IK"], T.IK[:], [[1, 1]], 0, 1)
+    op("G", g.iota, [], ["IRf"], T.IRf[:], [[1, 128]], 0, 0, allow_small_or_imprecise_dtypes=True)
+    for i in range(6):
+        dma("S" if i < 3 else "A", "dP", T.Pi[i::16, :], T.pts[i % 3::3, :], ["Pz"], ["Pi%d" % i])
+    dma("S", "dSW", T.SKi[:], T.nodes[6::16, :], [], ["SKi"])
+    dma("A", "dSW", T.Wi[:], T.nodes[7::16, :], [], ["Wi"])
+    dsts = [cores[(rank + e) % N] for e in range(1, N)]
+    deps("G", ["N0"], [])
+    ids = []
+    for dcore in dsts:
+        rid, pid, _ = topo.addr(dcore)
+        ids.append(DstId(rid=rid, pnc=pid))
+    lanes = len(topo.engines(core, dsts[0]))
+    total["ls"] += lanes
+    g.remote_dma_fused([RemoteDMATransfer(
+        dst_ids=ids, dma_engine_mask=topo.mask(core, dsts[0]), remote_sem=T.sem.box, srcs=[T.N0[:, 0:1]],
+        dsts=[T.BXi[:, N - e:N - e + 1] for e in range(1, N)])], local_sem=T.sem.ls)
+    total["box"] = (N - 1) * lanes
+    note((None, "box", total["box"]), [], ["BXi"])
+    dma("G", "dT0", T.TW[:, 0:1024], T.nodes[:, 0:1024], [], ["TWa"])
+    dma("G", "dT1", T.TW[:, 1024:2048], T.nodes[:, 1024:2048], [], ["TWb"])
+    op("G", g.iota, [], ["CJ"], T.CJ[:], [[0, 8], [-128, 2], [0, 8]], 255, -1, allow_small_or_imprecise_dtypes=True)
+    op("G", g.iota, [], ["AXm"], T.AX[:, 0:M], [[0, M]], 65536, 0, allow_small_or_imprecise_dtypes=True)
+
+    ts(["IK"], ["AI"], T.AI[:], T.IK[:], 15, None, ALU.bitwise_and)
+    vc(["IK"], ["KF"], T.KF[:], T.IK[:])
+    ts(["IK"], ["HI16"], T.HI16[:], T.IK[:], 4, None, ALU.logical_shift_right)
+    vc(["AI"], ["AF"], T.AF[:], T.AI[:])
+    ts(["IK"], ["UI"], T.UI[:], T.IK[:], 5, None, ALU.logical_shift_right)
+    vc(["HI16"], ["P16"], T.P16[:], T.HI16[:])
+    ts(["AF"], ["R1"], T.R1[:], T.AF[:], 2.5, None, ALU.is_gt)
+    ts(["AF"], ["R2"], T.R2[:], T.AF[:], 5.5, -2.0, ALU.is_lt, ALU.mult)
+    ts(["IRf", "P16"], ["G8"], T.G8[:], T.IRf[:, 0:8], T.P16[:, 0:1], None, ALU.is_equal)
+    ts(["AF"], ["VM"], T.VM[:], T.AF[:], 5.5, None, ALU.is_lt)
+    tt(["R1", "R2"], ["R3"], T.R3[:], T.R1[:], T.R2[:], ALU.mult)
+    ts(["IK"], ["VI"], T.VI[:], T.IK[:], 1, 3, ALU.logical_shift_right, ALU.bitwise_and)
+    ts(["IK"], ["BI"], T.BI[:], T.IK[:], 24, None, ALU.bitwise_and)
+    ts(["R3"], ["SG"], T.SG[:], T.R3[:], 1.0, None, ALU.add)
+    ts(["IK"], ["GI"], T.GI[:], T.IK[:], 1, None, ALU.bitwise_and)
+    ts(["G8", "VM"], ["CM"], T.CM[:], T.G8[:], T.VM[:, 0:1], None, ALU.mult)
+    ts(["UI"], ["U2"], T.U2[:], T.UI[:], 2.0, None, ALU.mult)
+    ts(["VI"], ["V32"], T.V32[:], T.VI[:], 32.0, None, ALU.mult)
+    ts(["GI"], ["PEN0"], T.PEN0[:], T.GI[:], 1000.0, None, ALU.mult)
+    ts(["GI"], ["PEN1"], T.PEN1[:], T.GI[:], -1000.0, 1000.0, ALU.mult, ALU.add)
+    tt(["U2", "V32"], ["UV"], T.UV[:], T.U2[:], T.V32[:], ALU.add)
+    ts(["IRf", "KF"], ["TRI"], T.TRI[:], T.IRf[:], T.KF[:, 0:1], None, ALU.is_gt)
+    tt(["UV", "BI"], ["BASE"], T.BASE[:], T.UV[:], T.BI[:], ALU.add)
+    fill("ONE", T.ONE[:], 1.0)
+    tt(["BASE", "PEN0"], ["TG0"], T.TG0[:], T.BASE[:], T.PEN0[:], ALU.add)
+    tt(["BASE", "PEN1"], ["TG1"], T.TG1[:], T.BASE[:], T.PEN1[:], ALU.add)
+    for x in (0, 1):
+        for y in (0, 1):
+            n = "L%d%d" % (x, y)
+            ts(["IRf", "TG%d" % x], [n], T[n][:], T.IRf[:], float(-y), T["TG%d" % x][:, 0:1], ALU.add, ALU.is_equal)
+    ts(["Pi%d" % i for i in range(6)] + ["SG"], ["PL0"], T.PL[:, 0:256], T.Pi[:], T.SG[:, 0:1], None, ALU.mult)
+    vc(["SKi"], ["SKh"], T.SKh[:], T.SKi[:])
+    ts(["Wi"], ["Wb"], T.Wb[:], T.Wi[:], 65536.0, None, ALU.add)
+    fill("C1", T.C1[:], 0.0)
+    vc(["Wb"], ["Wh"], T.Wh[:], T.Wb[:])
+    tt(["SKi", "SKh"], ["SKl"], T.SKl[:], T.SKi[:], T.SKh[:], ALU.subtract)
+    fill("C2", T.C2[:], 0.0)
+    tt(["Wb", "Wh"], ["Wl"], T.Wl[:], T.Wb[:], T.Wh[:], ALU.subtract)
+    for i, n in enumerate(("SKh", "SKl", "Wh", "Wl")):
+        dma("S", "dAX", T.AX[i::16, 0:M], T[n][:], [n, "AXm"], ["AX%d" % i])
+    fill("AXs", T.AX[:, M:MW], 1024.0)
+    AX = ["AXm", "AXs"] + ["AX%d" % i for i in range(4)]
+    act(["TWa", "SG"], ["TWa"], T.TW[:, 0:1024], T.TW[:, 0:1024], COPY, scale=T.SG[:, 0:1])
+    act(["TWb", "SG"], ["TWb"], T.TW[:, 1024:M], T.TW[:, 1024:M], COPY, scale=T.SG[:, 0:1])
+    TW = ["TWa", "TWb", "TWs"]
+
+    def coefficients():
+        await_("V", wr["C1"] + wr["C2"])
+        for (n, q, col, f) in (("C1", 0, "VM", 4096.0), ("C1", 1, "VM", -2048.0), ("C1", 3, "VM", -2048.0),
+                               ("C2", 0, "V4", 2.0 ** -16), ("C2", 1, "W3", 2.0 ** -6), ("C2", 2, "V1", 1.0),
+                               ("C2", 3, "V4", 2.0 ** -6)):
+            ts(["G8", col], [n], T[n][:, q::4], T.G8[:], T[col][:, 0:1], f, ALU.mult, ALU.mult)
+
+    COUNT, POS, EXCH = ["PF", "AC"], ["PR", "PQ"], ["EX", "PS0"]
+
+    def inside(d):
+        ts(["PL0", "BX%d" % min(d, 1)], ["F0_%d" % d], T.F0[:, d * 256:d * 256 + 256], T.PL[:, 0:256], T.BX[:, d:d + 1], None, ALU.is_lt)
+        ps = COUNT[d // 4]
+        for jb in (0, 1):
+            c = d * 16 + jb * 8
+            mm(["F0_%d" % d, "CM"], [ps], T[ps][:, c % 64:c % 64 + 8],
+               T.F0[:, d * 256 + jb * 128:d * 256 + jb * 128 + 128], T.CM[:], True, True)
+
+    def cols(n, k):
+        return T[n][:, 64 * k:64 * k + 64]
+
+    def hits(k):
+        ts([COUNT[k]], ["HB%d" % k], cols("HB", k), T[COUNT[k]][:, 0:64], 0.5, None, ALU.is_lt)
+        ts([COUNT[k]], ["NB%d" % k], cols("NB", k), T[COUNT[k]][:, 0:64], 0.5, None, ALU.is_gt)
+        ps = POS[k]
+        mm(["HB%d" % k, "TRI"], [ps], T[ps][:, 0:64], T.TRI[:], cols("HB", k), True, False)
+        for d in range(4):
+            mm(["HB%d" % k, "ONE"], [ps], T[ps][:, d * 16 + 8:d * 16 + 16], T.ONE[:],
+               T.HB[:, k * 64 + d * 16:k * 64 + d * 16 + 8], False, d == 3)
+
+    def away(k):
+        tt(["NB%d" % k, "CJ"], ["MS%d" % k], cols("MS", k), cols("NB", k), cols("CJ", k), ALU.mult)
+
+    def place(k):
+        tt([POS[k], "MS%d" % k], ["SC%d" % k], cols("SC", k), T[POS[k]][:, 0:64], cols("MS", k), ALU.add)
+
+    def exchange(x, ps, c, n):
+        tag, buf = x
+        for b in range(n):
+            for g0 in (0, 1):
+                for p4 in (0, 1):
+                    m = "L%d%d" % (g0, p4)
+                    mm([tag, m], [ps], T[ps][:, b * 32 + g0 * 16:b * 32 + g0 * 16 + 16], T[m][:],
+                       T[buf][:, c + b * 32 + p4 * 16:c + b * 32 + p4 * 16 + 16], p4 == 0, p4 == 1)
+
+    def swap(k):
+        turn("SC%d" % k, "SX%d" % k, cols("SX", k), cols("SC", k))
+        exchange(("SX%d" % k, "SX"), EXCH[k], 64 * k, 2)
+
+    def back(k):
+        turn(EXCH[k], "ST%d" % k, cols("ST", k), T[EXCH[k]][:, 0:64])
+
+    def list_(k):
+        vc(["ST%d" % k], ["SO%d" % k], cols("SO", k), cols("ST", k))
+
+    def scatter(d):
+        vc(["PL0", "SO%d" % (d // 4)], ["CP%d" % d], T.CP[:, (d - 1) * 256:d * 256].indirect(T.SO[:, d * 16:d * 16 + 16]), T.PL[:, 0:256])
+        deps("G", ["CP%d" % d] + ["RZ%d" % k for k in range(8)], [])
+        dst = cores[(rank + d) % N]
+        rid, pid, _ = topo.addr(dst)
+        total["ls"] += len(topo.engines(core, dst))
+        g.remote_dma(T.PL[:, 256 + 96 * (d - 1):256 + 96 * d], T.CP[:, (d - 1) * 256:(d - 1) * 256 + 96],
+                     T.sem["pt%d" % d], T.sem.ls, pid, rid, topo.mask(core, dst))
+        total["pt%d" % d] = len(topo.engines(cores[(rank - d) % N], core))
+        note((None, "pt%d" % d, total["pt%d" % d]), [], ["PL%d" % d])
+
+    def zero_slot(d):
+        fill("RZ%d" % d, T["RW%d" % d][:, (256 if d == 0 else 96):(288 if d == 0 else 128)], 0.0)
+
+    ts(["N0", "SG"], ["BX0"], T.BX[:, 0:1], T.N0[:, 0:1], T.SG[:, 0:1], None, ALU.mult)
+    inside_0 = len(wr)
+    ts(["BXi", "SG"], ["BX1"], T.BX[:, 1:8], T.BXi[:, 1:8], T.SG[:, 0:1], None, ALU.mult)
+    for d in (0, 1, 2, 3, 4):
+        inside(d)
+    hits(0)
+    inside(5)
+    away(0)
+    inside(6)
+    place(0)
+    inside(7)
+    swap(0)
+    hits(1)
+    away(1)
+    for d in range(8):
+        zero_slot(d)
+    back(0)
+    place(1)
+    list_(0)
+    ts(["AF"], ["W1"], T.W1[:], T.AF[:], 1.5, None, ALU.is_gt)
+    swap(1)
+    scatter(1)
+    back(1)
+    ts(["AF"], ["W2"], T.W2[:], T.AF[:], 3.5, None, ALU.is_lt)
+    list_(1)
+    for d in range(2, 8):
+        scatter(d)
+    ts(["AF"], ["V4"], T.V4[:], T.AF[:], 4.0, None, ALU.is_equal)
+    ts(["AF"], ["V1"], T.V1[:], T.AF[:], 1.5, None, ALU.is_lt)
+    tt(["W1", "W2"], ["W3"], T.W3[:], T.W1[:], T.W2[:], ALU.mult)
+    ts(AX + ["IRf"], ["AX0"], T.AX0[:], T.IRf[:], 0.0, T.AX[:, 0:1], ALU.mult, ALU.add)
+    for b in "012":
+        fill("OF" + b, T["OF" + b][:], 1)
+        fill("PS" + b, T["PS" + b][:, 0:96], 0.0)
+    fill("TWs", T.TW[:, M:MW], 4194304.0)
+    coefficients()
+    for b in "012":
+        ts(["IRf"], ["NX" + b], T["NX" + b][:], T.IRf[:, 0:32], 0.0, 1.0, ALU.mult, ALU.add)
+    ts(["IRf", "KF"], ["IDf"], T.IDf[:], T.IRf[:], T.KF[:, 0:1], None, ALU.is_equal)
+
+    def blocks(b):
+        n = BATCH[b][1]
+        return [(k, k * 128, min(n, k * 128 + 128)) for k in range(3)]
+
+    def sources(lo, hi):
+        return (["PL0"] if lo < 256 else []) + ["PL%d" % d for d in range(1, 8) if lo < 256 + 96 * d and hi > 160 + 96 * d]
+
+    def visit(b, t):
+        lo, n = BATCH[b]
+        offs = T["OF%d" % b][:, 0:n // 16]
+        out, pt = T["D1_%d" % b][:, 0:n], T.PL[:, lo:lo + n]
+        rs, ws = TW + sources(lo, lo + n), ["D1_%d" % b]
+        if t == 1:
+            ts(rs, ws, out, pt, T.TW[:, 1:2], None, ALU.is_lt)
+        else:
+            tt(rs + ["OF%d" % b], ws, out, T.TW[:].indirect(offs), pt, ALU.is_gt)
+        act(AX + ["OF%d" % b], ["D2_%d" % b], T["D2_%d" % b][:, 0:n], T.AX[:].indirect(offs), COPY)
+        for (j, x, y) in blocks(b):
+            out = T["PS%d" % b][0:y - x, j * 32:j * 32 + 32]
+            mm(["D2_%d" % b, "C2"], ["PS%d" % b], out, T["D2_%d" % b][:, x:y], T.C2[:], True, False)
+            mm(["D1_%d" % b, "C1"], ["PS%d" % b], out, T["D1_%d" % b][:, x:y], T.C1[:], False, True)
+
+    def weigh(b):
+        act(["PS%d" % b], ["ZZ%d" % b], T.ZZ[:, b * 48:b * 48 + 48], T["PS%d" % b][:, 1:96:2], RELU)
+
+    def add_up(b, t):
+        if b == 1:
+            mm(["ZZ0", "ZZ1", "IDf"], ["AC"], T.AC[:, 0:96], T.IDf[:], T.ZZ[:, 0:96], t == 0, t == STEPS - 1)
+        if b == 2:
+            mm(["ZZ2", "IDf"], ["PF"], T.PF[:, 0:48], T.IDf[:], T.ZZ[:, 96:144], t == 0, t == STEPS - 1)
+
+    def list_work(s):
+        if s == 0:
+            for k in (0, 1):
+                ts([POS[k]], ["Q1_%d" % k], cols("Q1", k), T[POS[k]][:, 0:64], -96.0, None, ALU.add)
+            ts(["CJ"], ["JT"], T.JT[:], T.CJ[:, 0:16], -1.0, -1.0, ALU.mult, ALU.add)
+            fill("F0z", T.F0[:, 0:1152], 0.0)
+        if s == 1:
+            tt(["Q1_0", "Q1_1", "HB0", "HB1"], ["GQ"], T.GQ[:, 16:128], T.Q1[:, 16:128], T.HB[:, 16:128], ALU.mult)
+            op("V", v.tensor_tensor, ["JT", "HB0"], ["GQ"], T.GQ[:, 0:16], T.JT[:], T.HB[:, 0:16], ALU.mult, add=True)
+            vc(["F0z"], ["HITz"], T.HIT[:], T.F0[:, 0:1152])
+        if s == 2:
+            turn("GQ", "GX", T.GX[:], T.GQ[:])
+            exchange(("GX", "GX"), "PR", 0, 4)
+            vc(["F0z"], ["LOTz"], T.LOT[:], T.F0[:, 0:1152])
+        if s == 4:
+            turn("PR", "GT", T.GT[:], T.PR[:, 0:128])
+        if s == 5:
+            ts(["GT"], ["GO0"], T.GO[:, 0:16], T.GT[:, 0:16], 256.0, None, ALU.add)
+            ts(["GT"], ["GO1"], T.GO[:, 16:128], T.GT[:, 16:128], 96.0, None, ALU.add)
+            ts(["IRf", "KF"], ["IDh"], T.IDh[:], T.IRf[:], T.KF[:, 0:1], None, ALU.is_equal)
+
+    for b in range(3):
+        for (j, x, y) in blocks(b):
+            mm(["AX0", "C2"], ["PS%d" % b], T["PS%d" % b][0:y - x, j * 32:j * 32 + 32], T.AX0[:, 0:y - x], T.C2[:], True, True)
+        weigh(b)
+        add_up(b, 0)
+    for s in range(3 * STEPS):
+        t, b = s // 3 + 1, s % 3
+        t1, b1 = (s - 1) // 3 + 1, (s - 1) % 3
+        t2, b2 = (s - 2) // 3 + 1, (s - 2) % 3
+        go1, go2 = s >= 1 and t1 < STEPS, s >= 2 and t2 < STEPS
+        visit(b, t)
+        ps, nx, tmp, xt = "PS%d" % b1, "NX%d" % b1, "TT%d" % b1, "XT%d" % b1
+        if go1:
+            tt([ps, nx], [tmp], T[tmp][:], T[ps][:, 0:96:4], T[nx][:, 0:24], ALU.add)
+        if go2:
+            turn("EX", "WT%d" % b2, T["WT%d" % b2][:], T.EX[:, 0:32])
+        if go1:
+            tt([ps, tmp], [nx], T[nx][:, 0:24], T[ps][:, 2:96:4], T[tmp][:], ALU.min)
+        if go2:
+            vc(["WT%d" % b2], ["OF%d" % b2], T["OF%d" % b2][:], T["WT%d" % b2][:])
+            weigh(b2)
+        if go1:
+            turn(nx, xt, T[xt][:], T[nx][:])
+            exchange((xt, xt), "EX", 0, 1)
+        if go2:
+            add_up(b2, t2)
+        if s >= 1 and t1 == STEPS:
+            weigh(b1)
+        list_work(s)
+    weigh(2)
+
+    def last_1(b):
+        x = slice(b * 48, b * 48 + 48)
+        acc = T.AC[:, x] if b < 2 else T.PF[:, 0:48]
+        tt(["AC" if b < 2 else "PF", "ZZ%d" % b], ["EE%d" % b], T.EE[:, x], acc, T.ZZ[:, x], ALU.add)
+
+    def last_2(b):
+        tt(["EE%d" % b], ["SS%d" % b], T.SS[:, b * 24:b * 24 + 24], T.EE[:, b * 48:b * 48 + 48:2],
+           T.EE[:, b * 48 + 1:b * 48 + 48:2], ALU.subtract)
+
+    def last_3(b):
+        vc(["SS%d" % b, "HITz"], ["HIT%d" % b], T.HIT[:, b * 384:b * 384 + 384:16], T.SS[:, b * 24:b * 24 + 24])
+
+    def last_4(b):
+        tt(["SS%d" % b, "HIT%d" % b, "LOTz"], ["LOT%d" % b], T.LOT[:, b * 384:b * 384 + 384:16],
+           T.SS[:, b * 24:b * 24 + 24], T.HIT[:, b * 384:b * 384 + 384:16], ALU.subtract)
+
+    def rows(b):
+        ps = "PS%d" % b
+        for (j, x, y) in blocks(b):
+            c = (b * 3 + j) * 128
+            mm(["HIT%d" % b, "IDh"], [ps], T[ps][:, x:y], T.HIT[:, c:c + 128], T.IDh[:, 0:y - x], True, False)
+            mm(["LOT%d" % b, "IDh"], [ps], T[ps][:, x:y], T.LOT[:, c:c + 128], T.IDh[:, 0:y - x], False, True)
+        if b == 0:
+            act([ps], ["SA0"], T.SA[:, 0:64], T[ps][:, 256:320], COPY, scale=64.0)
+            act([ps], ["RV0"], T.RW0[:, 0:256], T[ps][:, 0:256], COPY, scale=64.0)
+        else:
+            lo, n = BATCH[b][0] - 256, BATCH[b][1]
+            act([ps], ["SA%d" % b], T.SA[:, lo:lo + n], T[ps][:, 0:n], COPY, scale=64.0)
+
+    def send(ds, tags, cuts):
+        deps("G", tags, [])
+        trs = []
+        for i, d in enumerate(ds):
+            dst = cores[(rank - d) % N]
+            rid, pid, _ = topo.addr(dst)
+            es = topo.engines(core, dst)[cuts[i]:cuts[i + 1]]
+            trs.append(RemoteDMATransfer(
+                dst_ids=[DstId(rid=rid, pnc=pid)], dma_engine_mask=sum(1 << e for e in es), remote_sem=T.sem["rt%d" % d],
+                srcs=[T.SA[:, 96 * (d - 1):96 * d]], dsts=[T["RW%d" % d][:, 0:96]]))
+            total["ls"] += len(es)
+            total["rt%d" % d] = len(topo.engines(cores[(rank + d) % N], core)[cuts[i]:cuts[i + 1]])
+            note((None, "rt%d" % d, total["rt%d" % d]), [], ["RV%d" % d])
+        g.remote_dma_fused(trs, local_sem=T.sem.ls)
+
+    for f in (last_1, last_2, last_3, last_4):
+        f(0)
+        f(1)
+    rows(0)
+    rows(1)
+    for f in (last_1, last_2, last_3, last_4):
+        f(2)
+    rows(2)
+    send((1, 2, 3, 4), ["SA0", "SA1"], (0, 4, 8, 12, 16))
+    send((5, 6, 7), ["SA2"], (0, 4, 8, 16))
+
+    def sums_of(d):
+        return T["RW%d" % d][:].indirect(T.GO[:, d * 16:d * 16 + 16]), ["RV%d" % d, "RZ%d" % d, "GO%d" % min(d, 1)]
+
+    def plus(d, x, y):
+        win, rs = sums_of(d)
+        tt(rs + [x], [y], T[y][:], win, T[x][:], ALU.add)
+
+    for d in range(3):
+        win, rs = sums_of(d)
+        act(rs, ["A%d" % d], T["A%d" % d][:], win, COPY)
+    plus(3, "A0", "Y0")
+    plus(4, "A1", "Y1")
+    tt(["Y0", "A2"], ["Y2"], T.Y2[:], T.Y0[:], T.A2[:], ALU.add)
+    tt(["Y1", "Y2"], ["Y3"], T.Y3[:], T.Y1[:], T.Y2[:], ALU.add)
+    plus(5, "Y3", "Y0")
+    plus(6, "Y0", "Y1")
+    plus(7, "Y1", "Y2")
+    dma("S", "dY", T.y[:, :], T.Y2[0::16, :], ["Y2"], ["y"])
+    for sem in sorted(total):
+        if max([seen.get((q, sem), 0) for q in queue]) < total[sem]:
+            g.wait_ge(T.sem[sem], total[sem])

@@ -1,43 +1,55 @@
 from concourse.bass import DstId, RemoteDMATransfer
-from concourse.mybir import AluOpType, ActivationFunctionType
+from concourse.mybir import AluOpType, ActivationFunctionType, AxisListType
 
 N = 8
 M = 2048
-MW = 2056
-STEPS = 14
-BATCH = [(0, 320), (320, 320), (640, 288)]
+STEPS = 7
+FIRST = (3, 4, 5, 6, 7)
+BATCH = [(0, 480), (480, 448)]
+OWN = 480
+CW = 448
+RWW = 112
 ALU = AluOpType
 COPY = ActivationFunctionType.Copy
-RELU = ActivationFunctionType.Relu
+IDENT = ActivationFunctionType.Identity
+K, KP, SH = 2.0 ** 22, 4096.0, 1024.0
+C, K0, K6 = 2.0 ** 21, 5.0 * 2 ** 20, 9.0 * 2 ** 18
+FAR = 2.0 ** 22
 
 SCRATCH = {}
 for _n, _w, _t in (
-        [(n, 1, "float32") for n in ("KF AF U2 V32 UV BASE PEN0 PEN1 TG0 TG1 R1 R2 R3 SG P16 VM V4 V1 W1 W2 W3").split()]
-        + [(n, 1, "int32") for n in "IK AI UI VI BI GI HI16".split()]
-        + [(n, 128, "int32") for n in "SKi Wi".split()]
-        + [(n, 128, "float32") for n in "CJ IRf IDf Wb MS ST Q1 GT".split()]
-        + [(n, 128, "bfloat16") for n in "TRI ONE AX0 SKh SKl Wh Wl HB NB".split()]
-        + [(n, 128, "float16") for n in "IDh L00 L01 L10 L11 SC SX GQ GX".split()]
-        + [(n, 256, "float32") for n in "A0 A1 A2 Y0 Y1 Y2 Y3".split()]
-        + [("SO", 128, "uint16"), ("GO", 128, "uint16"), ("G8", 8, "float32"), ("CM", 8, "bfloat16"),
-           ("C1", 32, "bfloat16"), ("C2", 32, "bfloat16"), ("JT", 16, "float32"), ("N0", 8, "int32"),
-           ("BXi", 8, "int32"), ("BX", 8, "float32"), ("Pi", 256, "int32"), ("PL", 928, "float32"),
-           ("TW", MW, "float32"), ("AX", MW, "bfloat16"), ("F0", 2048, "bfloat16"), ("CP", 7 * 256, "float32"),
-           ("HIT", 1152, "float16"), ("LOT", 1152, "float16"), ("EE", 144, "float32"), ("SS", 72, "float32"),
-           ("SA", 672, "float32"), ("ZZ", 144, "float32"), ("RW0", 288, "float32")]
-        + [("RW%d" % d, 128, "float32") for d in range(1, 8)]):
-    SCRATCH[_n] = ("sbuf", [128, _w], _t)
-for _b in range(3):
-    for _n, _w, _t in (("D1_", 320, "bfloat16"), ("D2_", 320, "bfloat16"), ("OF", 32, "uint16"), ("NX", 32, "float16"),
-                       ("TT", 24, "float32"), ("XT", 32, "float16"), ("WT", 32, "float32")):
-        SCRATCH["%s%d" % (_n, _b)] = ("sbuf", [128, _w], _t)
-PSUM = ["PF", "PR", "PQ", "PS0", "PS1", "PS2", "EX", "AC"]
-for _n in PSUM:
-    SCRATCH[_n] = ("psum", [128, 512], "float32")
+        [(n, [1], "float32") for n in "KF RF GF LO3 MID UP SB A0 A1 A2 NM S2 PB NC0 NC1 KF2 R128 BI XE E25 E913 E048".split()]
+        + [(n, [1], "int32") for n in "IK RI GI R8".split()]
+        + [(n, [128], "float32") for n in "IR IDf SEL NI X0B".split()]
+        + [(n, [128], "float16") for n in "IDh TRI ONE DG0 DG1 DN HB".split()]
+        + [(n, [8], "float32") for n in "G8 G8K G8N G87".split()]
+        + [(n, [16], "float32") for n in "OH LB LX TB TX".split()]
+        + [("IDb", [128], "bfloat16"), ("SY", [8], "bfloat16"), ("CM", [16], "bfloat16"), ("CZ", [2, 8], "float32"),
+           ("C1", [2, 56], "bfloat16"), ("C2", [2, 56], "float32"), ("IV", [16, 9], "float32"),
+           ("BXi", [16], "int32"), ("NB", [4], "int32"), ("BX", [4], "float32"), ("Pi", [256], "int32"), ("Pf", [256], "float32"),
+           ("B0", [2, 4, 16], "int32"), ("OT", [128], "int32"), ("OS", [130], "uint16"),
+           ("X", [M + 8], "float32"), ("W1", [M + 8], "float32"), ("W2", [M + 16], "float32"),
+           ("PL", [928], "float32"), ("F0", [1024], "bfloat16"), ("ZL", [1040], "float16"), ("SO", [128], "uint16"),
+           ("GO", [128], "uint16"), ("CP", [7 * CW], "float32"), ("SA", [672], "bfloat16"), ("RW", [7 * RWW], "bfloat16"),
+           ("RO", [272], "bfloat16"), ("GD", [2048], "bfloat16"), ("Y", [256], "float32")]):
+    SCRATCH[_n] = ("sbuf", [128] + _w, _t)
+for _b in range(2):
+    for _n, _w, _t in (("D1_", [480], "bfloat16"), ("D2_", [480], "float32"), ("OF", [32], "uint16"), ("D0_", [224], "float32"),
+                       ("SP", [56, 16], "float32"), ("WS", [224], "float32"), ("Z", [144], "float16"),
+                       ("H", [3, 32], "float32"), ("ZS", [512], "bfloat16")):
+        SCRATCH["%s%d" % (_n, _b)] = ("sbuf", [128] + _w, _t)
+    SCRATCH["PS%d" % _b] = ("psum", [128, 2, 256], "float32")
+for _b in range(6):
+    SCRATCH["Q%d" % _b] = ("psum", [128, 512], "float32")
+PSUM = ["PS0", "PS1"] + ["Q%d" % _b for _b in range(6)]
 
-DMASEMS = ["dN0", "dP", "dSW", "dT0", "dT1", "dAX", "dY"]
+DMASEMS = ["dN", "dP", "dB", "dX", "dW", "dV", "dY"]
 SEMAPHORES = (["cV", "cA", "cP", "cG", "box", "ls"] + DMASEMS
               + ["pt%d" % d for d in range(1, 8)] + ["rt%d" % d for d in range(1, 8)])
+
+
+def slot(d):
+    return 96 * (d - 3) if d in FIRST else (OWN if d == 0 else OWN + 160 + 96 * d)
 
 
 def rank_program(g, core, T, topo):
@@ -81,18 +93,19 @@ def rank_program(g, core, T, topo):
                 wr[t] = [h]
                 rd[t] = []
 
-    def op(q, method, reads, writes, *args, add=False, **kw):
+    def op(q, method, reads, writes, *args, **kw):
         deps(q, reads, writes)
         sem = "c" + q
         total[sem] = total.get(sem, 0) + 1
-        h = (q, sem, total[sem])
         method(*args, **kw).then_inc(T.sem[sem], 1)
-        note(h, reads, writes, add)
+        note((q, sem, total[sem]), reads, writes)
 
-    def dma(q, sem, out, in_, reads, writes):
-        deps(q, reads, writes)
-        total[sem] = total.get(sem, 0) + 16
-        queue[q].dma_start(out, in_).then_inc(T.sem[sem], 16)
+    def dmas(sem, reads, writes, moves):
+        for q in sorted(set(m[0] for m in moves)):
+            deps(q, reads, writes)
+        for (q, out, in_) in moves:
+            total[sem] = total.get(sem, 0) + 16
+            queue[q].dma_start(out, in_).then_inc(T.sem[sem], 16)
         note((None, sem, total[sem]), reads, writes)
 
     v, a, p = g.vector, g.scalar, g.tensor
@@ -106,9 +119,6 @@ def rank_program(g, core, T, topo):
     def vc(reads, writes, out, in_):
         op("V", v.tensor_copy, reads, writes, out, in_)
 
-    def turn(x, y, out, in_):
-        op("V", v.transpose, [x], [y], out, in_)
-
     def fill(tag, ap, c):
         op("V", v.memset, [], [tag], ap, c)
 
@@ -118,342 +128,313 @@ def rank_program(g, core, T, topo):
     def act(reads, writes, out, in_, func, **kw):
         op("A", a.activation, reads, writes, out, in_, func, **kw)
 
-    dma("S", "dN0", T.N0[:], T.nodes[:, 0:8], [], ["N0"])
-    fill("Pz", T.Pi[:], 0)
+    def col(n):
+        return T[n][:, 0:1]
+
+    def ids(ranks):
+        return [DstId(rid=topo.addr(cores[r % N])[0], pnc=topo.addr(cores[r % N])[1]) for r in ranks]
+
+    def lanes(other, lo, hi):
+        return topo.engines(core, cores[other % N])[lo:hi]
+
+    dmas("dN", [], ["BXa", "NB"], [("S", T.BXi[:, 0:2], T.nodes[:, 0:2]), ("A", T.NB[8:128, 0:2], T.nodes[0:120, 0:2]),
+                                   ("A", T.NB[0:8, 0:2], T.nodes[8:16, 0:2])])
+    dmas("dP", [], ["Pi"], [("S", T.Pi[0:24, :], T.pts[:, :])])
+    dmas("dB", [], ["B0"], [("S", T.B0[:, i], T.nodes[6 + 16 * i::32, :]) for i in (0, 1)])
     op("G", g.iota, [], ["IK"], T.IK[:], [[1, 1]], 0, 1)
-    op("G", g.iota, [], ["IRf"], T.IRf[:], [[1, 128]], 0, 0, allow_small_or_imprecise_dtypes=True)
-    for i in range(6):
-        dma("S" if i < 3 else "A", "dP", T.Pi[i::16, :], T.pts[i % 3::3, :], ["Pz"], ["Pi%d" % i])
-    dma("S", "dSW", T.SKi[:], T.nodes[6::16, :], [], ["SKi"])
-    dma("A", "dSW", T.Wi[:], T.nodes[7::16, :], [], ["Wi"])
-    dsts = [cores[(rank + e) % N] for e in range(1, N)]
-    deps("G", ["N0"], [])
-    ids = []
-    for dcore in dsts:
-        rid, pid, _ = topo.addr(dcore)
-        ids.append(DstId(rid=rid, pnc=pid))
-    lanes = len(topo.engines(core, dsts[0]))
-    total["ls"] += lanes
-    g.remote_dma_fused([RemoteDMATransfer(
-        dst_ids=ids, dma_engine_mask=topo.mask(core, dsts[0]), remote_sem=T.sem.box, srcs=[T.N0[:, 0:1]],
-        dsts=[T.BXi[:, N - e:N - e + 1] for e in range(1, N)])], local_sem=T.sem.ls)
-    total["box"] = (N - 1) * lanes
+    op("G", g.iota, [], ["IR"], T.IR[:], [[1, 128]], 0, 0, allow_small_or_imprecise_dtypes=True)
+    op("G", g.iota, [], ["IV"], T.IV[0:32], [[3, 8], [0, 6], [1, 3]], 0, -1, allow_small_or_imprecise_dtypes=True)
+    deps("G", ["BXa", "NB"], [])
+    trs = []
+    for (src, ds, at, lo) in ((T.BXi[:, 0:1], (2, 4, 6), 0, 0), (T.NB[:, 0:1], (1, 3, 5, 7), 8, 8)):
+        es = lanes(rank - ds[0], lo, lo + 8)
+        trs.append(RemoteDMATransfer(
+            dst_ids=ids([rank - d for d in ds]), dma_engine_mask=sum(1 << e for e in es), remote_sem=T.sem.box, srcs=[src],
+            dsts=[T.BXi[:, (d if at == 0 else at + d // 2):(d if at == 0 else at + d // 2) + 1] for d in ds]))
+        total["ls"] += len(es)
+        total["box"] = total.get("box", 0) + len(ds) * len(es)
+    g.remote_dma_fused(trs, local_sem=T.sem.ls)
     note((None, "box", total["box"]), [], ["BXi"])
-    dma("G", "dT0", T.TW[:, 0:1024], T.nodes[:, 0:1024], [], ["TWa"])
-    dma("G", "dT1", T.TW[:, 1024:2048], T.nodes[:, 1024:2048], [], ["TWb"])
-    op("G", g.iota, [], ["CJ"], T.CJ[:], [[0, 8], [-128, 2], [0, 8]], 255, -1, allow_small_or_imprecise_dtypes=True)
-    op("G", g.iota, [], ["AXm"], T.AX[:, 0:M], [[0, M]], 65536, 0, allow_small_or_imprecise_dtypes=True)
+    dmas("dX", [], ["Xa"], [("G", T.X[:, 0:M], T.nodes[:, :])])
 
-    ts(["IK"], ["AI"], T.AI[:], T.IK[:], 15, None, ALU.bitwise_and)
+    fill("ZL", T.ZL[:], 0.0)
+    ts(["IK"], ["RI"], T.RI[:], T.IK[:], 15, None, ALU.bitwise_and)
+    ts(["IK"], ["GI"], T.GI[:], T.IK[:], 4, None, ALU.logical_shift_right)
+    ts(["IK"], ["R8"], T.R8[:], T.IK[:], 7, None, ALU.bitwise_and)
     vc(["IK"], ["KF"], T.KF[:], T.IK[:])
-    ts(["IK"], ["HI16"], T.HI16[:], T.IK[:], 4, None, ALU.logical_shift_right)
-    vc(["AI"], ["AF"], T.AF[:], T.AI[:])
-    ts(["IK"], ["UI"], T.UI[:], T.IK[:], 5, None, ALU.logical_shift_right)
-    vc(["HI16"], ["P16"], T.P16[:], T.HI16[:])
-    ts(["AF"], ["R1"], T.R1[:], T.AF[:], 2.5, None, ALU.is_gt)
-    ts(["AF"], ["R2"], T.R2[:], T.AF[:], 5.5, -2.0, ALU.is_lt, ALU.mult)
-    ts(["IRf", "P16"], ["G8"], T.G8[:], T.IRf[:, 0:8], T.P16[:, 0:1], None, ALU.is_equal)
-    ts(["AF"], ["VM"], T.VM[:], T.AF[:], 5.5, None, ALU.is_lt)
-    tt(["R1", "R2"], ["R3"], T.R3[:], T.R1[:], T.R2[:], ALU.mult)
-    ts(["IK"], ["VI"], T.VI[:], T.IK[:], 1, 3, ALU.logical_shift_right, ALU.bitwise_and)
-    ts(["IK"], ["BI"], T.BI[:], T.IK[:], 24, None, ALU.bitwise_and)
-    ts(["R3"], ["SG"], T.SG[:], T.R3[:], 1.0, None, ALU.add)
-    ts(["IK"], ["GI"], T.GI[:], T.IK[:], 1, None, ALU.bitwise_and)
-    ts(["G8", "VM"], ["CM"], T.CM[:], T.G8[:], T.VM[:, 0:1], None, ALU.mult)
-    ts(["UI"], ["U2"], T.U2[:], T.UI[:], 2.0, None, ALU.mult)
-    ts(["VI"], ["V32"], T.V32[:], T.VI[:], 32.0, None, ALU.mult)
-    ts(["GI"], ["PEN0"], T.PEN0[:], T.GI[:], 1000.0, None, ALU.mult)
-    ts(["GI"], ["PEN1"], T.PEN1[:], T.GI[:], -1000.0, 1000.0, ALU.mult, ALU.add)
-    tt(["U2", "V32"], ["UV"], T.UV[:], T.U2[:], T.V32[:], ALU.add)
-    ts(["IRf", "KF"], ["TRI"], T.TRI[:], T.IRf[:], T.KF[:, 0:1], None, ALU.is_gt)
-    tt(["UV", "BI"], ["BASE"], T.BASE[:], T.UV[:], T.BI[:], ALU.add)
+    vc(["RI"], ["RF"], T.RF[:], T.RI[:])
+    vc(["GI"], ["GF"], T.GF[:], T.GI[:])
+    ts(["R8"], ["LO3"], T.LO3[:], T.R8[:], 2.5, 2.0, ALU.is_lt, ALU.mult)
+    ts(["R8"], ["MID"], T.MID[:], T.R8[:], 5.5, None, ALU.is_lt)
+    ts(["RI"], ["UP"], T.UP[:], T.RI[:], 7.5, None, ALU.is_gt)
+    ts(["R8"], ["NM"], T.NM[:], T.R8[:], 5.5, None, ALU.is_gt)
+    vc(["Pi"], ["Pf"], T.Pf[0:24, :], T.Pi[0:24, :])
+    ts(["IV"], ["SEL"], T.SEL[0:24, :], T.IV[0:24, :, 0:8], 0.0, None, ALU.is_equal)
+    mm(["SEL", "Pf"], ["Q0"], T.Q0[:, 0:256], T.SEL[0:24, :], T.Pf[0:24, :], True, True)
+    tt(["LO3", "MID"], ["SB"], T.SB[:], T.LO3[:], T.MID[:], ALU.subtract)
+    ts(["UP"], ["S2"], T.S2[:], T.UP[:], -2.0, 1.0, ALU.mult, ALU.add)
+    ts(["IR", "GF"], ["G8"], T.G8[:], T.IR[:, 0:8], col("GF"), None, ALU.is_equal)
+    ts(["IR", "RF"], ["OH"], T.OH[:], T.IR[:, 0:16], col("RF"), None, ALU.is_equal)
+    tt(["NM", "S2"], ["A2"], T.A2[:], T.NM[:], T.S2[:], ALU.mult)
+    tt(["SB", "UP"], ["A1"], T.A1[:], T.SB[:], T.UP[:], ALU.mult)
+    ts(["IR", "KF"], ["IDf"], T.IDf[:], T.IR[:], col("KF"), None, ALU.is_equal)
+    ts(["SB", "A2"], ["PB"], T.PB[:], T.SB[:], col("A2"), 0.5, ALU.add, ALU.mult)
+    tt(["SB", "A1"], ["A0"], T.A0[:], T.SB[:], T.A1[:], ALU.subtract)
+    ts(["KF"], ["NC0"], T.NC0[:], T.KF[:], 96.0, -1.0, ALU.add, ALU.mult)
+    ts(["KF"], ["NC1"], T.NC1[:], T.KF[:], 224.0, -1.0, ALU.add, ALU.mult)
+    act(["Q0", "PB"], ["PL0"], T.PL[:, OWN:OWN + 256], T.Q0[:, 0:256], IDENT, bias=col("PB"))
+    for (n, s) in (("IDh", 1.0), ("DG0", col("NC0")), ("DG1", col("NC1")), ("DN", -256.0), ("IDb", 1.0)):
+        act(["IDf", "NC0", "NC1"], [n], T[n][:], T.IDf[:], COPY, scale=s)
+    ts(["G8", "A1"], ["CM1"], T.CM[:, 8:16], T.G8[:], col("A1"), None, ALU.mult)
+    ts(["IR", "KF"], ["TRI"], T.TRI[:], T.IR[:], col("KF"), None, ALU.is_gt)
+    ts(["G8", "A0"], ["CM0"], T.CM[:, 0:8], T.G8[:], col("A0"), None, ALU.mult)
     fill("ONE", T.ONE[:], 1.0)
-    tt(["BASE", "PEN0"], ["TG0"], T.TG0[:], T.BASE[:], T.PEN0[:], ALU.add)
-    tt(["BASE", "PEN1"], ["TG1"], T.TG1[:], T.BASE[:], T.PEN1[:], ALU.add)
-    for x in (0, 1):
-        for y in (0, 1):
-            n = "L%d%d" % (x, y)
-            ts(["IRf", "TG%d" % x], [n], T[n][:], T.IRf[:], float(-y), T["TG%d" % x][:, 0:1], ALU.add, ALU.is_equal)
-    ts(["Pi%d" % i for i in range(6)] + ["SG"], ["PL0"], T.PL[:, 0:256], T.Pi[:], T.SG[:, 0:1], None, ALU.mult)
-    vc(["SKi"], ["SKh"], T.SKh[:], T.SKi[:])
-    ts(["Wi"], ["Wb"], T.Wb[:], T.Wi[:], 65536.0, None, ALU.add)
-    fill("C1", T.C1[:], 0.0)
-    vc(["Wb"], ["Wh"], T.Wh[:], T.Wb[:])
-    tt(["SKi", "SKh"], ["SKl"], T.SKl[:], T.SKi[:], T.SKh[:], ALU.subtract)
-    fill("C2", T.C2[:], 0.0)
-    tt(["Wb", "Wh"], ["Wl"], T.Wl[:], T.Wb[:], T.Wh[:], ALU.subtract)
-    for i, n in enumerate(("SKh", "SKl", "Wh", "Wl")):
-        dma("S", "dAX", T.AX[i::16, 0:M], T[n][:], [n, "AXm"], ["AX%d" % i])
-    fill("AXs", T.AX[:, M:MW], 1024.0)
-    AX = ["AXm", "AXs"] + ["AX%d" % i for i in range(4)]
-    act(["TWa", "SG"], ["TWa"], T.TW[:, 0:1024], T.TW[:, 0:1024], COPY, scale=T.SG[:, 0:1])
-    act(["TWb", "SG"], ["TWb"], T.TW[:, 1024:M], T.TW[:, 1024:M], COPY, scale=T.SG[:, 0:1])
-    TW = ["TWa", "TWb", "TWs"]
+    for i in range(4):
+        op("V", v.transpose, ["B0"], ["OT%d" % i], T.OT[:, i::4], T.B0[:, :, i, :])
+    fill("OSe", T.OS[:, 128:130], M)
+    fill("LX", T.LX[:], 0.0)
+    fill("LB", T.LB[:], 0.0)
+    vc(["OT%d" % i for i in range(4)], ["OS"], T.OS[:, 0:128], T.OT[:])
+    await_("V", wr["LX"] + wr["LB"])
+    for (x, y, c) in ((0, 6, FAR), (6, 7, M + 1.0), (10, 12, M + 0.0), (14, 15, M + 0.0)):
+        fill("LX%d" % x, T.LX[:, x:y], c)
+    for (r, c) in ((2, 2.0 ** 23), (6, -SH), (8, -C), (9, -6 * K6), (10, 1 - SH), (11, -SH - 3 * KP), (12, 3 * K0 - C),
+                   (14, 2 - SH + 6 * KP), (15, -2.5 * KP)):
+        fill("LB%d" % r, T.LB[:, r:r + 1], c)
+    ts(["RF"], ["R128"], T.R128[:], T.RF[:], 128.0, None, ALU.mult)
+    tt(["OH", "LX14"], ["TX"], T.TX[:], T.OH[:], T.LX[:], ALU.mult)
+    tt(["OH", "LB15"], ["TB"], T.TB[:], T.OH[:], T.LB[:], ALU.mult)
+    ts(["IR", "R128"], ["NI"], T.NI[:], T.IR[:], col("R128"), None, ALU.add)
+    op("V", v.tensor_reduce, ["TX"], ["XE"], T.XE[:], T.TX[:], AxisListType.X, ALU.add)
+    op("V", v.tensor_reduce, ["TB"], ["BI"], T.BI[:], T.TB[:], AxisListType.X, ALU.add)
+    for d in range(1, 8):
+        fill("CPz%d" % d, T.CP[:, (d - 1) * CW:(d - 1) * CW + 96], 0.0)
+    ts(["IR", "XE"], ["Xe"], T.X[:, M:M + 8], T.IR[:, 0:8], 0.0, col("XE"), ALU.mult, ALU.add)
+    fill("RZ", T.RW[:], 0.0)
+    fill("RO", T.RO[:, 256:272], 0.0)
+    act(["G8"], ["G8K"], T.G8K[:], T.G8[:], COPY, scale=K)
+    act(["G8"], ["G8N"], T.G8N[:], T.G8[:], COPY, scale=-1.0)
+    act(["OH"], ["E913"], T.E913[:], T.OH[:, 9:10], IDENT, bias=T.OH[:, 13:14])
+    act(["OH"], ["E25"], T.E25[:], T.OH[:, 2:3], IDENT, bias=T.OH[:, 5:6])
+    for (t, n, r) in ((2, "G8N", 6), (3, "G8", 10), (4, "G8", 15), (5, "G8", 11), (9, "G8", 8), (10, "G8", 7), (11, "G8N", 12),
+                      (6, "G8N", 14), (0, "G8K", 5), (1, "G8K", 2), (7, "G8K", 5), (8, "G8K", 2)):
+        act([n, "OH"], ["C2_%d" % t], T.C2[:, t // 7, t % 7::7], T[n][:], COPY, scale=T.OH[:, r:r + 1])
+    act(["G8"], ["C2_13"], T.C2[:, 1, 6::7], T.G8[:], COPY, scale=0.0)
+    act(["G8", "E913"], ["C2"], T.C2[:, 1, 5::7], T.G8[:], COPY, scale=col("E913"))
+    act(["G8K", "E25"], ["CZ0"], T.CZ[:, 0], T.G8K[:], COPY, scale=col("E25"))
+    act(["G8K", "OH"], ["CZ"], T.CZ[:, 1], T.G8K[:], COPY, scale=T.OH[:, 2:3])
+    act(["G8", "OH"], ["G87"], T.G87[:], T.G8[:], COPY, scale=T.OH[:, 7:8])
 
-    def coefficients():
-        await_("V", wr["C1"] + wr["C2"])
-        for (n, q, col, f) in (("C1", 0, "VM", 4096.0), ("C1", 1, "VM", -2048.0), ("C1", 3, "VM", -2048.0),
-                               ("C2", 0, "V4", 2.0 ** -16), ("C2", 1, "W3", 2.0 ** -6), ("C2", 2, "V1", 1.0),
-                               ("C2", 3, "V4", 2.0 ** -6)):
-            ts(["G8", col], [n], T[n][:, q::4], T.G8[:], T[col][:, 0:1], f, ALU.mult, ALU.mult)
+    X = ["Xa", "Xe"]
+    act(X + ["OS", "OSe"], ["W2"], T.W2[:], T.X[:].indirect(T.OS[:, 0:129]), COPY)
+    dmas("dW", X, ["W1a"], [("S", T.W1[r + 8 * i::16, 0:M + 2], T.X[r::16, i:M + 2 + i]) for i in (0, 1) for r in range(6)])
+    dmas("dV", X + ["W2", "NI"], ["W1b", "W2b"],
+         [("S" if i % 2 else "A", out, in_) for i, (out, in_) in enumerate(
+             [(T.W1[r::16, 0:M + 2], T.W2[x::16, 0:M + 2]) for (r, x) in ((6, 0), (7, 1), (14, 3), (15, 4))]
+             + [(T.W2[r::16, 0:M], T.X[x::16, i:M + i]) for (r, x, i) in ((9, 7, 0), (10, 6, 0), (11, 6, 1), (12, 7, 0), (13, 7, 1))]
+             + [(T.W2[14::16, 0:M], T.NI[:])])])
+    act(["Xa", "IR"], ["X0B"], T.X0B[:], T.IR[:], IDENT, scale=0.0, bias=T.X[:, 0:1])
+    W1, W2 = ["W1a", "W1b"], ["W2", "W2b"]
 
-    COUNT, POS, EXCH = ["PF", "AC"], ["PR", "PQ"], ["EX", "PS0"]
+    tt(["BXa", "BXi"], ["BX"], T.BX[:], T.BXi[:, 0:8:2], T.BXi[:, 8:12], ALU.add)
+    for e in range(4):
+        ts(["PL0", "BX"], ["F0_%d" % e], T.F0[:, e * 256:e * 256 + 256], T.PL[:, OWN:OWN + 256], T.BX[:, e:e + 1], None, ALU.is_lt)
+        for b in (0, 1):
+            mm(["F0_%d" % e, "CM0", "CM1"], ["Q1"], T.Q1[:, b * 64 + e * 16:b * 64 + e * 16 + 16],
+               T.F0[:, e * 256 + b:e * 256 + 256:2], T.CM[:], True, True)
+    ts(["Q1"], ["HB"], T.HB[:], T.Q1[:, 0:128], -2.5, None, ALU.is_lt)
+    mm(["HB", "TRI"], ["Q2"], T.Q2[:, 8:64], T.TRI[:], T.HB[:, 8:64], True, False)
+    mm(["HB", "DG0"], ["Q2"], T.Q2[:, 8:64], T.DG0[:], T.HB[:, 8:64], False, True)
+    mm(["HB"], ["Q2"], T.Q2[:, 72:128], T.TRI[:], T.HB[:, 72:128], True, False)
+    mm(["HB", "ONE"], ["Q2"], T.Q2[:, 72:128], T.ONE[:], T.HB[:, 8:64], False, False)
+    mm(["HB", "DG1"], ["Q2"], T.Q2[:, 72:128], T.DG1[:], T.HB[:, 72:128], False, True)
+    for b in (0, 1):
+        mm(["HB", "DN"], ["Q2"], T.Q2[:, b * 64:b * 64 + 8], T.DN[:], T.HB[:, b * 64:b * 64 + 8], True, True)
+    ts(["KF"], ["KF2"], T.KF2[:], T.KF[:], 2.0, None, ALU.mult)
+    for b in (0, 1):
+        ts(["Q2", "KF", "ZL"], ["ZL%d" % b], T.ZL[:, 142 + b:1030:16], T.Q2[:, b * 64 + 8:b * 64 + 64], col("KF"), 96.0 + 128 * b,
+           ALU.add, ALU.add)
+    for b in (0, 1):
+        ts(["Q2", "KF2", "ZL"], ["ZO%d" % b], T.ZL[:, 14 + b:128:16], T.Q2[:, b * 64:b * 64 + 8], col("KF2"), 256.0 + b,
+           ALU.add, ALU.add)
 
-    def inside(d):
-        ts(["PL0", "BX%d" % min(d, 1)], ["F0_%d" % d], T.F0[:, d * 256:d * 256 + 256], T.PL[:, 0:256], T.BX[:, d:d + 1], None, ALU.is_lt)
-        ps = COUNT[d // 4]
-        for jb in (0, 1):
-            c = d * 16 + jb * 8
-            mm(["F0_%d" % d, "CM"], [ps], T[ps][:, c % 64:c % 64 + 8],
-               T.F0[:, d * 256 + jb * 128:d * 256 + jb * 128 + 128], T.CM[:], True, True)
+    def places(ds, ps):
+        for d in ds:
+            for i in range(8):
+                mm(["ZL0", "ZL1", "ZO0", "ZO1", "IDh"], [ps], T[ps][:, d * 16:d * 16 + 16],
+                   T.ZL[:, 128 * d + 14 - 2 * i:128 * d + 142 - 2 * i], T.IDh[:, i::8], i == 0, i == 7)
 
-    def cols(n, k):
-        return T[n][:, 64 * k:64 * k + 64]
-
-    def hits(k):
-        ts([COUNT[k]], ["HB%d" % k], cols("HB", k), T[COUNT[k]][:, 0:64], 0.5, None, ALU.is_lt)
-        ts([COUNT[k]], ["NB%d" % k], cols("NB", k), T[COUNT[k]][:, 0:64], 0.5, None, ALU.is_gt)
-        ps = POS[k]
-        mm(["HB%d" % k, "TRI"], [ps], T[ps][:, 0:64], T.TRI[:], cols("HB", k), True, False)
-        for d in range(4):
-            mm(["HB%d" % k, "ONE"], [ps], T[ps][:, d * 16 + 8:d * 16 + 16], T.ONE[:],
-               T.HB[:, k * 64 + d * 16:k * 64 + d * 16 + 8], False, d == 3)
-
-    def away(k):
-        tt(["NB%d" % k, "CJ"], ["MS%d" % k], cols("MS", k), cols("NB", k), cols("CJ", k), ALU.mult)
-
-    def place(k):
-        tt([POS[k], "MS%d" % k], ["SC%d" % k], cols("SC", k), T[POS[k]][:, 0:64], cols("MS", k), ALU.add)
-
-    def exchange(x, ps, c, n):
-        tag, buf = x
-        for b in range(n):
-            for g0 in (0, 1):
-                for p4 in (0, 1):
-                    m = "L%d%d" % (g0, p4)
-                    mm([tag, m], [ps], T[ps][:, b * 32 + g0 * 16:b * 32 + g0 * 16 + 16], T[m][:],
-                       T[buf][:, c + b * 32 + p4 * 16:c + b * 32 + p4 * 16 + 16], p4 == 0, p4 == 1)
-
-    def swap(k):
-        turn("SC%d" % k, "SX%d" % k, cols("SX", k), cols("SC", k))
-        exchange(("SX%d" % k, "SX"), EXCH[k], 64 * k, 2)
-
-    def back(k):
-        turn(EXCH[k], "ST%d" % k, cols("ST", k), T[EXCH[k]][:, 0:64])
-
-    def list_(k):
-        vc(["ST%d" % k], ["SO%d" % k], cols("SO", k), cols("ST", k))
+    def list_(ds, ps):
+        vc([ps], ["SO%d" % d for d in ds], T.SO[:, ds[0] * 16:ds[-1] * 16 + 16], T[ps][:, ds[0] * 16:ds[-1] * 16 + 16])
 
     def scatter(d):
-        vc(["PL0", "SO%d" % (d // 4)], ["CP%d" % d], T.CP[:, (d - 1) * 256:d * 256].indirect(T.SO[:, d * 16:d * 16 + 16]), T.PL[:, 0:256])
-        deps("G", ["CP%d" % d] + ["RZ%d" % k for k in range(8)], [])
+        vc(["PL0", "SO%d" % d, "CPz%d" % d], ["CP%d" % d], T.CP[:, (d - 1) * CW:d * CW].indirect(T.SO[:, d * 16:d * 16 + 16]),
+           T.PL[:, OWN:OWN + 256])
+        deps("G", ["CP%d" % d, "RZ"], [])
         dst = cores[(rank + d) % N]
         rid, pid, _ = topo.addr(dst)
         total["ls"] += len(topo.engines(core, dst))
-        g.remote_dma(T.PL[:, 256 + 96 * (d - 1):256 + 96 * d], T.CP[:, (d - 1) * 256:(d - 1) * 256 + 96],
+        g.remote_dma(T.PL[:, slot(d):slot(d) + 96], T.CP[:, (d - 1) * CW:(d - 1) * CW + 96],
                      T.sem["pt%d" % d], T.sem.ls, pid, rid, topo.mask(core, dst))
         total["pt%d" % d] = len(topo.engines(cores[(rank - d) % N], core))
         note((None, "pt%d" % d, total["pt%d" % d]), [], ["PL%d" % d])
 
-    def zero_slot(d):
-        fill("RZ%d" % d, T["RW%d" % d][:, (256 if d == 0 else 96):(288 if d == 0 else 128)], 0.0)
-
-    ts(["N0", "SG"], ["BX0"], T.BX[:, 0:1], T.N0[:, 0:1], T.SG[:, 0:1], None, ALU.mult)
-    inside_0 = len(wr)
-    ts(["BXi", "SG"], ["BX1"], T.BX[:, 1:8], T.BXi[:, 1:8], T.SG[:, 0:1], None, ALU.mult)
-    for d in (0, 1, 2, 3, 4):
-        inside(d)
-    hits(0)
-    inside(5)
-    away(0)
-    inside(6)
-    place(0)
-    inside(7)
-    swap(0)
-    hits(1)
-    away(1)
-    for d in range(8):
-        zero_slot(d)
-    back(0)
-    place(1)
-    list_(0)
-    ts(["AF"], ["W1"], T.W1[:], T.AF[:], 1.5, None, ALU.is_gt)
-    swap(1)
-    scatter(1)
-    back(1)
-    ts(["AF"], ["W2"], T.W2[:], T.AF[:], 3.5, None, ALU.is_lt)
-    list_(1)
-    for d in range(2, 8):
-        scatter(d)
-    ts(["AF"], ["V4"], T.V4[:], T.AF[:], 4.0, None, ALU.is_equal)
-    ts(["AF"], ["V1"], T.V1[:], T.AF[:], 1.5, None, ALU.is_lt)
-    tt(["W1", "W2"], ["W3"], T.W3[:], T.W1[:], T.W2[:], ALU.mult)
-    ts(AX + ["IRf"], ["AX0"], T.AX0[:], T.IRf[:], 0.0, T.AX[:, 0:1], ALU.mult, ALU.add)
-    for b in "012":
+    places((3,), "Q3")
+    places((4, 5, 6, 7), "Q4")
+    places((0, 1, 2), "Q5")
+    fill("C1", T.C1[:], 0.0)
+    for b in "01":
+        fill("D0_" + b, T["D0_" + b][:], 0.0)
+    list_((3,), "Q3")
+    for b in "01":
         fill("OF" + b, T["OF" + b][:], 1)
-        fill("PS" + b, T["PS" + b][:, 0:96], 0.0)
-    fill("TWs", T.TW[:, M:MW], 4194304.0)
-    coefficients()
-    for b in "012":
-        ts(["IRf"], ["NX" + b], T["NX" + b][:], T.IRf[:, 0:32], 0.0, 1.0, ALU.mult, ALU.add)
-    ts(["IRf", "KF"], ["IDf"], T.IDf[:], T.IRf[:], T.KF[:, 0:1], None, ALU.is_equal)
+    scatter(3)
+    list_((4, 5, 6, 7), "Q4")
+    for b in "01":
+        fill("D0a" + b, T["D0_" + b][:, 0::7], -2.0 ** 60)
+    scatter(4)
+    list_((0, 1, 2), "Q5")
+    for d in (5, 6, 7, 1, 2):
+        scatter(d)
+    for (t, n, c) in ((1, "A2", K * K), (4, "A0", -KP), (5, "A0", -KP), (6, "SB", -KP), (8, "A2", K * K), (11, "A0", -K0),
+                      (12, "SB", -K6)):
+        ts(["G8", n, "C1"], ["C1_%d" % t], T.C1[:, t // 7, t % 7::7], T.G8[:], col(n), c, ALU.mult, ALU.mult)
+    for b in "01":
+        fill("Z" + b, T["Z" + b][:], 0.0)
+        fill("SPz" + b, T["SP" + b][:, 6::7, :], 0.0)
+        fill("ZS" + b, T["ZS" + b][:], 0.0)
 
-    def blocks(b):
-        n = BATCH[b][1]
-        return [(k, k * 128, min(n, k * 128 + 128)) for k in range(3)]
+    def points(b):
+        return ["PL%d" % d for d in (FIRST if b == 0 else (0, 1, 2))]
 
-    def sources(lo, hi):
-        return (["PL0"] if lo < 256 else []) + ["PL%d" % d for d in range(1, 8) if lo < 256 + 96 * d and hi > 160 + 96 * d]
+    def depth(b):
+        lo, n = BATCH[b]
+        ps = "PS%d" % b
+        for j in range(4):
+            mm(points(b) + ["CZ0", "CZ"], [ps], T[ps][0:n // 4, :, 8 * j:8 * j + 8], T.PL[:, lo + j:lo + n:4], T.CZ[:], True, True)
+        for i in (0, 1):
+            act([ps, "D0_%d" % b, "D0a%d" % b], ["D0b%d" % b], T["D0_%d" % b][0:n // 4, 1 + i::7], T[ps][0:n // 4, i, 0:32], COPY)
 
     def visit(b, t):
         lo, n = BATCH[b]
-        offs = T["OF%d" % b][:, 0:n // 16]
-        out, pt = T["D1_%d" % b][:, 0:n], T.PL[:, lo:lo + n]
-        rs, ws = TW + sources(lo, lo + n), ["D1_%d" % b]
-        if t == 1:
-            ts(rs, ws, out, pt, T.TW[:, 1:2], None, ALU.is_lt)
+        offs, of, d1, d2, ps = T["OF%d" % b][:, 0:n // 16], "OF%d" % b, "D1_%d" % b, "D2_%d" % b, "PS%d" % b
+        act(W2 + [of, "BI"], [d2], T[d2][:, 0:n], T.W2[:].indirect(offs), IDENT, bias=col("BI"))
+        if t == 0:
+            ts(W1 + points(b), [d1], T[d1][:, 0:n], T.PL[:, lo:lo + n], T.W1[:, 1:2], None, ALU.is_lt)
         else:
-            tt(rs + ["OF%d" % b], ws, out, T.TW[:].indirect(offs), pt, ALU.is_gt)
-        act(AX + ["OF%d" % b], ["D2_%d" % b], T["D2_%d" % b][:, 0:n], T.AX[:].indirect(offs), COPY)
-        for (j, x, y) in blocks(b):
-            out = T["PS%d" % b][0:y - x, j * 32:j * 32 + 32]
-            mm(["D2_%d" % b, "C2"], ["PS%d" % b], out, T["D2_%d" % b][:, x:y], T.C2[:], True, False)
-            mm(["D1_%d" % b, "C1"], ["PS%d" % b], out, T["D1_%d" % b][:, x:y], T.C1[:], False, True)
+            tt(W1 + points(b) + [of], [d1], T[d1][:, 0:n], T.W1[:, 0:M + 2].indirect(offs), T.PL[:, lo:lo + n], ALU.is_gt)
 
-    def weigh(b):
-        act(["PS%d" % b], ["ZZ%d" % b], T.ZZ[:, b * 48:b * 48 + 48], T["PS%d" % b][:, 1:96:2], RELU)
+    def sums(b, js):
+        n, ps = BATCH[b][1], "PS%d" % b
+        for j in js:
+            out = T[ps][0:n // 4, :, 56 * j:56 * j + 56]
+            mm(["D1_%d" % b, "C1_12"], [ps], out, T["D1_%d" % b][:, j:n:4], T.C1[:], True, False)
+            mm(["D2_%d" % b, "C2"], [ps], out, T["D2_%d" % b][:, j:n:4], T.C2[:], False, True)
+
+    def scan(b, x, out, i, lo, hi):
+        m, ps = BATCH[b][1] // 4, "PS%d" % b
+        op("V", v.tensor_tensor_scan, [ps, "D0b%d" % b, "SPz%d" % b], [x], out, T["D0_%d" % b][0:m, lo:hi],
+           T[ps][0:m, i, lo:hi], 0.0, ALU.subtract, ALU.max)
+
+    def nodes(b):
+        m, z, ex = BATCH[b][1] // 4, "Z%d" % b, "Q%d" % b
+        for j in range(4):
+            scan(b, "SP%d" % b, T["SP%d" % b][0:m, :, j], 0, 56 * j, 56 * j + 56)
+        act(["SP%d" % b, z], [z + "v"], T[z][0:m, 12:140], T["SP%d" % b][0:m, 6::7, :], COPY, scale=-1.0)
+        for i in range(4):
+            mm([z + "v"], [ex], T[ex][:, 0:m // 4], T[z][0:m, 12 - 4 * i:140 - 4 * i], T.IDh[0:m, i:m:4], i == 0, i == 3)
+
+    def weights(b):
+        scan(b, "WS%d" % b, T["WS%d" % b][0:BATCH[b][1] // 4, :], 1, 0, 224)
+
+    def offsets(b):
+        k = BATCH[b][1] // 16
+        ts(["Q%d" % b], ["OF%d" % b], T["OF%d" % b][:, 0:k], T["Q%d" % b][:, 0:k], SH, None, ALU.add)
 
     def add_up(b, t):
-        if b == 1:
-            mm(["ZZ0", "ZZ1", "IDf"], ["AC"], T.AC[:, 0:96], T.IDf[:], T.ZZ[:, 0:96], t == 0, t == STEPS - 1)
-        if b == 2:
-            mm(["ZZ2", "IDf"], ["PF"], T.PF[:, 0:48], T.IDf[:], T.ZZ[:, 96:144], t == 0, t == STEPS - 1)
-
-    def list_work(s):
-        if s == 0:
-            for k in (0, 1):
-                ts([POS[k]], ["Q1_%d" % k], cols("Q1", k), T[POS[k]][:, 0:64], -96.0, None, ALU.add)
-            ts(["CJ"], ["JT"], T.JT[:], T.CJ[:, 0:16], -1.0, -1.0, ALU.mult, ALU.add)
-            fill("F0z", T.F0[:, 0:1152], 0.0)
-        if s == 1:
-            tt(["Q1_0", "Q1_1", "HB0", "HB1"], ["GQ"], T.GQ[:, 16:128], T.Q1[:, 16:128], T.HB[:, 16:128], ALU.mult)
-            op("V", v.tensor_tensor, ["JT", "HB0"], ["GQ"], T.GQ[:, 0:16], T.JT[:], T.HB[:, 0:16], ALU.mult, add=True)
-            vc(["F0z"], ["HITz"], T.HIT[:], T.F0[:, 0:1152])
-        if s == 2:
-            turn("GQ", "GX", T.GX[:], T.GQ[:])
-            exchange(("GX", "GX"), "PR", 0, 4)
-            vc(["F0z"], ["LOTz"], T.LOT[:], T.F0[:, 0:1152])
-        if s == 4:
-            turn("PR", "GT", T.GT[:], T.PR[:, 0:128])
-        if s == 5:
-            ts(["GT"], ["GO0"], T.GO[:, 0:16], T.GT[:, 0:16], 256.0, None, ALU.add)
-            ts(["GT"], ["GO1"], T.GO[:, 16:128], T.GT[:, 16:128], 96.0, None, ALU.add)
-            ts(["IRf", "KF"], ["IDh"], T.IDh[:], T.IRf[:], T.KF[:, 0:1], None, ALU.is_equal)
-
-    for b in range(3):
-        for (j, x, y) in blocks(b):
-            mm(["AX0", "C2"], ["PS%d" % b], T["PS%d" % b][0:y - x, j * 32:j * 32 + 32], T.AX0[:, 0:y - x], T.C2[:], True, True)
-        weigh(b)
-        add_up(b, 0)
-    for s in range(3 * STEPS):
-        t, b = s // 3 + 1, s % 3
-        t1, b1 = (s - 1) // 3 + 1, (s - 1) % 3
-        t2, b2 = (s - 2) // 3 + 1, (s - 2) % 3
-        go1, go2 = s >= 1 and t1 < STEPS, s >= 2 and t2 < STEPS
-        visit(b, t)
-        ps, nx, tmp, xt = "PS%d" % b1, "NX%d" % b1, "TT%d" % b1, "XT%d" % b1
-        if go1:
-            tt([ps, nx], [tmp], T[tmp][:], T[ps][:, 0:96:4], T[nx][:, 0:24], ALU.add)
-        if go2:
-            turn("EX", "WT%d" % b2, T["WT%d" % b2][:], T.EX[:, 0:32])
-        if go1:
-            tt([ps, tmp], [nx], T[nx][:, 0:24], T[ps][:, 2:96:4], T[tmp][:], ALU.min)
-        if go2:
-            vc(["WT%d" % b2], ["OF%d" % b2], T["OF%d" % b2][:], T["WT%d" % b2][:])
-            weigh(b2)
-        if go1:
-            turn(nx, xt, T[xt][:], T[nx][:])
-            exchange((xt, xt), "EX", 0, 1)
-        if go2:
-            add_up(b2, t2)
-        if s >= 1 and t1 == STEPS:
-            weigh(b1)
-        list_work(s)
-    weigh(2)
-
-    def last_1(b):
-        x = slice(b * 48, b * 48 + 48)
-        acc = T.AC[:, x] if b < 2 else T.PF[:, 0:48]
-        tt(["AC" if b < 2 else "PF", "ZZ%d" % b], ["EE%d" % b], T.EE[:, x], acc, T.ZZ[:, x], ALU.add)
-
-    def last_2(b):
-        tt(["EE%d" % b], ["SS%d" % b], T.SS[:, b * 24:b * 24 + 24], T.EE[:, b * 48:b * 48 + 48:2],
-           T.EE[:, b * 48 + 1:b * 48 + 48:2], ALU.subtract)
-
-    def last_3(b):
-        vc(["SS%d" % b, "HITz"], ["HIT%d" % b], T.HIT[:, b * 384:b * 384 + 384:16], T.SS[:, b * 24:b * 24 + 24])
-
-    def last_4(b):
-        tt(["SS%d" % b, "HIT%d" % b, "LOTz"], ["LOT%d" % b], T.LOT[:, b * 384:b * 384 + 384:16],
-           T.SS[:, b * 24:b * 24 + 24], T.HIT[:, b * 384:b * 384 + 384:16], ALU.subtract)
-
-    def rows(b):
-        ps = "PS%d" % b
-        for (j, x, y) in blocks(b):
-            c = (b * 3 + j) * 128
-            mm(["HIT%d" % b, "IDh"], [ps], T[ps][:, x:y], T.HIT[:, c:c + 128], T.IDh[:, 0:y - x], True, False)
-            mm(["LOT%d" % b, "IDh"], [ps], T[ps][:, x:y], T.LOT[:, c:c + 128], T.IDh[:, 0:y - x], False, True)
-        if b == 0:
-            act([ps], ["SA0"], T.SA[:, 0:64], T[ps][:, 256:320], COPY, scale=64.0)
-            act([ps], ["RV0"], T.RW0[:, 0:256], T[ps][:, 0:256], COPY, scale=64.0)
-        else:
-            lo, n = BATCH[b][0] - 256, BATCH[b][1]
-            act([ps], ["SA%d" % b], T.SA[:, lo:lo + n], T[ps][:, 0:n], COPY, scale=64.0)
+        m, ac = BATCH[b][1] // 4, "Q%d" % (2 + b)
+        mm(["WS%d" % b, "IDf"], [ac], T[ac][0:m, 0:32], T.IDf[0:m, 0:m], T["WS%d" % b][0:m, 5::7], t == 0, t == STEPS - 1)
+        if t == 0:
+            for j in range(4):
+                mm(["X0B", "G87"], [ac], T[ac][0:m, 8 * j:8 * j + 8], T.X0B[:, 0:m], T.G87[:], False, False)
 
     def send(ds, tags, cuts):
         deps("G", tags, [])
         trs = []
         for i, d in enumerate(ds):
-            dst = cores[(rank - d) % N]
-            rid, pid, _ = topo.addr(dst)
-            es = topo.engines(core, dst)[cuts[i]:cuts[i + 1]]
+            es = lanes(rank - d, cuts[i], cuts[i + 1])
+            at = slot(d) if d in FIRST else slot(d) - 256
             trs.append(RemoteDMATransfer(
-                dst_ids=[DstId(rid=rid, pnc=pid)], dma_engine_mask=sum(1 << e for e in es), remote_sem=T.sem["rt%d" % d],
-                srcs=[T.SA[:, 96 * (d - 1):96 * d]], dsts=[T["RW%d" % d][:, 0:96]]))
+                dst_ids=ids([rank - d]), dma_engine_mask=sum(1 << e for e in es), remote_sem=T.sem["rt%d" % d],
+                srcs=[T.SA[:, at:at + 96]], dsts=[T.RW[:, (d - 1) * RWW:(d - 1) * RWW + 96]]))
             total["ls"] += len(es)
-            total["rt%d" % d] = len(topo.engines(cores[(rank + d) % N], core)[cuts[i]:cuts[i + 1]])
+            total["rt%d" % d] = len(es)
             note((None, "rt%d" % d, total["rt%d" % d]), [], ["RV%d" % d])
         g.remote_dma_fused(trs, local_sem=T.sem.ls)
 
-    for f in (last_1, last_2, last_3, last_4):
-        f(0)
-        f(1)
-    rows(0)
-    rows(1)
-    for f in (last_1, last_2, last_3, last_4):
-        f(2)
-    rows(2)
-    send((1, 2, 3, 4), ["SA0", "SA1"], (0, 4, 8, 12, 16))
-    send((5, 6, 7), ["SA2"], (0, 4, 8, 16))
+    def pieces(b):
+        n = BATCH[b][1]
+        m, ac, h, zs, row = n // 4, "Q%d" % (2 + b), T["H%d" % b], "ZS%d" % b, "Q%d" % (4 + b)
+        for i, e in enumerate((44, 37, 30)):
+            ts([ac], ["H%d_%d" % (b, i)], h[0:m, i], T[ac][0:m, 0:32], 1.5 * 2.0 ** e, 1.5 * 2.0 ** e, ALU.add, ALU.subtract)
+        for i in (0, 1):
+            tt(["H%d_%d" % (b, i), "H%d_%d" % (b, i + 1), zs], [zs + "_%d" % i], T[zs][0:m, i::16], h[0:m, i + 1], h[0:m, i],
+               ALU.subtract)
+        tt([ac, "H%d_2" % b, zs], [zs + "_2"], T[zs][0:m, 2::16], T[ac][0:m, 0:32], h[0:m, 2], ALU.subtract)
+        for j in range(4):
+            mm([zs + "_0", zs + "_1", zs + "_2", "IDb"], [row], T[row][:, j:n:4], T[zs][0:m, 128 * j:128 * j + 128], T.IDb[0:m, 0:m], True, True)
+        if b == 0:
+            act([row], ["SA0"], T.SA[:, 0:480], T[row][:, 0:480], COPY)
+            send(FIRST, ["SA0"], (0, 4, 8, 12, 14, 16))
+        else:
+            act([row], ["SA1"], T.SA[:, 480:672], T[row][:, 256:448], COPY)
+            send((1, 2), ["SA1"], (0, 8, 16))
+            act([row], ["RV0"], T.RO[:, 0:256], T[row][:, 0:256], COPY)
 
-    def sums_of(d):
-        return T["RW%d" % d][:].indirect(T.GO[:, d * 16:d * 16 + 16]), ["RV%d" % d, "RZ%d" % d, "GO%d" % min(d, 1)]
+    def spare(s):
+        if s == 1:
+            ts(["SO0"], ["GO0"], T.GO[:, 0:16], T.SO[:, 0:16], 256.0, None, ALU.min)
+            ts(["SO%d" % d for d in range(1, 8)], ["GO1"], T.GO[:, 16:128], T.SO[:, 16:128], 96.0, None, ALU.min)
+            op("V", v.tensor_reduce, ["OH"], ["E048"], T.E048[:], T.OH[:, 0:3], AxisListType.X, ALU.add)
+        if s == 2:
+            ts(["G8", "E048"], ["SY"], T.SY[:], T.G8[:], col("E048"), None, ALU.mult)
 
-    def plus(d, x, y):
-        win, rs = sums_of(d)
-        tt(rs + [x], [y], T[y][:], win, T[x][:], ALU.add)
+    depth(0)
+    visit(0, 0)
+    depth(1)
+    for s in range(1, 2 * STEPS + 1):
+        b, t = s % 2, s // 2
+        o, u = 1 - b, (s - 1) // 2
+        if s == 1:
+            sums(o, range(4))
+        if s < 2 * STEPS:
+            visit(b, t)
+            sums(b, (0, 1))
+        if u < STEPS - 1:
+            nodes(o)
+            weights(o)
+            spare(s)
+            sums(b, (2, 3))
+            add_up(o, u)
+            offsets(o)
+        else:
+            weights(o)
+            add_up(o, u)
+            if o == 0:
+                sums(b, (2, 3))
+            pieces(o)
 
-    for d in range(3):
-        win, rs = sums_of(d)
-        act(rs, ["A%d" % d], T["A%d" % d][:], win, COPY)
-    plus(3, "A0", "Y0")
-    plus(4, "A1", "Y1")
-    tt(["Y0", "A2"], ["Y2"], T.Y2[:], T.Y0[:], T.A2[:], ALU.add)
-    tt(["Y1", "Y2"], ["Y3"], T.Y3[:], T.Y1[:], T.Y2[:], ALU.add)
-    plus(5, "Y3", "Y0")
-    plus(6, "Y0", "Y1")
-    plus(7, "Y1", "Y2")
-    dma("S", "dY", T.y[:, :], T.Y2[0::16, :], ["Y2"], ["y"])
+    order = FIRST + (0, 1, 2)
+    for i, d in enumerate(order):
+        win = (T.RO[:] if d == 0 else T.RW[:, (d - 1) * RWW:d * RWW]).indirect(T.GO[:, d * 16:d * 16 + 16])
+        rs, out = ["RV%d" % d, "RZ", "RO", "GO%d" % min(d, 1)], T.GD[:, d * 256:d * 256 + 256]
+        if i % 2 == 0:
+            vc(rs, ["GD%d" % d], out, win)
+        else:
+            act(rs, ["GD%d" % d], out, win, COPY)
+        mm(["GD%d" % d, "SY"], ["Q0"], T.Q0[0:8, 0:256], T.SY[:], out, i == 0, i == 7)
+    vc(["Q0"], ["Y"], T.Y[0:8, :], T.Q0[0:8, 0:256])
+    dmas("dY", ["Y"], ["y"], [("S", T.y[:, :], T.Y[0:8, :])])
     for sem in sorted(total):
         if max([seen.get((q, sem), 0) for q in queue]) < total[sem]:
             g.wait_ge(T.sem[sem], total[sem])

@@ -5,9 +5,11 @@ N = 8
 M = 2048
 STEPS = 7
 FIRST = (3, 4, 5, 6, 7)
+PAIRS = ((3, 4), (5, 6), (7, 1), (2,))
 BATCH = [(0, 480), (480, 448)]
+CUTA = 352
+CUT = 160
 OWN = 480
-CW = 448
 RWW = 112
 ALU = AluOpType
 COPY = ActivationFunctionType.Copy
@@ -15,26 +17,32 @@ IDENT = ActivationFunctionType.Identity
 K, KP, SH = 2.0 ** 22, 4096.0, 1024.0
 C, K0, K6 = 2.0 ** 21, 5.0 * 2 ** 20, 9.0 * 2 ** 18
 FAR = 2.0 ** 22
+UP16 = 1536.0
+Z0 = 4096 * UP16 - 2048
+COLUMNS = "ZH ZL0 ZL1 V2 V3 U0 U1 U2 U4 U5 P5 P6 T0 T1 E25".split()
 
 SCRATCH = {}
 for _n, _w, _t in (
-        [(n, [1], "float32") for n in "KF RF GF LO3 MID UP SB A0 A1 A2 NM S2 PB NC0 NC1 KF2 R128 BI XE E25 E913 E048".split()]
-        + [(n, [1], "int32") for n in "IK RI GI R8".split()]
-        + [(n, [128], "float32") for n in "IR IDf SEL NI X0B".split()]
-        + [(n, [128], "float16") for n in "IDh TRI ONE DG0 DG1 DN HB".split()]
-        + [(n, [8], "float32") for n in "G8 G8K G8N G87".split()]
-        + [(n, [16], "float32") for n in "OH LB LX TB TX".split()]
-        + [("IDb", [128], "bfloat16"), ("SY", [8], "bfloat16"), ("CM", [16], "bfloat16"), ("CZ", [2, 8], "float32"),
-           ("C1", [2, 56], "bfloat16"), ("C2", [2, 56], "float32"), ("IV", [16, 9], "float32"),
+        [(n, [1], "float32") for n in "KF RF GF LO3 MID UP SB A0 A1 A2 NM S2 PB KF2 KF3 R128 BI SC XE E012 N0 N1 T2 G6 R7 QM".split()]
+        + [("CO", [len(COLUMNS)], "float32")]
+        + [(n, [1], "int32") for n in "IK RI GI R8 R3".split()]
+        + [(n, [128], "float32") for n in "IR IDf SEL X0B".split()]
+        + [(n, [128], "float16") for n in "IDh TRI ONE DG DN DS HB HI LO MK D2 MM0 MM1 MM2 MM3".split()]
+        + [(n, [8], "float32") for n in "G8 G8N G87".split()]
+        + [(n, [16], "float32") for n in "OH LB LX LS TB TX TS".split()]
+        + [("IDb", [128], "bfloat16"), ("SY", [8], "bfloat16"), ("CM", [16], "bfloat16"), ("CZ", [16], "float32"),
+           ("C1", [2, 56], "bfloat16"), ("C2", [2, 56], "bfloat16"), ("IV", [16, 9], "float32"), ("SN", [12], "float16"),
            ("BXi", [16], "int32"), ("NB", [4], "int32"), ("BX", [4], "float32"), ("Pi", [256], "int32"), ("Pf", [256], "float32"),
-           ("B0", [2, 4, 16], "int32"), ("OT", [128], "int32"), ("OS", [130], "uint16"),
-           ("X", [M + 8], "float32"), ("W1", [M + 8], "float32"), ("W2", [M + 16], "float32"),
-           ("PL", [928], "float32"), ("F0", [1024], "bfloat16"), ("ZL", [1040], "float16"), ("SO", [128], "uint16"),
-           ("GO", [128], "uint16"), ("CP", [7 * CW], "float32"), ("SA", [672], "bfloat16"), ("RW", [7 * RWW], "bfloat16"),
-           ("RO", [272], "bfloat16"), ("GD", [2048], "bfloat16"), ("Y", [256], "float32")]):
+           ("B0", [2, 4, 16], "int32"), ("OT", [128], "int32"), ("OS", [130], "uint16"), ("NI", [128], "int32"),
+           ("CC", [384], "int32"), ("CL", [384], "int32"), ("G16", [8, 16], "float32"),
+           ("X", [M + 8], "int32"), ("G", [M + 16], "int32"), ("W1", [M + 8], "int32"), ("W2", [M + 8], "int32"),
+           ("PL", [928], "float32"), ("F0", [1024], "bfloat16"), ("ZL", [1040], "float16"), ("LM", [14 * 128], "float16"),
+           ("HM", [14 * 64], "float16"), ("IX", [48], "uint16"), ("GO", [128], "uint16"), ("CP", [672], "float32"),
+           ("SA", [672], "bfloat16"), ("RW", [7 * RWW], "bfloat16"), ("RO", [272], "bfloat16"), ("GD", [2048], "bfloat16"),
+           ("Y", [256], "float32")]):
     SCRATCH[_n] = ("sbuf", [128] + _w, _t)
 for _b in range(2):
-    for _n, _w, _t in (("D1_", [480], "bfloat16"), ("D2_", [480], "float32"), ("OF", [32], "uint16"), ("D0_", [224], "float32"),
+    for _n, _w, _t in (("D1_", [480], "bfloat16"), ("D2_", [480], "float16"), ("OF", [32], "uint16"), ("D0_", [224], "float32"),
                        ("SP", [56, 16], "float32"), ("WS", [224], "float32"), ("Z", [144], "float16"),
                        ("H", [3, 32], "float32"), ("ZS", [512], "bfloat16")):
         SCRATCH["%s%d" % (_n, _b)] = ("sbuf", [128] + _w, _t)
@@ -43,7 +51,7 @@ for _b in range(6):
     SCRATCH["Q%d" % _b] = ("psum", [128, 512], "float32")
 PSUM = ["PS0", "PS1"] + ["Q%d" % _b for _b in range(6)]
 
-DMASEMS = ["dN", "dP", "dB", "dX", "dW", "dV", "dY"]
+DMASEMS = ["dN", "dP", "dB", "dC", "dX", "dL", "dW", "dU", "dV", "dY"]
 SEMAPHORES = (["cV", "cA", "cP", "cG", "box", "ls"] + DMASEMS
               + ["pt%d" % d for d in range(1, 8)] + ["rt%d" % d for d in range(1, 8)])
 
@@ -76,22 +84,19 @@ def rank_program(g, core, T, topo):
     def deps(q, reads, writes):
         hs = []
         for t in reads:
-            hs += wr.get(t, [])
+            hs += wr[t]
             if t in PSUM:
                 hs += [h for h in rd.get(t, []) if h[0] != q]
         for t in writes:
             hs += [h for h in wr.get(t, []) + rd.get(t, []) if h[0] != q]
         await_(q, hs)
 
-    def note(h, reads, writes, add=False):
+    def note(h, reads, writes):
         for t in reads:
             rd.setdefault(t, []).append(h)
         for t in writes:
-            if add:
-                wr.setdefault(t, []).append(h)
-            else:
-                wr[t] = [h]
-                rd[t] = []
+            wr[t] = [h]
+            rd[t] = []
 
     def op(q, method, reads, writes, *args, **kw):
         deps(q, reads, writes)
@@ -129,35 +134,53 @@ def rank_program(g, core, T, topo):
         op("A", a.activation, reads, writes, out, in_, func, **kw)
 
     def col(n):
-        return T[n][:, 0:1]
+        return T.CO[:, COLUMNS.index(n):COLUMNS.index(n) + 1] if n in COLUMNS else T[n][:, 0:1]
 
-    def ids(ranks):
-        return [DstId(rid=topo.addr(cores[r % N])[0], pnc=topo.addr(cores[r % N])[1]) for r in ranks]
+    def row(r):
+        return T.OH[:, r:r + 1]
 
-    def lanes(other, lo, hi):
-        return topo.engines(core, cores[other % N])[lo:hi]
+    def remote(moves, tags):
+        deps("G", tags, [])
+        trs, at = [], 0
+        for (d, sem, src, dst, lanes) in moves:
+            other = cores[(rank + d) % N]
+            es = topo.engines(core, other)[at:at + lanes]
+            at += lanes
+            trs.append(RemoteDMATransfer(dst_ids=[DstId(rid=topo.addr(other)[0], pnc=topo.addr(other)[1])], remote_sem=T.sem[sem],
+                                         dma_engine_mask=sum(1 << e for e in es), srcs=[src], dsts=[dst]))
+            total["ls"] += len(es)
+            total[sem] = len(es)
+        g.remote_dma_fused(trs, local_sem=T.sem.ls)
 
     dmas("dN", [], ["BXa", "NB"], [("S", T.BXi[:, 0:2], T.nodes[:, 0:2]), ("A", T.NB[8:128, 0:2], T.nodes[0:120, 0:2]),
                                    ("A", T.NB[0:8, 0:2], T.nodes[8:16, 0:2])])
     dmas("dP", [], ["Pi"], [("S", T.Pi[0:24, :], T.pts[:, :])])
+    dmas("dC", [], ["CC"], [("A", T.CC[:, 128 * i:128 * i + 128], T.nodes[r::16, :]) for i, r in enumerate((2, 5, 7))])
     dmas("dB", [], ["B0"], [("S", T.B0[:, i], T.nodes[6 + 16 * i::32, :]) for i in (0, 1)])
+    dmas("dX", [], ["Xa"], [("SA"[i % 2], T.X[r::16, 0:M], T.nodes[x::16, :]) for i, (r, x) in enumerate(
+        [(r, r) for r in range(8)] + [(8, 3), (9, 4), (11, 8), (12, 8), (14, 8)])])
     op("G", g.iota, [], ["IK"], T.IK[:], [[1, 1]], 0, 1)
     op("G", g.iota, [], ["IR"], T.IR[:], [[1, 128]], 0, 0, allow_small_or_imprecise_dtypes=True)
     op("G", g.iota, [], ["IV"], T.IV[0:32], [[3, 8], [0, 6], [1, 3]], 0, -1, allow_small_or_imprecise_dtypes=True)
     deps("G", ["BXa", "NB"], [])
     trs = []
-    for (src, ds, at, lo) in ((T.BXi[:, 0:1], (2, 4, 6), 0, 0), (T.NB[:, 0:1], (1, 3, 5, 7), 8, 8)):
-        es = lanes(rank - ds[0], lo, lo + 8)
+    for (src, ds, at) in ((T.BXi[:, 0:1], (2, 4, 6), 0), (T.NB[:, 0:1], (1, 3, 5, 7), 8)):
+        others = [cores[(rank - d) % N] for d in ds]
+        es = topo.engines(core, others[0])[at:at + 8]
         trs.append(RemoteDMATransfer(
-            dst_ids=ids([rank - d for d in ds]), dma_engine_mask=sum(1 << e for e in es), remote_sem=T.sem.box, srcs=[src],
+            dst_ids=[DstId(rid=topo.addr(c)[0], pnc=topo.addr(c)[1]) for c in others], dma_engine_mask=sum(1 << e for e in es),
+            remote_sem=T.sem.box, srcs=[src],
             dsts=[T.BXi[:, (d if at == 0 else at + d // 2):(d if at == 0 else at + d // 2) + 1] for d in ds]))
         total["ls"] += len(es)
         total["box"] = total.get("box", 0) + len(ds) * len(es)
     g.remote_dma_fused(trs, local_sem=T.sem.ls)
     note((None, "box", total["box"]), [], ["BXi"])
-    dmas("dX", [], ["Xa"], [("G", T.X[:, 0:M], T.nodes[:, :])])
+    op("G", g.iota, [], ["G16"], T.G16[:], [[1, 8], [0, 16]], 0, 0, allow_small_or_imprecise_dtypes=True)
 
-    fill("ZL", T.ZL[:], 0.0)
+    fill("HM", T.HM[:], 0.0)
+    fill("W1e", T.W1[:, M - 8:M + 8], FAR)
+    fill("W2e", T.W2[:, M:M + 8], M)
+    fill("LX", T.LX[:], 0.0)
     ts(["IK"], ["RI"], T.RI[:], T.IK[:], 15, None, ALU.bitwise_and)
     ts(["IK"], ["GI"], T.GI[:], T.IK[:], 4, None, ALU.logical_shift_right)
     ts(["IK"], ["R8"], T.R8[:], T.IK[:], 7, None, ALU.bitwise_and)
@@ -168,213 +191,249 @@ def rank_program(g, core, T, topo):
     ts(["R8"], ["MID"], T.MID[:], T.R8[:], 5.5, None, ALU.is_lt)
     ts(["RI"], ["UP"], T.UP[:], T.RI[:], 7.5, None, ALU.is_gt)
     ts(["R8"], ["NM"], T.NM[:], T.R8[:], 5.5, None, ALU.is_gt)
+    ts(["IR", "RF", "LX"], ["OH"], T.OH[:], T.IR[:, 0:16], col("RF"), None, ALU.is_equal)
+    for (x, y, c) in ((0, 6, FAR), (6, 7, M + 1.0), (8, 10, FAR)):
+        fill("LX%d" % x, T.LX[:, x:y], c)
     vc(["Pi"], ["Pf"], T.Pf[0:24, :], T.Pi[0:24, :])
     ts(["IV"], ["SEL"], T.SEL[0:24, :], T.IV[0:24, :, 0:8], 0.0, None, ALU.is_equal)
     mm(["SEL", "Pf"], ["Q0"], T.Q0[:, 0:256], T.SEL[0:24, :], T.Pf[0:24, :], True, True)
     tt(["LO3", "MID"], ["SB"], T.SB[:], T.LO3[:], T.MID[:], ALU.subtract)
     ts(["UP"], ["S2"], T.S2[:], T.UP[:], -2.0, 1.0, ALU.mult, ALU.add)
     ts(["IR", "GF"], ["G8"], T.G8[:], T.IR[:, 0:8], col("GF"), None, ALU.is_equal)
-    ts(["IR", "RF"], ["OH"], T.OH[:], T.IR[:, 0:16], col("RF"), None, ALU.is_equal)
+    ts(["CC"], ["CLz"], T.CL[:, 0:256], T.CC[:, 0:256], 4095, None, ALU.bitwise_and)
+    ts(["CC"], ["CLw"], T.CL[:, 256:384], T.CC[:, 256:384], 255, None, ALU.bitwise_and)
     tt(["NM", "S2"], ["A2"], T.A2[:], T.NM[:], T.S2[:], ALU.mult)
     tt(["SB", "UP"], ["A1"], T.A1[:], T.SB[:], T.UP[:], ALU.mult)
-    ts(["IR", "KF"], ["IDf"], T.IDf[:], T.IR[:], col("KF"), None, ALU.is_equal)
+    tt(["OH", "LX8"], ["TX"], T.TX[:], T.OH[:], T.LX[:], ALU.mult)
     ts(["SB", "A2"], ["PB"], T.PB[:], T.SB[:], col("A2"), 0.5, ALU.add, ALU.mult)
     tt(["SB", "A1"], ["A0"], T.A0[:], T.SB[:], T.A1[:], ALU.subtract)
-    ts(["KF"], ["NC0"], T.NC0[:], T.KF[:], 96.0, -1.0, ALU.add, ALU.mult)
-    ts(["KF"], ["NC1"], T.NC1[:], T.KF[:], 224.0, -1.0, ALU.add, ALU.mult)
-    act(["Q0", "PB"], ["PL0"], T.PL[:, OWN:OWN + 256], T.Q0[:, 0:256], IDENT, bias=col("PB"))
-    for (n, s) in (("IDh", 1.0), ("DG0", col("NC0")), ("DG1", col("NC1")), ("DN", -256.0), ("IDb", 1.0)):
-        act(["IDf", "NC0", "NC1"], [n], T[n][:], T.IDf[:], COPY, scale=s)
+    op("V", v.tensor_reduce, ["TX"], ["XE"], T.XE[:], T.TX[:], AxisListType.X, ALU.add)
+    ts(["IR", "KF"], ["IDf"], T.IDf[:], T.IR[:], col("KF"), None, ALU.is_equal)
+    for i in range(4):
+        op("V", v.transpose, ["B0"], ["OT%d" % i], T.OT[:, i::4], T.B0[:, :, i, :])
+    ts(["IR", "XE"], ["Xe"], T.X[:, M:M + 8], T.IR[:, 0:8], 0.0, col("XE"), ALU.mult, ALU.add)
+    fill("OSe", T.OS[:, 128:130], M)
+    ts(["RF"], ["R128"], T.R128[:], T.RF[:], 128.0, None, ALU.mult)
+    vc(["OT%d" % i for i in range(4)], ["OS"], T.OS[:, 0:128], T.OT[:])
     ts(["G8", "A1"], ["CM1"], T.CM[:, 8:16], T.G8[:], col("A1"), None, ALU.mult)
     ts(["IR", "KF"], ["TRI"], T.TRI[:], T.IR[:], col("KF"), None, ALU.is_gt)
     ts(["G8", "A0"], ["CM0"], T.CM[:, 0:8], T.G8[:], col("A0"), None, ALU.mult)
     fill("ONE", T.ONE[:], 1.0)
-    for i in range(4):
-        op("V", v.transpose, ["B0"], ["OT%d" % i], T.OT[:, i::4], T.B0[:, :, i, :])
-    fill("OSe", T.OS[:, 128:130], M)
-    fill("LX", T.LX[:], 0.0)
-    fill("LB", T.LB[:], 0.0)
-    vc(["OT%d" % i for i in range(4)], ["OS"], T.OS[:, 0:128], T.OT[:])
-    await_("V", wr["LX"] + wr["LB"])
-    for (x, y, c) in ((0, 6, FAR), (6, 7, M + 1.0), (10, 12, M + 0.0), (14, 15, M + 0.0)):
-        fill("LX%d" % x, T.LX[:, x:y], c)
-    for (r, c) in ((2, 2.0 ** 23), (6, -SH), (8, -C), (9, -6 * K6), (10, 1 - SH), (11, -SH - 3 * KP), (12, 3 * K0 - C),
-                   (14, 2 - SH + 6 * KP), (15, -2.5 * KP)):
-        fill("LB%d" % r, T.LB[:, r:r + 1], c)
-    ts(["RF"], ["R128"], T.R128[:], T.RF[:], 128.0, None, ALU.mult)
-    tt(["OH", "LX14"], ["TX"], T.TX[:], T.OH[:], T.LX[:], ALU.mult)
-    tt(["OH", "LB15"], ["TB"], T.TB[:], T.OH[:], T.LB[:], ALU.mult)
     ts(["IR", "R128"], ["NI"], T.NI[:], T.IR[:], col("R128"), None, ALU.add)
-    op("V", v.tensor_reduce, ["TX"], ["XE"], T.XE[:], T.TX[:], AxisListType.X, ALU.add)
-    op("V", v.tensor_reduce, ["TB"], ["BI"], T.BI[:], T.TB[:], AxisListType.X, ALU.add)
-    for d in range(1, 8):
-        fill("CPz%d" % d, T.CP[:, (d - 1) * CW:(d - 1) * CW + 96], 0.0)
-    ts(["IR", "XE"], ["Xe"], T.X[:, M:M + 8], T.IR[:, 0:8], 0.0, col("XE"), ALU.mult, ALU.add)
-    fill("RZ", T.RW[:], 0.0)
-    fill("RO", T.RO[:, 256:272], 0.0)
-    act(["G8"], ["G8K"], T.G8K[:], T.G8[:], COPY, scale=K)
-    act(["G8"], ["G8N"], T.G8N[:], T.G8[:], COPY, scale=-1.0)
-    act(["OH"], ["E913"], T.E913[:], T.OH[:, 9:10], IDENT, bias=T.OH[:, 13:14])
-    act(["OH"], ["E25"], T.E25[:], T.OH[:, 2:3], IDENT, bias=T.OH[:, 5:6])
-    for (t, n, r) in ((2, "G8N", 6), (3, "G8", 10), (4, "G8", 15), (5, "G8", 11), (9, "G8", 8), (10, "G8", 7), (11, "G8N", 12),
-                      (6, "G8N", 14), (0, "G8K", 5), (1, "G8K", 2), (7, "G8K", 5), (8, "G8K", 2)):
-        act([n, "OH"], ["C2_%d" % t], T.C2[:, t // 7, t % 7::7], T[n][:], COPY, scale=T.OH[:, r:r + 1])
-    act(["G8"], ["C2_13"], T.C2[:, 1, 6::7], T.G8[:], COPY, scale=0.0)
-    act(["G8", "E913"], ["C2"], T.C2[:, 1, 5::7], T.G8[:], COPY, scale=col("E913"))
-    act(["G8K", "E25"], ["CZ0"], T.CZ[:, 0], T.G8K[:], COPY, scale=col("E25"))
-    act(["G8K", "OH"], ["CZ"], T.CZ[:, 1], T.G8K[:], COPY, scale=T.OH[:, 2:3])
-    act(["G8", "OH"], ["G87"], T.G87[:], T.G8[:], COPY, scale=T.OH[:, 7:8])
+    ts(["KF"], ["KF2"], T.KF2[:], T.KF[:], 2.0, None, ALU.mult)
+    ts(["KF"], ["KF3"], T.KF3[:], T.KF[:], 2.0, 1.0, ALU.mult, ALU.add)
+    ts(["IK"], ["R3"], T.R3[:], T.IK[:], 3, 7, ALU.logical_shift_right, ALU.bitwise_and)
+    ts(["KF"], ["G6"], T.G6[:], T.KF[:], 63.5, 6.0, ALU.is_gt, ALU.mult)
+    ts(["R8"], ["R7"], T.R7[:], T.R8[:], 5.5, 100.0, ALU.is_gt, ALU.mult)
+    vc(["R3"], ["QM"], T.QM[:], T.R3[:])
+    ts(["R8", "G6", "R7"], ["T2"], T.T2[:], T.R8[:], col("G6"), col("R7"), ALU.add, ALU.add)
+    ts(["G16", "QM"], ["MK"], T.MK[:], T.G16[:], col("QM"), None, ALU.is_equal)
+    vc(["BXa"], ["N0"], T.N0[:], T.BXi[:, 0:1])
+    ts(["IR", "T2"], ["SN"], T.SN[:], T.IR[:, 0:12], col("T2"), None, ALU.is_equal)
+    fill("RZ", T.RW[:, 96::RWW], 0.0)
+    fill("ZL", T.ZL[:], 0.0)
+    act(["Q0", "PB"], ["PL0"], T.PL[:, OWN:OWN + 256], T.Q0[:, 0:256], IDENT, bias=col("PB"))
+    for (n, s) in (("DG", -96.0), ("DN", -256.0), ("DS", -16.0), ("IDh", 1.0), ("IDb", 1.0)):
+        act(["IDf"], [n], T[n][:], T.IDf[:], COPY, scale=s)
 
-    X = ["Xa", "Xe"]
-    act(X + ["OS", "OSe"], ["W2"], T.W2[:], T.X[:].indirect(T.OS[:, 0:129]), COPY)
-    dmas("dW", X, ["W1a"], [("S", T.W1[r + 8 * i::16, 0:M + 2], T.X[r::16, i:M + 2 + i]) for i in (0, 1) for r in range(6)])
-    dmas("dV", X + ["W2", "NI"], ["W1b", "W2b"],
-         [("S" if i % 2 else "A", out, in_) for i, (out, in_) in enumerate(
-             [(T.W1[r::16, 0:M + 2], T.W2[x::16, 0:M + 2]) for (r, x) in ((6, 0), (7, 1), (14, 3), (15, 4))]
-             + [(T.W2[r::16, 0:M], T.X[x::16, i:M + i]) for (r, x, i) in ((9, 7, 0), (10, 6, 0), (11, 6, 1), (12, 7, 0), (13, 7, 1))]
-             + [(T.W2[14::16, 0:M], T.NI[:])])])
-    act(["Xa", "IR"], ["X0B"], T.X0B[:], T.IR[:], IDENT, scale=0.0, bias=T.X[:, 0:1])
-    W1, W2 = ["W1a", "W1b"], ["W2", "W2b"]
+    def column(n, r, c, plus=None):
+        if plus is None:
+            act(["OH"], [n], col(n), row(r), COPY, scale=c)
+        elif plus in range(16):
+            act(["OH"], [n], col(n), row(r), IDENT, scale=c, bias=row(plus))
+        else:
+            act(["OH", plus], [n], col(n), row(r), IDENT, scale=c, bias=col(plus))
+
+    def coefficients():
+        act(["G8"], ["G8N"], T.G8N[:], T.G8[:], COPY, scale=-1.0)
+        for x in (("T0", 13, K), ("T1", 10, K), ("V2", 7, 256.0, 15), ("U0", 3, 256.0, 11), ("U1", 4, 256.0, 12),
+                  ("P5", 14, -3 * KP, 1), ("P6", 14, 6 * KP, 9), ("E25", 2, 1.0, 5), ("ZH", 5, 4096 * K, "T0"),
+                  ("ZL0", 2, 4096 * K, "T1"), ("V3", 14, -256 * UP16, "V2"), ("U4", 14, 3 * K0 - C - 256 * UP16, "U0"),
+                  ("U2", 14, -6 * K6 - 512 * UP16, "U1"), ("ZL1", 14, 2 * K * K, "ZL0")):
+            column(*x)
+        act(["U0", "U2"], ["U5"], col("U5"), col("U0"), IDENT, bias=col("U2"))
+        for (t, n, c) in ((2, "G8N", 6), (3, "G8", 0), (0, "G8", "ZH"), (1, "G8", "ZL1"), (5, "G8", "P5"), (6, "G8N", "P6"),
+                          (7, "G8", "ZH"), (8, "G8", "ZL1"), (10, "G8", "V3"), (11, "G8N", "U4"), (12, "G8", "U5")):
+            act([n, "OH" if c in range(16) else c], ["C2_%d" % t], T.C2[:, t // 7, t % 7::7], T[n][:], COPY,
+                scale=row(c) if c in range(16) else col(c))
+        act(["G8", "OH"], ["T3"], T.G87[:], T.G8[:], COPY, scale=row(14))
+        for (t, c) in ((4, -2.5 * KP), (9, -C), (13, 0.0)):
+            act(["T3"], ["C2"], T.C2[:, t // 7, t % 7::7], T.G87[:], COPY, scale=c)
+        act(["G8", "E25"], ["CZ0"], T.CZ[:, 0::2], T.G8[:], COPY, scale=col("E25"))
+        act(["G8", "OH"], ["CZ"], T.CZ[:, 1::2], T.G8[:], COPY, scale=row(2))
+        act(["G8", "OH", "C2"], ["G87"], T.G87[:], T.G8[:], COPY, scale=row(7))
+        act(["N0", "IR"], ["X0B"], T.X0B[:], T.IR[:], IDENT, scale=0.0, bias=col("N0"))
+
+    dmas("dL", ["CLz", "CLw"], ["Xb"], [("S", T.X[r::16, 0:M], T.CL[:, 128 * i:128 * i + 128]) for i, r in enumerate((10, 13, 15))])
+    X = ["Xa", "Xb", "Xe"]
+    coefficients()
+    act(X + ["OS", "OSe"], ["G"], T.G[:], T.X[:].indirect(T.OS[:, 0:129]), COPY)
+    dmas("dW", ["W1e", "BXi"], ["W1a"], [("S", T.W1[r + 8 * i::16, 0:M - i], T.nodes[r::16, i:M]) for i in (0, 1) for r in range(6)])
+    dmas("dU", X + ["NI"], ["W2a"],
+         [("S", T.W2[0::8, 0:M], T.X[6::8, 0:M]), ("S", T.W2[3::8, 0:M], T.X[7::8, 0:M]), ("S", T.W2[4::8, 0:M], T.X[7::8, 1:M + 1]),
+          ("S", T.W2[1::16, 0:M], T.X[6::16, 1:M + 1]), ("S", T.W2[9::16, 0:M], T.NI[:])])
+    dmas("dV", ["G", "W1e", "W2e"], ["W1b", "W2b"],
+         [("S", T.W1[6 + i::8, 0:M + 2], T.G[i::8, 0:M + 2]) for i in (0, 1)]
+         + [("S", T.W2[r::8, 0:M + 2], T.G[r::8, 0:M + 2]) for r in (2, 5, 6, 7)])
+    W1, W2 = ["W1a", "W1b"], ["W2a", "W2b"]
 
     tt(["BXa", "BXi"], ["BX"], T.BX[:], T.BXi[:, 0:8:2], T.BXi[:, 8:12], ALU.add)
     for e in range(4):
         ts(["PL0", "BX"], ["F0_%d" % e], T.F0[:, e * 256:e * 256 + 256], T.PL[:, OWN:OWN + 256], T.BX[:, e:e + 1], None, ALU.is_lt)
         for b in (0, 1):
-            mm(["F0_%d" % e, "CM0", "CM1"], ["Q1"], T.Q1[:, b * 64 + e * 16:b * 64 + e * 16 + 16],
-               T.F0[:, e * 256 + b:e * 256 + 256:2], T.CM[:], True, True)
+            for (at, x, y) in (((112 + 8 * b, 0, 8), (56 * b, 8, 16)) if e == 0 else ((56 * b + 16 * e - 8, 0, 16),)):
+                mm(["F0_%d" % e, "CM0", "CM1"], ["Q1"], T.Q1[:, at:at + y - x], T.F0[:, e * 256 + b:e * 256 + 256:2], T.CM[:, x:y],
+                   True, True)
     ts(["Q1"], ["HB"], T.HB[:], T.Q1[:, 0:128], -2.5, None, ALU.is_lt)
-    mm(["HB", "TRI"], ["Q2"], T.Q2[:, 8:64], T.TRI[:], T.HB[:, 8:64], True, False)
-    mm(["HB", "DG0"], ["Q2"], T.Q2[:, 8:64], T.DG0[:], T.HB[:, 8:64], False, True)
-    mm(["HB"], ["Q2"], T.Q2[:, 72:128], T.TRI[:], T.HB[:, 72:128], True, False)
-    mm(["HB", "ONE"], ["Q2"], T.Q2[:, 72:128], T.ONE[:], T.HB[:, 8:64], False, False)
-    mm(["HB", "DG1"], ["Q2"], T.Q2[:, 72:128], T.DG1[:], T.HB[:, 72:128], False, True)
-    for b in (0, 1):
-        mm(["HB", "DN"], ["Q2"], T.Q2[:, b * 64:b * 64 + 8], T.DN[:], T.HB[:, b * 64:b * 64 + 8], True, True)
-    ts(["KF"], ["KF2"], T.KF2[:], T.KF[:], 2.0, None, ALU.mult)
-    for b in (0, 1):
-        ts(["Q2", "KF", "ZL"], ["ZL%d" % b], T.ZL[:, 142 + b:1030:16], T.Q2[:, b * 64 + 8:b * 64 + 64], col("KF"), 96.0 + 128 * b,
-           ALU.add, ALU.add)
-    for b in (0, 1):
-        ts(["Q2", "KF2", "ZL"], ["ZO%d" % b], T.ZL[:, 14 + b:128:16], T.Q2[:, b * 64:b * 64 + 8], col("KF2"), 256.0 + b,
-           ALU.add, ALU.add)
 
-    def places(ds, ps):
-        for d in ds:
-            for i in range(8):
-                mm(["ZL0", "ZL1", "ZO0", "ZO1", "IDh"], [ps], T[ps][:, d * 16:d * 16 + 16],
-                   T.ZL[:, 128 * d + 14 - 2 * i:128 * d + 142 - 2 * i], T.IDh[:, i::8], i == 0, i == 7)
+    def ranks(ps, last):
+        mm(["HB", "TRI"], [ps], T[ps][:, 0:112], T.TRI[:], T.HB[:, 0:112], True, False)
+        mm(["HB", "ONE"], [ps], T[ps][:, 56:112], T.ONE[:], T.HB[:, 0:56], False, False)
+        mm(["HB", "DG"], [ps], T[ps][:, 0:112], T.DG[:], T.HB[:, 0:112], False, last)
 
-    def list_(ds, ps):
-        vc([ps], ["SO%d" % d for d in ds], T.SO[:, ds[0] * 16:ds[-1] * 16 + 16], T[ps][:, ds[0] * 16:ds[-1] * 16 + 16])
-
-    def scatter(d):
-        vc(["PL0", "SO%d" % d, "CPz%d" % d], ["CP%d" % d], T.CP[:, (d - 1) * CW:d * CW].indirect(T.SO[:, d * 16:d * 16 + 16]),
-           T.PL[:, OWN:OWN + 256])
-        deps("G", ["CP%d" % d, "RZ"], [])
-        dst = cores[(rank + d) % N]
-        rid, pid, _ = topo.addr(dst)
-        total["ls"] += len(topo.engines(core, dst))
-        g.remote_dma(T.PL[:, slot(d):slot(d) + 96], T.CP[:, (d - 1) * CW:(d - 1) * CW + 96],
-                     T.sem["pt%d" % d], T.sem.ls, pid, rid, topo.mask(core, dst))
-        total["pt%d" % d] = len(topo.engines(cores[(rank - d) % N], core))
-        note((None, "pt%d" % d, total["pt%d" % d]), [], ["PL%d" % d])
-
-    places((3,), "Q3")
-    places((4, 5, 6, 7), "Q4")
-    places((0, 1, 2), "Q5")
+    ranks("Q2", True)
+    ranks("Q1", False)
+    mm(["HB", "DN"], ["Q2"], T.Q2[:, 112:128], T.DN[:], T.HB[:, 112:128], True, True)
+    fill("LS", T.LS[:], 1.0)
+    fill("LB", T.LB[:], 0.0)
     fill("C1", T.C1[:], 0.0)
+    ts(["Q2"], ["HI"], T.HI[:, 0:112], T.Q2[:, 0:112], 1 / 16, 6 + UP16 - 0.5 + 1 / 32, ALU.mult, ALU.add)
+    mm(["HI", "DS"], ["Q1"], T.Q1[:, 0:112], T.DS[:], T.HI[:, 0:112], False, True)
+    for n in range(6):
+        for b in (0, 1):
+            ts(["HI", "HM", "KF2", "KF3"], ["HM%d" % b], T.HM[:, 448 * b + n:448 * b + 448:8], T.HI[:, 56 * b:56 * b + 56], UP16 + n,
+               col("KF3" if b else "KF2"), ALU.is_equal, ALU.mult)
+        if n == 1:
+            ts(["Q1"], ["LO"], T.LO[:, 0:112], T.Q1[:, 0:112], 96 + 16 * UP16, None, ALU.add)
+    for c in range(16):
+        ts(["LO"], ["LM"], T.LM[:, c::16], T.LO[:, 0:112], float(c), None, ALU.is_equal)
+    BANK = ("Q3", "Q4", "Q5", "Q0")
+    for i, ds in enumerate(PAIRS):
+        for h, d in enumerate(ds):
+            for b in (0, 1):
+                k = 7 * b + d - 1
+                mm(["HM0", "HM1", "LM"], [BANK[i]], T[BANK[i]][64 * h:64 * h + 64, 0:128], T.HM[:, 64 * k:64 * k + 64],
+                   T.LM[:, 128 * k:128 * k + 128], b == 0, b == 1)
+
+    def own_scene(i):
+        n, ps, m = 64 * len(PAIRS[i]), "PS%d" % (i % 2), "MM%d" % i
+        tt([BANK[i], "MK"], [m], T[m][0:n, :], T[BANK[i]][0:n, 0:128], T.MK[0:n, :], ALU.mult)
+        mm([m, "SN"], [ps], T[ps][:, 0, 0:12], T[m][0:n, :], T.SN[0:n, :], True, True)
+        act([ps], ["IX%d" % i], T.IX[:, 12 * i:12 * i + 12], T[ps][:, 0, 0:12], COPY)
+
+    def pick(i):
+        ds = PAIRS[i]
+        n = 96 * len(ds)
+        vc(["PL0", "IX%d" % i], ["CP%d" % i], T.CP[:, 192 * i:192 * i + n],
+           T.PL[:, OWN:OWN + 256].indirect(T.IX[:, 12 * i:12 * i + n // 16]))
+        remote([(d, "pt%d" % d, T.CP[:, 192 * i + 96 * h:192 * i + 96 * h + 96], T.PL[:, slot(d):slot(d) + 96], 16 // len(ds))
+                for h, d in enumerate(ds)], ["CP%d" % i, "RZ"])
+        for d in ds:
+            note((None, "pt%d" % d, total["pt%d" % d]), [], ["PL%d" % d])
+
+    await_("V", wr["LS"] + wr["LB"])
+    for (x, c) in ((slice(2, 6, 3), 2.0 ** -12), (slice(3, 5), 2.0 ** -8), (slice(7, 8), 2.0 ** -8)):
+        fill("LS1", T.LS[:, x], c)
+    own_scene(0)
+    own_scene(1)
+    fill("LB1", T.LB[:, 14:15], 1.0)
+    own_scene(2)
+    pick(0)
+    own_scene(3)
+    for i in (1, 2, 3):
+        pick(i)
+    for b in (0, 1):
+        act(["Q2", "ZL"], ["ZL%d" % b], T.ZL[:, 142 + b:1030:16], T.Q2[:, 56 * b:56 * b + 56], IDENT, bias=96.0)
+        act(["Q2", "ZL", "KF2", "KF3"], ["ZO%d" % b], T.ZL[:, 14 + b:128:16], T.Q2[:, 112 + 8 * b:120 + 8 * b], IDENT,
+            bias=col("KF3" if b else "KF2"))
+    for (x, c) in ((slice(2, 6, 3), UP16 - 0.5 + 2.0 ** -13), (slice(3, 5), UP16 - 0.5 + 2.0 ** -9), (slice(7, 8), UP16 - 0.5 + 2.0 ** -9),
+                   (slice(10, 14, 3), -2048.0), (slice(1, 7, 5), -SH), (slice(0, 1), 1 - SH), (slice(9, 10), 2 - SH)):
+        fill("LB1", T.LB[:, x], c)
+    tt(["OH", "LS1"], ["TS"], T.TS[:], T.OH[:], T.LS[:], ALU.mult)
+    fill("OF1", T.OF1[:], 1)
+    tt(["OH", "LB1"], ["TB"], T.TB[:], T.OH[:], T.LB[:], ALU.mult)
+    op("V", v.tensor_reduce, ["TS"], ["SC"], T.SC[:], T.TS[:], AxisListType.X, ALU.add)
     for b in "01":
         fill("D0_" + b, T["D0_" + b][:], 0.0)
-    list_((3,), "Q3")
-    for b in "01":
-        fill("OF" + b, T["OF" + b][:], 1)
-    scatter(3)
-    list_((4, 5, 6, 7), "Q4")
-    for b in "01":
-        fill("D0a" + b, T["D0_" + b][:, 0::7], -2.0 ** 60)
-    scatter(4)
-    list_((0, 1, 2), "Q5")
-    for d in (5, 6, 7, 1, 2):
-        scatter(d)
+    op("V", v.tensor_reduce, ["TB"], ["BI"], T.BI[:], T.TB[:], AxisListType.X, ALU.add)
     for (t, n, c) in ((1, "A2", K * K), (4, "A0", -KP), (5, "A0", -KP), (6, "SB", -KP), (8, "A2", K * K), (11, "A0", -K0),
                       (12, "SB", -K6)):
         ts(["G8", n, "C1"], ["C1_%d" % t], T.C1[:, t // 7, t % 7::7], T.G8[:], col(n), c, ALU.mult, ALU.mult)
+    vc(W1 + ["D0_1"], ["N1"], T.N1[:], T.W1[:, 1:2])
     for b in "01":
+        fill("D0a" + b, T["D0_" + b][:, 0::7], -2.0 ** 60)
         fill("Z" + b, T["Z" + b][:], 0.0)
         fill("SPz" + b, T["SP" + b][:, 6::7, :], 0.0)
-        fill("ZS" + b, T["ZS" + b][:], 0.0)
 
     def points(b):
         return ["PL%d" % d for d in (FIRST if b == 0 else (0, 1, 2))]
 
     def depth(b):
         lo, n = BATCH[b]
-        ps = "PS%d" % b
+        ps = "Q%d" % b
         for j in range(4):
-            mm(points(b) + ["CZ0", "CZ"], [ps], T[ps][0:n // 4, :, 8 * j:8 * j + 8], T.PL[:, lo + j:lo + n:4], T.CZ[:], True, True)
+            mm(points(b) + ["CZ0", "CZ"], [ps], T[ps][0:n // 4, 16 * j:16 * j + 16], T.PL[:, lo + j:lo + n:4], T.CZ[:], True, True)
         for i in (0, 1):
-            act([ps, "D0_%d" % b, "D0a%d" % b], ["D0b%d" % b], T["D0_%d" % b][0:n // 4, 1 + i::7], T[ps][0:n // 4, i, 0:32], COPY)
+            act([ps, "D0_%d" % b, "D0a%d" % b], ["D0b%d" % b], T["D0_%d" % b][0:n // 4, 1 + i::7], T[ps][0:n // 4, i:64:2],
+                IDENT, scale=K, bias=(2 - i) * Z0 * K)
 
-    def visit(b, t):
+    def rows(b, part):
+        n, of = BATCH[b][1], "OF%d" % b
+        x, y = (0, CUTA) if part == 0 else (CUTA, n)
+        act(W2 + [of, "BI", "SC"], ["D2_%d_%d" % (b, part)], T["D2_%d" % b][:, x:y], T.W2[:, 0:M + 2].indirect(T[of][:, x // 16:y // 16]),
+            IDENT, scale=col("SC"), bias=col("BI"))
+
+    def tests(b, t, part):
         lo, n = BATCH[b]
-        offs, of, d1, d2, ps = T["OF%d" % b][:, 0:n // 16], "OF%d" % b, "D1_%d" % b, "D2_%d" % b, "PS%d" % b
-        act(W2 + [of, "BI"], [d2], T[d2][:, 0:n], T.W2[:].indirect(offs), IDENT, bias=col("BI"))
+        x, y = (0, CUT) if part == 0 else (CUT, n)
+        of, d1, out, pt = "OF%d" % b, "D1_%d_%d" % (b, part), T["D1_%d" % b][:, x:y], T.PL[:, lo + x:lo + y]
         if t == 0:
-            ts(W1 + points(b), [d1], T[d1][:, 0:n], T.PL[:, lo:lo + n], T.W1[:, 1:2], None, ALU.is_lt)
+            ts(["N1"] + points(b), [d1], out, pt, col("N1"), None, ALU.is_lt)
         else:
-            tt(W1 + points(b) + [of], [d1], T[d1][:, 0:n], T.W1[:, 0:M + 2].indirect(offs), T.PL[:, lo:lo + n], ALU.is_gt)
+            tt(W1 + points(b) + [of], [d1], out, T.W1[:, 0:M + 2].indirect(T[of][:, x // 16:y // 16]), pt, ALU.is_gt)
 
-    def sums(b, js):
-        n, ps = BATCH[b][1], "PS%d" % b
-        for j in js:
-            out = T[ps][0:n // 4, :, 56 * j:56 * j + 56]
-            mm(["D1_%d" % b, "C1_12"], [ps], out, T["D1_%d" % b][:, j:n:4], T.C1[:], True, False)
-            mm(["D2_%d" % b, "C2"], [ps], out, T["D2_%d" % b][:, j:n:4], T.C2[:], False, True)
+    def sums(b, i, first=False):
+        n, ps, d = BATCH[b][1], "PS%d" % b, "D%d_%d" % (i, b)
+        for j in range(4):
+            mm((["D2"] if first else [d + "_0", d + "_1"]) + ["C2" if i == 2 else "C1_12"], [ps], T[ps][0:n // 4, :, 56 * j:56 * j + 56],
+               T.D2[:, 0:n // 4] if first else T[d][:, j:n:4], T["C%d" % i][:], i == 2 and j == 0, i == 1 and j == 3)
 
     def scan(b, x, out, i, lo, hi):
         m, ps = BATCH[b][1] // 4, "PS%d" % b
-        op("V", v.tensor_tensor_scan, [ps, "D0b%d" % b, "SPz%d" % b], [x], out, T["D0_%d" % b][0:m, lo:hi],
-           T[ps][0:m, i, lo:hi], 0.0, ALU.subtract, ALU.max)
+        op("V", v.tensor_tensor_scan, [ps, "D0b%d" % b, "SPz%d" % b], [x], out,
+           T["D0_%d" % b][0:m, lo:hi], T[ps][0:m, i, lo:hi], 0.0, ALU.subtract, ALU.max)
 
     def nodes(b):
         m, z, ex = BATCH[b][1] // 4, "Z%d" % b, "Q%d" % b
         for j in range(4):
             scan(b, "SP%d" % b, T["SP%d" % b][0:m, :, j], 0, 56 * j, 56 * j + 56)
         act(["SP%d" % b, z], [z + "v"], T[z][0:m, 12:140], T["SP%d" % b][0:m, 6::7, :], COPY, scale=-1.0)
+
+    def turn(b):
+        m, z, ex = BATCH[b][1] // 4, "Z%d" % b, "Q%d" % b
         for i in range(4):
-            mm([z + "v"], [ex], T[ex][:, 0:m // 4], T[z][0:m, 12 - 4 * i:140 - 4 * i], T.IDh[0:m, i:m:4], i == 0, i == 3)
+            mm([z + "v", "IDh"], [ex], T[ex][:, 0:m // 4], T[z][0:m, 12 - 4 * i:140 - 4 * i], T.IDh[0:m, i:m:4], i == 0, i == 3)
+        act([ex], ["OF%d" % b], T["OF%d" % b][:, 0:m // 4], T[ex][:, 0:m // 4], IDENT, bias=SH)
 
     def weights(b):
         scan(b, "WS%d" % b, T["WS%d" % b][0:BATCH[b][1] // 4, :], 1, 0, 224)
 
-    def offsets(b):
-        k = BATCH[b][1] // 16
-        ts(["Q%d" % b], ["OF%d" % b], T["OF%d" % b][:, 0:k], T["Q%d" % b][:, 0:k], SH, None, ALU.add)
-
     def add_up(b, t):
         m, ac = BATCH[b][1] // 4, "Q%d" % (2 + b)
         mm(["WS%d" % b, "IDf"], [ac], T[ac][0:m, 0:32], T.IDf[0:m, 0:m], T["WS%d" % b][0:m, 5::7], t == 0, t == STEPS - 1)
-        if t == 0:
+        if t == 1:
             for j in range(4):
                 mm(["X0B", "G87"], [ac], T[ac][0:m, 8 * j:8 * j + 8], T.X0B[:, 0:m], T.G87[:], False, False)
 
-    def send(ds, tags, cuts):
-        deps("G", tags, [])
-        trs = []
-        for i, d in enumerate(ds):
-            es = lanes(rank - d, cuts[i], cuts[i + 1])
-            at = slot(d) if d in FIRST else slot(d) - 256
-            trs.append(RemoteDMATransfer(
-                dst_ids=ids([rank - d]), dma_engine_mask=sum(1 << e for e in es), remote_sem=T.sem["rt%d" % d],
-                srcs=[T.SA[:, at:at + 96]], dsts=[T.RW[:, (d - 1) * RWW:(d - 1) * RWW + 96]]))
-            total["ls"] += len(es)
-            total["rt%d" % d] = len(es)
+    def send(ds, tag, lanes):
+        at = [slot(d) if d in FIRST else slot(d) - 256 for d in ds]
+        remote([(-d, "rt%d" % d, T.SA[:, x:x + 96], T.RW[:, (d - 1) * RWW:(d - 1) * RWW + 96], n) for d, x, n in zip(ds, at, lanes)], [tag])
+        for d in ds:
             note((None, "rt%d" % d, total["rt%d" % d]), [], ["RV%d" % d])
-        g.remote_dma_fused(trs, local_sem=T.sem.ls)
 
     def pieces(b):
         n = BATCH[b][1]
-        m, ac, h, zs, row = n // 4, "Q%d" % (2 + b), T["H%d" % b], "ZS%d" % b, "Q%d" % (4 + b)
+        m, ac, h, zs, ps = n // 4, "Q%d" % (2 + b), T["H%d" % b], "ZS%d" % b, "Q%d" % (4 + b)
         for i, e in enumerate((44, 37, 30)):
             ts([ac], ["H%d_%d" % (b, i)], h[0:m, i], T[ac][0:m, 0:32], 1.5 * 2.0 ** e, 1.5 * 2.0 ** e, ALU.add, ALU.subtract)
         for i in (0, 1):
@@ -382,51 +441,74 @@ def rank_program(g, core, T, topo):
                ALU.subtract)
         tt([ac, "H%d_2" % b, zs], [zs + "_2"], T[zs][0:m, 2::16], T[ac][0:m, 0:32], h[0:m, 2], ALU.subtract)
         for j in range(4):
-            mm([zs + "_0", zs + "_1", zs + "_2", "IDb"], [row], T[row][:, j:n:4], T[zs][0:m, 128 * j:128 * j + 128], T.IDb[0:m, 0:m], True, True)
+            mm([zs + "_0", zs + "_1", zs + "_2", "IDb"], [ps], T[ps][:, j:n:4], T[zs][0:m, 128 * j:128 * j + 128], T.IDb[0:m, 0:m],
+               True, True)
         if b == 0:
-            act([row], ["SA0"], T.SA[:, 0:480], T[row][:, 0:480], COPY)
-            send(FIRST, ["SA0"], (0, 4, 8, 12, 14, 16))
+            act([ps], ["SA0"], T.SA[:, 0:480], T[ps][:, 0:480], COPY)
+            send(FIRST, "SA0", (4, 4, 4, 2, 2))
         else:
-            act([row], ["SA1"], T.SA[:, 480:672], T[row][:, 256:448], COPY)
-            send((1, 2), ["SA1"], (0, 8, 16))
-            act([row], ["RV0"], T.RO[:, 0:256], T[row][:, 0:256], COPY)
+            act([ps], ["SA1"], T.SA[:, 480:672], T[ps][:, 256:448], COPY)
+            send((1, 2), "SA1", (8, 8))
+            act([ps], ["RV0"], T.RO[:, 0:256], T[ps][:, 0:256], COPY)
 
     def spare(s):
-        if s == 1:
-            ts(["SO0"], ["GO0"], T.GO[:, 0:16], T.SO[:, 0:16], 256.0, None, ALU.min)
-            ts(["SO%d" % d for d in range(1, 8)], ["GO1"], T.GO[:, 16:128], T.SO[:, 16:128], 96.0, None, ALU.min)
-            op("V", v.tensor_reduce, ["OH"], ["E048"], T.E048[:], T.OH[:, 0:3], AxisListType.X, ALU.add)
-        if s == 2:
-            ts(["G8", "E048"], ["SY"], T.SY[:], T.G8[:], col("E048"), None, ALU.mult)
+        if s in (2, 3, 4, 5):
+            for d in (2 * s - 4, 2 * s - 3):
+                for i in range(8):
+                    mm(["ZL0", "ZL1", "ZO0", "ZO1", "IDh"], ["Q4"], T.Q4[:, d * 16:d * 16 + 16],
+                       T.ZL[:, 128 * d + 14 - 2 * i:128 * d + 142 - 2 * i], T.IDh[:, i::8], i == 0, i == 7)
+        if s in (1, 2):
+            fill("ZS%d" % (s - 1), T["ZS%d" % (s - 1)][:], 0.0)
+        if s == 3:
+            op("V", v.tensor_reduce, ["OH"], ["E012"], T.E012[:], T.OH[:, 0:3], AxisListType.X, ALU.add)
+            fill("RO", T.RO[:, 256:272], 0.0)
+        if s == 4:
+            ts(["G8", "E012"], ["SY"], T.SY[:], T.G8[:], col("E012"), None, ALU.mult)
+        if s == 6:
+            ts(["Q4"], ["GO0"], T.GO[:, 0:16], T.Q4[:, 0:16], 256.0, 256.0, ALU.add, ALU.min)
+        if s == 7:
+            ts(["Q4"], ["GO1"], T.GO[:, 16:128], T.Q4[:, 16:128], 96.0, None, ALU.min)
 
+    act(W2 + ["OF1", "BI", "SC"], ["D2"], T.D2[:], T.W2[:, 0:M + 2].indirect(T.OF1[:, 0:8]), IDENT, scale=col("SC"), bias=col("BI"))
     depth(0)
-    visit(0, 0)
-    depth(1)
+    sums(0, 2, True)
+    sums(1, 2, True)
+    tests(0, 0, 0)
+    tests(0, 0, 1)
+    sums(0, 1)
     for s in range(1, 2 * STEPS + 1):
         b, t = s % 2, s // 2
         o, u = 1 - b, (s - 1) // 2
-        if s == 1:
-            sums(o, range(4))
+        more = u < STEPS - 1
         if s < 2 * STEPS:
-            visit(b, t)
-            sums(b, (0, 1))
-        if u < STEPS - 1:
+            tests(b, t, 0)
+        if more:
             nodes(o)
-            weights(o)
-            spare(s)
-            sums(b, (2, 3))
-            add_up(o, u)
-            offsets(o)
+            if s == 1:
+                depth(1)
         else:
             weights(o)
             add_up(o, u)
-            if o == 0:
-                sums(b, (2, 3))
+        if 1 < s < 2 * STEPS:
+            rows(b, 1)
+        if more:
+            turn(o)
+            rows(o, 0)
+        if s < 2 * STEPS:
+            if s > 1:
+                sums(b, 2)
+            tests(b, t, 1)
+            sums(b, 1)
+        if more:
+            weights(o)
+            add_up(o, u)
+            spare(s)
+        else:
             pieces(o)
 
     order = FIRST + (0, 1, 2)
     for i, d in enumerate(order):
-        win = (T.RO[:] if d == 0 else T.RW[:, (d - 1) * RWW:d * RWW]).indirect(T.GO[:, d * 16:d * 16 + 16])
+        win = (T.RO[:] if d == 0 else T.RW[:, (d - 1) * RWW:(d - 1) * RWW + 97]).indirect(T.GO[:, d * 16:d * 16 + 16])
         rs, out = ["RV%d" % d, "RZ", "RO", "GO%d" % min(d, 1)], T.GD[:, d * 256:d * 256 + 256]
         if i % 2 == 0:
             vc(rs, ["GD%d" % d], out, win)

@@ -7,13 +7,12 @@ STEPS = 7
 FIRST = (3, 4, 5, 6, 7)
 PAIRS = ((3, 4), (5, 6), (7, 1), (2,))
 BATCH = [(0, 480), (480, 448)]
-CUTA = 352
-CUT = 160
+CUT, CUTA = 96, 320
 OWN = 480
 RWW = 112
 ALU = AluOpType
-COPY = ActivationFunctionType.Copy
-IDENT = ActivationFunctionType.Identity
+FN = ActivationFunctionType
+COPY, IDENT = FN.Copy, FN.Identity
 K, KP, SH = 2.0 ** 22, 4096.0, 1024.0
 C, K0, K6 = 2.0 ** 21, 5.0 * 2 ** 20, 9.0 * 2 ** 18
 FAR = 2.0 ** 22
@@ -23,28 +22,27 @@ COLUMNS = "ZH ZL0 ZL1 V2 V3 U0 U1 U2 U4 U5 P5 P6 T0 T1 E25".split()
 
 SCRATCH = {}
 for _n, _w, _t in (
-        [(n, [1], "float32") for n in "KF RF GF LO3 MID UP SB A0 A1 A2 NM S2 PB KF2 KF3 R128 BI SC XE E012 N0 N1 T2 G6 R7 QM".split()]
+        [(n, [1], "float32") for n in "NK RF GF LO3 MID UP SB A0 A1 A2 NM S2 PB KF2 KF3 R128 BI SC XE E012 N0 N1 R8F P8F".split()]
         + [("CO", [len(COLUMNS)], "float32")]
-        + [(n, [1], "int32") for n in "IK RI GI R8 R3".split()]
-        + [(n, [128], "float32") for n in "IR IDf SEL X0B".split()]
+        + [(n, [1], "int32") for n in "IK RI GI R8 P8".split()]
+        + [(n, [128], "float32") for n in "IR IDf SEL X0B RU".split()]
         + [(n, [128], "float16") for n in "IDh TRI ONE DG DN DS HB HI LO MK D2 MM0 MM1 MM2 MM3".split()]
-        + [(n, [8], "float32") for n in "G8 G8N G87".split()]
-        + [(n, [16], "float32") for n in "OH LB LX LS TB TX TS".split()]
-        + [("IDb", [128], "bfloat16"), ("SY", [8], "bfloat16"), ("CM", [16], "bfloat16"), ("CZ", [16], "float32"),
-           ("C1", [2, 56], "bfloat16"), ("C2", [2, 56], "bfloat16"), ("IV", [16, 9], "float32"), ("SN", [12], "float16"),
+        + [(n, [8], "float32") for n in "G8 G8N G8E".split()] + [("G87", [32], "float32")]
+        + [(n, [16], "float32") for n in "OH LB LS TB TS".split()]
+        + [("IDb", [128], "bfloat16"), ("SY", [40], "bfloat16"), ("CM", [16], "bfloat16"), ("CZ", [16], "float32"),
+           ("C1", [2, 56], "bfloat16"), ("C2", [2, 56], "bfloat16"), ("IV", [16, 9], "float32"), ("SN", [16], "float16"),
            ("BXi", [16], "int32"), ("NB", [4], "int32"), ("BX", [4], "float32"), ("Pi", [256], "int32"), ("Pf", [256], "float32"),
            ("B0", [2, 4, 16], "int32"), ("OT", [128], "int32"), ("OS", [130], "uint16"), ("NI", [128], "int32"),
            ("CC", [384], "int32"), ("CL", [384], "int32"), ("G16", [8, 16], "float32"),
            ("X", [M + 8], "int32"), ("G", [M + 16], "int32"), ("W1", [M + 8], "int32"), ("W2", [M + 8], "int32"),
-           ("PL", [928], "float32"), ("F0", [1024], "bfloat16"), ("ZL", [1040], "float16"), ("LM", [14 * 128], "float16"),
-           ("HM", [14 * 64], "float16"), ("IX", [48], "uint16"), ("GO", [128], "uint16"), ("CP", [672], "float32"),
+           ("PL", [928], "float32"), ("F0", [1024], "bfloat16"), ("ZL", [1040], "bfloat16"), ("LM", [14 * 128], "float16"),
+           ("HM", [14, 64], "bfloat16"), ("IX", [48], "uint16"), ("GO", [128], "uint16"), ("CP", [672], "float32"),
            ("SA", [672], "bfloat16"), ("RW", [7 * RWW], "bfloat16"), ("RO", [272], "bfloat16"), ("GD", [2048], "bfloat16"),
-           ("Y", [256], "float32")]):
+           ("Y", [64], "float32"), ("ZS", [512], "bfloat16"), ("Z", [2, 144], "float16")]):
     SCRATCH[_n] = ("sbuf", [128] + _w, _t)
 for _b in range(2):
-    for _n, _w, _t in (("D1_", [480], "bfloat16"), ("D2_", [480], "float16"), ("OF", [32], "uint16"), ("D0_", [224], "float32"),
-                       ("SP", [56, 16], "float32"), ("WS", [224], "float32"), ("Z", [144], "float16"),
-                       ("H", [3, 32], "float32"), ("ZS", [512], "bfloat16")):
+    for _n, _w, _t in (("D1_", [480], "bfloat16"), ("D2_", [480], "float16"), ("OF", [32], "uint16"), ("D0_", [2, 224], "float32"),
+                       ("SP", [56, 16], "float32"), ("WS", [224], "float32"), ("H", [3, 32], "float32")):
         SCRATCH["%s%d" % (_n, _b)] = ("sbuf", [128] + _w, _t)
     SCRATCH["PS%d" % _b] = ("psum", [128, 2, 256], "float32")
 for _b in range(6):
@@ -124,8 +122,8 @@ def rank_program(g, core, T, topo):
     def vc(reads, writes, out, in_):
         op("V", v.tensor_copy, reads, writes, out, in_)
 
-    def fill(tag, ap, c):
-        op("V", v.memset, [], [tag], ap, c)
+    def fill(tag, ap, c, after=()):
+        op("V", v.memset, list(after), [tag], ap, c)
 
     def mm(reads, writes, out, lhsT, rhs, start, stop):
         op("P", p.matmul, reads, writes, out, lhsT, rhs, start, stop)
@@ -157,8 +155,6 @@ def rank_program(g, core, T, topo):
     dmas("dP", [], ["Pi"], [("S", T.Pi[0:24, :], T.pts[:, :])])
     dmas("dC", [], ["CC"], [("A", T.CC[:, 128 * i:128 * i + 128], T.nodes[r::16, :]) for i, r in enumerate((2, 5, 7))])
     dmas("dB", [], ["B0"], [("S", T.B0[:, i], T.nodes[6 + 16 * i::32, :]) for i in (0, 1)])
-    dmas("dX", [], ["Xa"], [("SA"[i % 2], T.X[r::16, 0:M], T.nodes[x::16, :]) for i, (r, x) in enumerate(
-        [(r, r) for r in range(8)] + [(8, 3), (9, 4), (11, 8), (12, 8), (14, 8)])])
     op("G", g.iota, [], ["IK"], T.IK[:], [[1, 1]], 0, 1)
     op("G", g.iota, [], ["IR"], T.IR[:], [[1, 128]], 0, 0, allow_small_or_imprecise_dtypes=True)
     op("G", g.iota, [], ["IV"], T.IV[0:32], [[3, 8], [0, 6], [1, 3]], 0, -1, allow_small_or_imprecise_dtypes=True)
@@ -175,65 +171,73 @@ def rank_program(g, core, T, topo):
         total["box"] = total.get("box", 0) + len(ds) * len(es)
     g.remote_dma_fused(trs, local_sem=T.sem.ls)
     note((None, "box", total["box"]), [], ["BXi"])
-    op("G", g.iota, [], ["G16"], T.G16[:], [[1, 8], [0, 16]], 0, 0, allow_small_or_imprecise_dtypes=True)
+    dmas("dX", [], ["Xa"], [("S", T.X[r::8, 0:M], T.nodes[r::8, :]) for r in (3, 4, 6)]
+         + [("S", T.X[r::16, 0:M], T.nodes[x::16, :]) for (r, x) in ((0, 0), (1, 1), (2, 2), (5, 5), (7, 7), (8, 3), (9, 4))])
 
-    fill("HM", T.HM[:], 0.0)
+    def whole(tag, out, n, c):
+        op("G", g.iota, [], [tag], out, [[0, n]], c, 0, allow_small_or_imprecise_dtypes=True)
+
+    whole("HM", T.HM[:, :, 48:64], 224, 0)
+    op("G", g.iota, [], ["G16"], T.G16[:], [[1, 8], [0, 16]], 0, 0, allow_small_or_imprecise_dtypes=True)
+    whole("LS", T.LS[:], 16, 1)
+    whole("LB", T.LB[:], 16, 0)
+    for (n, lo, hi, step, c) in (("LS", 2, 6, 3, 2.0 ** -12), ("LS", 3, 5, 1, 2.0 ** -8), ("LS", 7, 8, 1, 2.0 ** -8), ("LS", 14, 15, 1, 0.0),
+                                 ("LB", 2, 6, 3, UP16 - 0.5 + 2.0 ** -13), ("LB", 3, 5, 1, UP16 - 0.5 + 2.0 ** -9),
+                                 ("LB", 7, 8, 1, UP16 - 0.5 + 2.0 ** -9), ("LB", 10, 14, 3, -2048.0), ("LB", 1, 7, 5, -SH),
+                                 ("LB", 0, 1, 1, 1 - SH), ("LB", 9, 10, 1, 2 - SH), ("LB", 14, 15, 1, 1.0)):
+        x = T[n][:, lo:hi:step]
+        op("G", g.affine_select, ["LS", "LB"], [n + "1"], x, x, [[0, len(range(lo, hi, step))]], ALU.is_gt, c, 0, 0)
+    for b in "01":
+        whole("D0_" + b, T["D0_" + b][:], 448, 0)
+    for b in "01":
+        whole("SPz" + b, T["SP" + b][:, 6::7, :], 128, 0)
+
     fill("W1e", T.W1[:, M - 8:M + 8], FAR)
     fill("W2e", T.W2[:, M:M + 8], M)
-    fill("LX", T.LX[:], 0.0)
+    fill("OSe", T.OS[:, 128:130], M)
+    ts(["IK"], ["R8"], T.R8[:], T.IK[:], 7, None, ALU.bitwise_and)
     ts(["IK"], ["RI"], T.RI[:], T.IK[:], 15, None, ALU.bitwise_and)
     ts(["IK"], ["GI"], T.GI[:], T.IK[:], 4, None, ALU.logical_shift_right)
-    ts(["IK"], ["R8"], T.R8[:], T.IK[:], 7, None, ALU.bitwise_and)
-    vc(["IK"], ["KF"], T.KF[:], T.IK[:])
-    vc(["RI"], ["RF"], T.RF[:], T.RI[:])
-    vc(["GI"], ["GF"], T.GF[:], T.GI[:])
     ts(["R8"], ["LO3"], T.LO3[:], T.R8[:], 2.5, 2.0, ALU.is_lt, ALU.mult)
     ts(["R8"], ["MID"], T.MID[:], T.R8[:], 5.5, None, ALU.is_lt)
     ts(["RI"], ["UP"], T.UP[:], T.RI[:], 7.5, None, ALU.is_gt)
     ts(["R8"], ["NM"], T.NM[:], T.R8[:], 5.5, None, ALU.is_gt)
-    ts(["IR", "RF", "LX"], ["OH"], T.OH[:], T.IR[:, 0:16], col("RF"), None, ALU.is_equal)
-    for (x, y, c) in ((0, 6, FAR), (6, 7, M + 1.0), (8, 10, FAR)):
-        fill("LX%d" % x, T.LX[:, x:y], c)
-    vc(["Pi"], ["Pf"], T.Pf[0:24, :], T.Pi[0:24, :])
-    ts(["IV"], ["SEL"], T.SEL[0:24, :], T.IV[0:24, :, 0:8], 0.0, None, ALU.is_equal)
-    mm(["SEL", "Pf"], ["Q0"], T.Q0[:, 0:256], T.SEL[0:24, :], T.Pf[0:24, :], True, True)
+    vc(["GI"], ["GF"], T.GF[:], T.GI[:])
     tt(["LO3", "MID"], ["SB"], T.SB[:], T.LO3[:], T.MID[:], ALU.subtract)
     ts(["UP"], ["S2"], T.S2[:], T.UP[:], -2.0, 1.0, ALU.mult, ALU.add)
     ts(["IR", "GF"], ["G8"], T.G8[:], T.IR[:, 0:8], col("GF"), None, ALU.is_equal)
+    tt(["SB", "UP"], ["A1"], T.A1[:], T.SB[:], T.UP[:], ALU.mult)
+    tt(["NM", "S2"], ["A2"], T.A2[:], T.NM[:], T.S2[:], ALU.mult)
+    ts(["IV"], ["SEL"], T.SEL[0:24, :], T.IV[0:24, :, 0:8], 0.0, None, ALU.is_equal)
+    tt(["SB", "A1"], ["A0"], T.A0[:], T.SB[:], T.A1[:], ALU.subtract)
+    ts(["SB", "A2"], ["PB"], T.PB[:], T.SB[:], col("A2"), 0.5, ALU.add, ALU.mult)
+    ts(["G8", "A1"], ["CM1"], T.CM[:, 8:16], T.G8[:], col("A1"), None, ALU.mult)
+    ts(["RI"], ["XE"], T.XE[:], T.RI[:], 0.5, FAR, ALU.is_lt, ALU.mult)
+    ts(["G8", "A0"], ["CM0"], T.CM[:, 0:8], T.G8[:], col("A0"), None, ALU.mult)
+    vc(["RI"], ["RF"], T.RF[:], T.RI[:])
     ts(["CC"], ["CLz"], T.CL[:, 0:256], T.CC[:, 0:256], 4095, None, ALU.bitwise_and)
     ts(["CC"], ["CLw"], T.CL[:, 256:384], T.CC[:, 256:384], 255, None, ALU.bitwise_and)
-    tt(["NM", "S2"], ["A2"], T.A2[:], T.NM[:], T.S2[:], ALU.mult)
-    tt(["SB", "UP"], ["A1"], T.A1[:], T.SB[:], T.UP[:], ALU.mult)
-    tt(["OH", "LX8"], ["TX"], T.TX[:], T.OH[:], T.LX[:], ALU.mult)
-    ts(["SB", "A2"], ["PB"], T.PB[:], T.SB[:], col("A2"), 0.5, ALU.add, ALU.mult)
-    tt(["SB", "A1"], ["A0"], T.A0[:], T.SB[:], T.A1[:], ALU.subtract)
-    op("V", v.tensor_reduce, ["TX"], ["XE"], T.XE[:], T.TX[:], AxisListType.X, ALU.add)
-    ts(["IR", "KF"], ["IDf"], T.IDf[:], T.IR[:], col("KF"), None, ALU.is_equal)
+    ts(["W2e", "XE"], ["Xe"], T.X[:, M:M + 8], T.W2[:, M:M + 8], col("XE"), 1.0, ALU.add, ALU.add)
+    ts(["IR", "RF"], ["OH"], T.OH[:], T.IR[:, 0:16], col("RF"), None, ALU.is_equal)
     for i in range(4):
         op("V", v.transpose, ["B0"], ["OT%d" % i], T.OT[:, i::4], T.B0[:, :, i, :])
-    ts(["IR", "XE"], ["Xe"], T.X[:, M:M + 8], T.IR[:, 0:8], 0.0, col("XE"), ALU.mult, ALU.add)
-    fill("OSe", T.OS[:, 128:130], M)
-    ts(["RF"], ["R128"], T.R128[:], T.RF[:], 128.0, None, ALU.mult)
+    fill("C1", T.C1[:], 0.0)
     vc(["OT%d" % i for i in range(4)], ["OS"], T.OS[:, 0:128], T.OT[:])
-    ts(["G8", "A1"], ["CM1"], T.CM[:, 8:16], T.G8[:], col("A1"), None, ALU.mult)
-    ts(["IR", "KF"], ["TRI"], T.TRI[:], T.IR[:], col("KF"), None, ALU.is_gt)
-    ts(["G8", "A0"], ["CM0"], T.CM[:, 0:8], T.G8[:], col("A0"), None, ALU.mult)
-    fill("ONE", T.ONE[:], 1.0)
-    ts(["IR", "R128"], ["NI"], T.NI[:], T.IR[:], col("R128"), None, ALU.add)
-    ts(["KF"], ["KF2"], T.KF2[:], T.KF[:], 2.0, None, ALU.mult)
-    ts(["KF"], ["KF3"], T.KF3[:], T.KF[:], 2.0, 1.0, ALU.mult, ALU.add)
-    ts(["IK"], ["R3"], T.R3[:], T.IK[:], 3, 7, ALU.logical_shift_right, ALU.bitwise_and)
-    ts(["KF"], ["G6"], T.G6[:], T.KF[:], 63.5, 6.0, ALU.is_gt, ALU.mult)
-    ts(["R8"], ["R7"], T.R7[:], T.R8[:], 5.5, 100.0, ALU.is_gt, ALU.mult)
-    vc(["R3"], ["QM"], T.QM[:], T.R3[:])
-    ts(["R8", "G6", "R7"], ["T2"], T.T2[:], T.R8[:], col("G6"), col("R7"), ALU.add, ALU.add)
-    ts(["G16", "QM"], ["MK"], T.MK[:], T.G16[:], col("QM"), None, ALU.is_equal)
-    vc(["BXa"], ["N0"], T.N0[:], T.BXi[:, 0:1])
-    ts(["IR", "T2"], ["SN"], T.SN[:], T.IR[:, 0:12], col("T2"), None, ALU.is_equal)
-    fill("RZ", T.RW[:, 96::RWW], 0.0)
-    fill("ZL", T.ZL[:], 0.0)
+    for (t, n, c) in ((1, "A2", K * K), (4, "A0", -KP), (5, "A0", -KP), (6, "SB", -KP), (8, "A2", K * K), (11, "A0", -K0),
+                      (12, "SB", -K6)):
+        ts(["G8", n, "C1"], ["C1_%d" % t], T.C1[:, t // 7, t % 7::7], T.G8[:], col(n), c, ALU.mult, ALU.mult)
+    act(["IK"], ["NK"], T.NK[:], T.IK[:], COPY, scale=-1.0)
+    act(["Pi"], ["Pf"], T.Pf[0:24, :], T.Pi[0:24, :], COPY)
+    mm(["SEL", "Pf"], ["Q0"], T.Q0[:, 0:256], T.SEL[0:24, :], T.Pf[0:24, :], True, True)
+    act(["IR", "NK"], ["X0B"], T.X0B[:], T.IR[:], FN.Abs, bias=col("NK"))
+    act(["IR", "NK"], ["RU"], T.RU[:], T.IR[:], FN.Relu, bias=col("NK"))
+    act(["IK"], ["KF2"], T.KF2[:], T.IK[:], COPY, scale=2.0)
+    act(["X0B"], ["IDf"], T.IDf[:], T.X0B[:], FN.Relu, scale=-1.0, bias=1.0)
     act(["Q0", "PB"], ["PL0"], T.PL[:, OWN:OWN + 256], T.Q0[:, 0:256], IDENT, bias=col("PB"))
-    for (n, s) in (("DG", -96.0), ("DN", -256.0), ("DS", -16.0), ("IDh", 1.0), ("IDb", 1.0)):
+    act(["RU"], ["TRI"], T.TRI[:], T.RU[:], FN.Sign)
+    act(["IK"], ["KF3"], T.KF3[:], T.IK[:], IDENT, scale=2.0, bias=1.0)
+    act(["IR"], ["ONE"], T.ONE[:], T.IR[:], IDENT, scale=0.0, bias=1.0)
+    for (n, s) in (("DG", -96.0), ("DS", -16.0), ("DN", -256.0)):
         act(["IDf"], [n], T[n][:], T.IDf[:], COPY, scale=s)
 
     def column(n, r, c, plus=None):
@@ -244,47 +248,61 @@ def rank_program(g, core, T, topo):
         else:
             act(["OH", plus], [n], col(n), row(r), IDENT, scale=c, bias=col(plus))
 
+    for x in (("T0", 13, K), ("T1", 10, K), ("V2", 7, 256.0, 15), ("U0", 3, 256.0, 11), ("U1", 4, 256.0, 12),
+              ("P5", 14, -3 * KP, 1), ("P6", 14, 6 * KP, 9), ("E25", 2, 1.0, 5)):
+        column(*x)
+
     def coefficients():
         act(["G8"], ["G8N"], T.G8N[:], T.G8[:], COPY, scale=-1.0)
-        for x in (("T0", 13, K), ("T1", 10, K), ("V2", 7, 256.0, 15), ("U0", 3, 256.0, 11), ("U1", 4, 256.0, 12),
-                  ("P5", 14, -3 * KP, 1), ("P6", 14, 6 * KP, 9), ("E25", 2, 1.0, 5), ("ZH", 5, 4096 * K, "T0"),
-                  ("ZL0", 2, 4096 * K, "T1"), ("V3", 14, -256 * UP16, "V2"), ("U4", 14, 3 * K0 - C - 256 * UP16, "U0"),
-                  ("U2", 14, -6 * K6 - 512 * UP16, "U1"), ("ZL1", 14, 2 * K * K, "ZL0")):
+        for x in (("ZH", 5, 4096 * K, "T0"), ("ZL0", 2, 4096 * K, "T1"), ("V3", 14, -256 * UP16, "V2"),
+                  ("U4", 14, 3 * K0 - C - 256 * UP16, "U0"), ("U2", 14, -6 * K6 - 512 * UP16, "U1"), ("ZL1", 14, 2 * K * K, "ZL0")):
             column(*x)
+        for j in range(4):
+            act(["G8", "OH"], ["G87"], T.G87[:, 8 * j:8 * j + 8], T.G8[:], COPY, scale=row(7))
+        act(["G8", "OH"], ["T3"], T.G8E[:], T.G8[:], COPY, scale=row(14))
         act(["U0", "U2"], ["U5"], col("U5"), col("U0"), IDENT, bias=col("U2"))
-        for (t, n, c) in ((2, "G8N", 6), (3, "G8", 0), (0, "G8", "ZH"), (1, "G8", "ZL1"), (5, "G8", "P5"), (6, "G8N", "P6"),
-                          (7, "G8", "ZH"), (8, "G8", "ZL1"), (10, "G8", "V3"), (11, "G8N", "U4"), (12, "G8", "U5")):
-            act([n, "OH" if c in range(16) else c], ["C2_%d" % t], T.C2[:, t // 7, t % 7::7], T[n][:], COPY,
-                scale=row(c) if c in range(16) else col(c))
-        act(["G8", "OH"], ["T3"], T.G87[:], T.G8[:], COPY, scale=row(14))
-        for (t, c) in ((4, -2.5 * KP), (9, -C), (13, 0.0)):
-            act(["T3"], ["C2"], T.C2[:, t // 7, t % 7::7], T.G87[:], COPY, scale=c)
         act(["G8", "E25"], ["CZ0"], T.CZ[:, 0::2], T.G8[:], COPY, scale=col("E25"))
         act(["G8", "OH"], ["CZ"], T.CZ[:, 1::2], T.G8[:], COPY, scale=row(2))
-        act(["G8", "OH", "C2"], ["G87"], T.G87[:], T.G8[:], COPY, scale=row(7))
+        for (t, c) in ((4, -2.5 * KP), (9, -C), (13, -2.0 ** 60)):
+            act(["T3"], ["C2_%d" % t], T.C2[:, t // 7, t % 7::7], T.G8E[:], COPY, scale=c)
+        for (t, n, c) in ((2, "G8N", 6), (3, "G8", 0), (0, "G8", "ZH"), (1, "G8", "ZL1"), (5, "G8", "P5"), (6, "G8N", "P6"),
+                          (7, "G8", "ZH"), (8, "G8", "ZL1"), (10, "G8", "V3"), (11, "G8N", "U4"), (12, "G8", "U5")):
+            act([n, "OH" if c in range(16) else c], ["C2"], T.C2[:, t // 7, t % 7::7], T[n][:], COPY,
+                scale=row(c) if c in range(16) else col(c))
+        act(["BXa"], ["N0"], T.N0[:], T.BXi[:, 0:1], COPY)
+        act(["IDf"], ["IDh"], T.IDh[:], T.IDf[:], COPY)
         act(["N0", "IR"], ["X0B"], T.X0B[:], T.IR[:], IDENT, scale=0.0, bias=col("N0"))
 
-    dmas("dL", ["CLz", "CLw"], ["Xb"], [("S", T.X[r::16, 0:M], T.CL[:, 128 * i:128 * i + 128]) for i, r in enumerate((10, 13, 15))])
-    X = ["Xa", "Xb", "Xe"]
-    coefficients()
-    act(X + ["OS", "OSe"], ["G"], T.G[:], T.X[:].indirect(T.OS[:, 0:129]), COPY)
-    dmas("dW", ["W1e", "BXi"], ["W1a"], [("S", T.W1[r + 8 * i::16, 0:M - i], T.nodes[r::16, i:M]) for i in (0, 1) for r in range(6)])
-    dmas("dU", X + ["NI"], ["W2a"],
-         [("S", T.W2[0::8, 0:M], T.X[6::8, 0:M]), ("S", T.W2[3::8, 0:M], T.X[7::8, 0:M]), ("S", T.W2[4::8, 0:M], T.X[7::8, 1:M + 1]),
-          ("S", T.W2[1::16, 0:M], T.X[6::16, 1:M + 1]), ("S", T.W2[9::16, 0:M], T.NI[:])])
-    dmas("dV", ["G", "W1e", "W2e"], ["W1b", "W2b"],
-         [("S", T.W1[6 + i::8, 0:M + 2], T.G[i::8, 0:M + 2]) for i in (0, 1)]
-         + [("S", T.W2[r::8, 0:M + 2], T.G[r::8, 0:M + 2]) for r in (2, 5, 6, 7)])
-    W1, W2 = ["W1a", "W1b"], ["W2a", "W2b"]
-
     tt(["BXa", "BXi"], ["BX"], T.BX[:], T.BXi[:, 0:8:2], T.BXi[:, 8:12], ALU.add)
-    for e in range(4):
-        ts(["PL0", "BX"], ["F0_%d" % e], T.F0[:, e * 256:e * 256 + 256], T.PL[:, OWN:OWN + 256], T.BX[:, e:e + 1], None, ALU.is_lt)
+    for e in (2, 0, 3, 1):
+        out, pts = T.F0[:, e * 256:e * 256 + 256], T.PL[:, OWN:OWN + 256]
+        if e < 2:
+            act(["PL0", "BX"], ["F0_%d" % e], out, pts, FN.Sign, scale=-1.0, bias=T.BX[:, e:e + 1])
+        else:
+            ts(["PL0", "BX"], ["F0_%d" % e], out, pts, T.BX[:, e:e + 1], 2.0, ALU.is_lt, ALU.mult)
         for b in (0, 1):
             for (at, x, y) in (((112 + 8 * b, 0, 8), (56 * b, 8, 16)) if e == 0 else ((56 * b + 16 * e - 8, 0, 16),)):
                 mm(["F0_%d" % e, "CM0", "CM1"], ["Q1"], T.Q1[:, at:at + y - x], T.F0[:, e * 256 + b:e * 256 + 256:2], T.CM[:, x:y],
                    True, True)
-    ts(["Q1"], ["HB"], T.HB[:], T.Q1[:, 0:128], -2.5, None, ALU.is_lt)
+    ts(["RF"], ["R128"], T.R128[:], T.RF[:], 128.0, None, ALU.mult)
+    ts(["IK"], ["P8"], T.P8[:], T.IK[:], 3, None, ALU.logical_shift_right)
+    vc(["R8"], ["R8F"], T.R8F[:], T.R8[:])
+    fill("RZ", T.RW[:, 96::RWW], 0.0)
+    ts(["IR", "R128"], ["NI"], T.NI[:], T.IR[:], col("R128"), None, ALU.add)
+    ts(["Q1"], ["HB"], T.HB[:], T.Q1[:, 0:128], -5.0, None, ALU.is_lt)
+
+    dmas("dL", ["CLz", "CLw"], ["Xb"], [("S", T.X[r::16, 0:M], T.CL[:, 128 * i:128 * i + 128]) for i, r in enumerate((10, 13, 15))])
+    X = ["Xa", "Xb", "Xe"]
+    act(X + ["OS", "OSe"], ["G"], T.G[:], T.X[:].indirect(T.OS[:, 0:129]), COPY)
+    coefficients()
+    dmas("dW", ["W1e", "BXi"], ["W1a"], [("S", T.W1[r + 8 * i::16, 0:M - i], T.nodes[r::16, i:M]) for i in (0, 1) for r in range(6)])
+    dmas("dU", X + ["NI"], ["W2a"],
+         [("S", T.W2[0::8, 0:M], T.X[6::8, 0:M]), ("S", T.W2[3::8, 0:M], T.X[7::8, 0:M]), ("S", T.W2[4::8, 0:M], T.X[7::8, 1:M + 1]),
+          ("S", T.W2[1::16, 0:M], T.X[6::16, 1:M + 1]), ("S", T.W2[9::16, 0:M], T.NI[:])])
+    dmas("dV", ["G", "W1e", "W2e", "Xe"], ["W1b", "W2b"],
+         [("S", T.W1[6 + i::8, 0:M + 2], T.G[i::8, 0:M + 2]) for i in (0, 1)]
+         + [("S", T.W2[r::8, 0:M + 2], T.G[r::8, 0:M + 2]) for r in (2, 5, 6, 7)])
+    W1, W2 = ["W1a", "W1b"], ["W2a", "W2b"]
 
     def ranks(ps, last):
         mm(["HB", "TRI"], [ps], T[ps][:, 0:112], T.TRI[:], T.HB[:, 0:112], True, False)
@@ -293,33 +311,38 @@ def rank_program(g, core, T, topo):
 
     ranks("Q2", True)
     ranks("Q1", False)
-    mm(["HB", "DN"], ["Q2"], T.Q2[:, 112:128], T.DN[:], T.HB[:, 112:128], True, True)
-    fill("LS", T.LS[:], 1.0)
-    fill("LB", T.LB[:], 0.0)
-    fill("C1", T.C1[:], 0.0)
+    fill("OF1", T.OF1[:], 1)
+    fill("Z", T.Z[:], 0.0)
+    vc(["P8"], ["P8F"], T.P8F[:], T.P8[:])
     ts(["Q2"], ["HI"], T.HI[:, 0:112], T.Q2[:, 0:112], 1 / 16, 6 + UP16 - 0.5 + 1 / 32, ALU.mult, ALU.add)
     mm(["HI", "DS"], ["Q1"], T.Q1[:, 0:112], T.DS[:], T.HI[:, 0:112], False, True)
+    mm(["HB", "DN"], ["Q2"], T.Q2[:, 112:128], T.DN[:], T.HB[:, 112:128], True, True)
+    ts(["IR", "P8F"], ["SN"], T.SN[:], T.IR[:, 0:16], col("P8F"), None, ALU.is_equal)
     for n in range(6):
         for b in (0, 1):
-            ts(["HI", "HM", "KF2", "KF3"], ["HM%d" % b], T.HM[:, 448 * b + n:448 * b + 448:8], T.HI[:, 56 * b:56 * b + 56], UP16 + n,
+            ts(["HI", "KF2", "KF3"], ["HM%d" % b], T.HM[:, 7 * b:7 * b + 7, 8 * n:8 * n + 8], T.HI[:, 56 * b:56 * b + 56], UP16 + n,
                col("KF3" if b else "KF2"), ALU.is_equal, ALU.mult)
         if n == 1:
             ts(["Q1"], ["LO"], T.LO[:, 0:112], T.Q1[:, 0:112], 96 + 16 * UP16, None, ALU.add)
     for c in range(16):
         ts(["LO"], ["LM"], T.LM[:, c::16], T.LO[:, 0:112], float(c), None, ALU.is_equal)
     BANK = ("Q3", "Q4", "Q5", "Q0")
-    for i, ds in enumerate(PAIRS):
-        for h, d in enumerate(ds):
+
+    def product(i):
+        for h, d in enumerate(PAIRS[i]):
             for b in (0, 1):
                 k = 7 * b + d - 1
-                mm(["HM0", "HM1", "LM"], [BANK[i]], T[BANK[i]][64 * h:64 * h + 64, 0:128], T.HM[:, 64 * k:64 * k + 64],
+                mm(["HM", "HM0", "HM1", "LM"], [BANK[i]], T[BANK[i]][64 * h:64 * h + 64, 0:128], T.HM[:, k, :],
                    T.LM[:, 128 * k:128 * k + 128], b == 0, b == 1)
 
     def own_scene(i):
         n, ps, m = 64 * len(PAIRS[i]), "PS%d" % (i % 2), "MM%d" % i
         tt([BANK[i], "MK"], [m], T[m][0:n, :], T[BANK[i]][0:n, 0:128], T.MK[0:n, :], ALU.mult)
-        mm([m, "SN"], [ps], T[ps][:, 0, 0:12], T[m][0:n, :], T.SN[0:n, :], True, True)
-        act([ps], ["IX%d" % i], T.IX[:, 12 * i:12 * i + 12], T[ps][:, 0, 0:12], COPY)
+        mm([m, "SN"], [ps], T[ps][:, :, 0:8], T[m][0:n, :], T.SN[0:n, :], True, True)
+
+    def list_(i):
+        ps = "PS%d" % (i % 2)
+        vc([ps], ["IX%d" % i], T.IX[:, 12 * i:12 * i + 12], T[ps][:, :, 0:6])
 
     def pick(i):
         ds = PAIRS[i]
@@ -331,51 +354,48 @@ def rank_program(g, core, T, topo):
         for d in ds:
             note((None, "pt%d" % d, total["pt%d" % d]), [], ["PL%d" % d])
 
-    await_("V", wr["LS"] + wr["LB"])
-    for (x, c) in ((slice(2, 6, 3), 2.0 ** -12), (slice(3, 5), 2.0 ** -8), (slice(7, 8), 2.0 ** -8)):
-        fill("LS1", T.LS[:, x], c)
-    own_scene(0)
-    own_scene(1)
-    fill("LB1", T.LB[:, 14:15], 1.0)
-    own_scene(2)
-    pick(0)
-    own_scene(3)
-    for i in (1, 2, 3):
-        pick(i)
-    for b in (0, 1):
-        act(["Q2", "ZL"], ["ZL%d" % b], T.ZL[:, 142 + b:1030:16], T.Q2[:, 56 * b:56 * b + 56], IDENT, bias=96.0)
-        act(["Q2", "ZL", "KF2", "KF3"], ["ZO%d" % b], T.ZL[:, 14 + b:128:16], T.Q2[:, 112 + 8 * b:120 + 8 * b], IDENT,
-            bias=col("KF3" if b else "KF2"))
-    for (x, c) in ((slice(2, 6, 3), UP16 - 0.5 + 2.0 ** -13), (slice(3, 5), UP16 - 0.5 + 2.0 ** -9), (slice(7, 8), UP16 - 0.5 + 2.0 ** -9),
-                   (slice(10, 14, 3), -2048.0), (slice(1, 7, 5), -SH), (slice(0, 1), 1 - SH), (slice(9, 10), 2 - SH)):
-        fill("LB1", T.LB[:, x], c)
+    product(0)
+    product(1)
+    ts(["G16", "R8F"], ["MK"], T.MK[:], T.G16[:], col("R8F"), None, ALU.is_equal)
     tt(["OH", "LS1"], ["TS"], T.TS[:], T.OH[:], T.LS[:], ALU.mult)
-    fill("OF1", T.OF1[:], 1)
     tt(["OH", "LB1"], ["TB"], T.TB[:], T.OH[:], T.LB[:], ALU.mult)
     op("V", v.tensor_reduce, ["TS"], ["SC"], T.SC[:], T.TS[:], AxisListType.X, ALU.add)
-    for b in "01":
-        fill("D0_" + b, T["D0_" + b][:], 0.0)
+    own_scene(0)
+    product(2)
     op("V", v.tensor_reduce, ["TB"], ["BI"], T.BI[:], T.TB[:], AxisListType.X, ALU.add)
-    for (t, n, c) in ((1, "A2", K * K), (4, "A0", -KP), (5, "A0", -KP), (6, "SB", -KP), (8, "A2", K * K), (11, "A0", -K0),
-                      (12, "SB", -K6)):
-        ts(["G8", n, "C1"], ["C1_%d" % t], T.C1[:, t // 7, t % 7::7], T.G8[:], col(n), c, ALU.mult, ALU.mult)
-    vc(W1 + ["D0_1"], ["N1"], T.N1[:], T.W1[:, 1:2])
-    for b in "01":
-        fill("D0a" + b, T["D0_" + b][:, 0::7], -2.0 ** 60)
-        fill("Z" + b, T["Z" + b][:], 0.0)
-        fill("SPz" + b, T["SP" + b][:, 6::7, :], 0.0)
+    own_scene(1)
+    product(3)
+    list_(0)
+    own_scene(2)
+    list_(1)
+    pick(0)
+    own_scene(3)
+    list_(2)
+    pick(1)
+    list_(3)
+    pick(2)
+    pick(3)
+    whole("ZL", T.ZL[:], 1040, 0)
+    whole("ZS", T.ZS[:], 512, 0)
+    op("V", v.tensor_reduce, ["OH"], ["E012"], T.E012[:], T.OH[:, 0:3], AxisListType.X, ALU.add)
+    fill("SYz", T.SY[:], 0.0)
+    fill("RO", T.RO[:, 256:272], 0.0)
+    ts(["G8", "E012", "SYz"], ["SY"], T.SY[:, 3:35:4], T.G8[:], col("E012"), -1.0, ALU.mult, ALU.mult)
+    vc(W1, ["N1"], T.N1[:], T.W1[:, 1:2])
 
     def points(b):
         return ["PL%d" % d for d in (FIRST if b == 0 else (0, 1, 2))]
 
     def depth(b):
         lo, n = BATCH[b]
-        ps = "Q%d" % b
-        for j in range(4):
-            mm(points(b) + ["CZ0", "CZ"], [ps], T[ps][0:n // 4, 16 * j:16 * j + 16], T.PL[:, lo + j:lo + n:4], T.CZ[:], True, True)
-        for i in (0, 1):
-            act([ps, "D0_%d" % b, "D0a%d" % b], ["D0b%d" % b], T["D0_%d" % b][0:n // 4, 1 + i::7], T[ps][0:n // 4, i:64:2],
-                IDENT, scale=K, bias=(2 - i) * Z0 * K)
+        ps, d0, m = "Q%d" % b, "D0_%d" % b, n // 4
+        for (x, y) in ((0, 96), (96, m)):
+            for j in range(4):
+                mm(points(b)[:4 if x == 0 else 5] + ["CZ0", "CZ"], [ps], T[ps][x:y, 16 * j:16 * j + 16],
+                   T.PL[:, lo + 4 * x + j:lo + 4 * y:4], T.CZ[:], True, True)
+        for c in (0, 1):
+            for i in (0, 1):
+                act([ps, d0], [d0 + "_%d" % c], T[d0][0:m, c, 1 + i::7], T[ps][0:m, i:64:2], IDENT, scale=K, bias=(2 - i) * Z0 * K)
 
     def rows(b, part):
         n, of = BATCH[b][1], "OF%d" % b
@@ -385,45 +405,46 @@ def rank_program(g, core, T, topo):
 
     def tests(b, t, part):
         lo, n = BATCH[b]
-        x, y = (0, CUT) if part == 0 else (CUT, n)
+        cut = CUT if t else (384, 256)[b]
+        x, y = (0, cut) if part == 0 else (cut, n)
         of, d1, out, pt = "OF%d" % b, "D1_%d_%d" % (b, part), T["D1_%d" % b][:, x:y], T.PL[:, lo + x:lo + y]
         if t == 0:
-            ts(["N1"] + points(b), [d1], out, pt, col("N1"), None, ALU.is_lt)
+            ts(["N1"] + (points(b) if part else points(b)[:(4, 1)[b]]), [d1], out, pt, col("N1"), None, ALU.is_lt)
         else:
             tt(W1 + points(b) + [of], [d1], out, T.W1[:, 0:M + 2].indirect(T[of][:, x // 16:y // 16]), pt, ALU.is_gt)
 
-    def sums(b, i, first=False):
-        n, ps, d = BATCH[b][1], "PS%d" % b, "D%d_%d" % (i, b)
-        for j in range(4):
-            mm((["D2"] if first else [d + "_0", d + "_1"]) + ["C2" if i == 2 else "C1_12"], [ps], T[ps][0:n // 4, :, 56 * j:56 * j + 56],
-               T.D2[:, 0:n // 4] if first else T[d][:, j:n:4], T["C%d" % i][:], i == 2 and j == 0, i == 1 and j == 3)
+    def bank(b, c, x, y):
+        m = BATCH[b][1] // 4
+        return ("PS%d" % b, T["PS%d" % b][0:m, 0, x:y]) if c == 0 else ("Q%d" % (3 + 2 * b), T["Q%d" % (3 + 2 * b)][0:m, x:y])
 
-    def scan(b, x, out, i, lo, hi):
-        m, ps = BATCH[b][1] // 4, "PS%d" % b
-        op("V", v.tensor_tensor_scan, [ps, "D0b%d" % b, "SPz%d" % b], [x], out,
-           T["D0_%d" % b][0:m, lo:hi], T[ps][0:m, i, lo:hi], 0.0, ALU.subtract, ALU.max)
+    def sums(b, i, c, first=False):
+        n, d = BATCH[b][1], "D%d_%d" % (i, b)
+        for j in range(4):
+            ps, out = bank(b, c, 56 * j, 56 * j + 56)
+            mm((["D2"] if first else [d + "_0", d + "_1"]) + ["C2" if i == 2 else "C1_12"], [ps], out,
+               T.D2[:, 0:n // 4] if first else T[d][:, j:n:4], T["C%d" % i][:, c], i == 2 and j == 0, i == 1 and j == 3)
 
     def nodes(b):
-        m, z, ex = BATCH[b][1] // 4, "Z%d" % b, "Q%d" % b
+        m, ps, d0, sp = BATCH[b][1] // 4, "PS%d" % b, "D0_%d" % b, "SP%d" % b
         for j in range(4):
-            scan(b, "SP%d" % b, T["SP%d" % b][0:m, :, j], 0, 56 * j, 56 * j + 56)
-        act(["SP%d" % b, z], [z + "v"], T[z][0:m, 12:140], T["SP%d" % b][0:m, 6::7, :], COPY, scale=-1.0)
+            op("V", v.tensor_tensor_scan, [ps, d0 + "_0", "SPz%d" % b], [sp], T[sp][0:m, :, j], T[d0][0:m, 0, 56 * j:56 * j + 56],
+               T[ps][0:m, 0, 56 * j:56 * j + 56], 0.0, ALU.subtract, ALU.max)
+        act([sp, "Z"], ["Z%d" % b], T.Z[0:m, b, 12:140], T[sp][0:m, 6::7, :], COPY, scale=-1.0)
 
     def turn(b):
-        m, z, ex = BATCH[b][1] // 4, "Z%d" % b, "Q%d" % b
+        m, ex = BATCH[b][1] // 4, "Q%d" % b
         for i in range(4):
-            mm([z + "v", "IDh"], [ex], T[ex][:, 0:m // 4], T[z][0:m, 12 - 4 * i:140 - 4 * i], T.IDh[0:m, i:m:4], i == 0, i == 3)
+            mm(["Z%d" % b, "IDh"], [ex], T[ex][:, 0:m // 4], T.Z[0:m, b, 12 - 4 * i:140 - 4 * i], T.IDh[0:m, i:m:4], i == 0, i == 3)
         act([ex], ["OF%d" % b], T["OF%d" % b][:, 0:m // 4], T[ex][:, 0:m // 4], IDENT, bias=SH)
 
     def weights(b):
-        scan(b, "WS%d" % b, T["WS%d" % b][0:BATCH[b][1] // 4, :], 1, 0, 224)
+        m, d0, ws = BATCH[b][1] // 4, "D0_%d" % b, "WS%d" % b
+        ps, x = bank(b, 1, 0, 224)
+        op("V", v.tensor_tensor_scan, [ps, d0 + "_1", d0 + "_s"], [ws], T[ws][0:m, :], T[d0][0:m, 1, :], x, 0.0, ALU.subtract, ALU.max)
 
-    def add_up(b, t):
-        m, ac = BATCH[b][1] // 4, "Q%d" % (2 + b)
-        mm(["WS%d" % b, "IDf"], [ac], T[ac][0:m, 0:32], T.IDf[0:m, 0:m], T["WS%d" % b][0:m, 5::7], t == 0, t == STEPS - 1)
-        if t == 1:
-            for j in range(4):
-                mm(["X0B", "G87"], [ac], T[ac][0:m, 8 * j:8 * j + 8], T.X0B[:, 0:m], T.G87[:], False, False)
+    def carry(b):
+        m, d0, ws = BATCH[b][1] // 4, "D0_%d" % b, "WS%d" % b
+        op("G", g.affine_select, [ws], [d0 + "_s"], T[d0][0:m, 1, 6::7], T[ws][0:m, 6::7], [[0, 32]], ALU.is_ge, 0.0, 0, 0)
 
     def send(ds, tag, lanes):
         at = [slot(d) if d in FIRST else slot(d) - 256 for d in ds]
@@ -433,54 +454,59 @@ def rank_program(g, core, T, topo):
 
     def pieces(b):
         n = BATCH[b][1]
-        m, ac, h, zs, ps = n // 4, "Q%d" % (2 + b), T["H%d" % b], "ZS%d" % b, "Q%d" % (4 + b)
+        m, ws, h, ps = n // 4, "WS%d" % b, T["H%d" % b], "Q%d" % (4 - 2 * b)
         for i, e in enumerate((44, 37, 30)):
-            ts([ac], ["H%d_%d" % (b, i)], h[0:m, i], T[ac][0:m, 0:32], 1.5 * 2.0 ** e, 1.5 * 2.0 ** e, ALU.add, ALU.subtract)
+            ts([ws], ["H%d_%d" % (b, i)], h[0:m, i], T[ws][0:m, 6::7], 1.5 * 2.0 ** e, 1.5 * 2.0 ** e, ALU.add, ALU.subtract)
         for i in (0, 1):
-            tt(["H%d_%d" % (b, i), "H%d_%d" % (b, i + 1), zs], [zs + "_%d" % i], T[zs][0:m, i::16], h[0:m, i + 1], h[0:m, i],
-               ALU.subtract)
-        tt([ac, "H%d_2" % b, zs], [zs + "_2"], T[zs][0:m, 2::16], T[ac][0:m, 0:32], h[0:m, 2], ALU.subtract)
+            tt(["H%d_%d" % (b, i), "H%d_%d" % (b, i + 1), "ZS"], ["ZS_%d" % i], T.ZS[0:m, i::16], h[0:m, i + 1], h[0:m, i], ALU.subtract)
+        tt([ws, "H%d_2" % b, "ZS"], ["ZS_2"], T.ZS[0:m, 2::16], T[ws][0:m, 6::7], h[0:m, 2], ALU.subtract)
         for j in range(4):
-            mm([zs + "_0", zs + "_1", zs + "_2", "IDb"], [ps], T[ps][:, j:n:4], T[zs][0:m, 128 * j:128 * j + 128], T.IDb[0:m, 0:m],
-               True, True)
+            mm(["ZS_0", "ZS_1", "ZS_2", "IDb"], [ps], T[ps][:, j:n:4], T.ZS[0:m, 128 * j:128 * j + 128], T.IDb[0:m, 0:m], True, True)
         if b == 0:
-            act([ps], ["SA0"], T.SA[:, 0:480], T[ps][:, 0:480], COPY)
-            send(FIRST, "SA0", (4, 4, 4, 2, 2))
+            act([ps], ["SA0"], T.SA[:, 0:384], T[ps][:, 0:384], COPY)
+            send(FIRST[:4], "SA0", (4, 4, 4, 4))
+            act([ps], ["SA2"], T.SA[:, 384:480], T[ps][:, 384:480], COPY)
         else:
             act([ps], ["SA1"], T.SA[:, 480:672], T[ps][:, 256:448], COPY)
-            send((1, 2), "SA1", (8, 8))
+            send((1, 2, 7), "SA1", (4, 4, 8))
             act([ps], ["RV0"], T.RO[:, 0:256], T[ps][:, 0:256], COPY)
 
     def spare(s):
-        if s in (2, 3, 4, 5):
-            for d in (2 * s - 4, 2 * s - 3):
+        if s in (2, 3):
+            b = s - 2
+            act(["Q2", "ZL"], ["ZL%d" % b], T.ZL[:, 142 + b:1030:16], T.Q2[:, 56 * b:56 * b + 56], IDENT, bias=96.0)
+        if s in (4, 5):
+            b = s - 4
+            act(["Q2", "ZL", "KF2", "KF3"], ["ZO%d" % b], T.ZL[:, 14 + b:128:16], T.Q2[:, 112 + 8 * b:120 + 8 * b], IDENT,
+                bias=col("KF3" if b else "KF2"))
+        if s in (6, 7, 8, 9):
+            for d in (2 * s - 12, 2 * s - 11):
                 for i in range(8):
-                    mm(["ZL0", "ZL1", "ZO0", "ZO1", "IDh"], ["Q4"], T.Q4[:, d * 16:d * 16 + 16],
-                       T.ZL[:, 128 * d + 14 - 2 * i:128 * d + 142 - 2 * i], T.IDh[:, i::8], i == 0, i == 7)
-        if s in (1, 2):
-            fill("ZS%d" % (s - 1), T["ZS%d" % (s - 1)][:], 0.0)
-        if s == 3:
-            op("V", v.tensor_reduce, ["OH"], ["E012"], T.E012[:], T.OH[:, 0:3], AxisListType.X, ALU.add)
-            fill("RO", T.RO[:, 256:272], 0.0)
-        if s == 4:
-            ts(["G8", "E012"], ["SY"], T.SY[:], T.G8[:], col("E012"), None, ALU.mult)
-        if s == 6:
+                    mm(["ZL0", "ZL1", "ZO0", "ZO1", "IDb"], ["Q4"], T.Q4[:, d * 16:d * 16 + 16],
+                       T.ZL[:, 128 * d + 14 - 2 * i:128 * d + 142 - 2 * i], T.IDb[:, i::8], i == 0, i == 7)
+        if s == 10:
             ts(["Q4"], ["GO0"], T.GO[:, 0:16], T.Q4[:, 0:16], 256.0, 256.0, ALU.add, ALU.min)
-        if s == 7:
+        if s == 11:
             ts(["Q4"], ["GO1"], T.GO[:, 16:128], T.Q4[:, 16:128], 96.0, None, ALU.min)
 
     act(W2 + ["OF1", "BI", "SC"], ["D2"], T.D2[:], T.W2[:, 0:M + 2].indirect(T.OF1[:, 0:8]), IDENT, scale=col("SC"), bias=col("BI"))
+    mm(["X0B", "G87"], ["Q4"], T.Q4[:, 0:32], T.X0B[:], T.G87[:], True, True)
+    for b in (0, 1):
+        act(["Q4", "D0_%d" % b], ["D0_%d_s" % b], T["D0_%d" % b][:, 1, 6::7], T.Q4[:, 0:32], COPY, scale=-1.0)
+        for c in (0, 1):
+            sums(b, 2, c, True)
+    act(["IDf"], ["IDb"], T.IDb[:], T.IDf[:], COPY)
     depth(0)
-    sums(0, 2, True)
-    sums(1, 2, True)
+    tests(1, 0, 0)
     tests(0, 0, 0)
     tests(0, 0, 1)
-    sums(0, 1)
+    sums(0, 1, 0)
+    sums(0, 1, 1)
     for s in range(1, 2 * STEPS + 1):
         b, t = s % 2, s // 2
         o, u = 1 - b, (s - 1) // 2
         more = u < STEPS - 1
-        if s < 2 * STEPS:
+        if 1 < s < 2 * STEPS:
             tests(b, t, 0)
         if more:
             nodes(o)
@@ -488,35 +514,37 @@ def rank_program(g, core, T, topo):
                 depth(1)
         else:
             weights(o)
-            add_up(o, u)
         if 1 < s < 2 * STEPS:
             rows(b, 1)
         if more:
             turn(o)
             rows(o, 0)
         if s < 2 * STEPS:
-            if s > 1:
-                sums(b, 2)
             tests(b, t, 1)
-            sums(b, 1)
+            for c in (0, 1) if t < STEPS - 1 else (1,):
+                if s > 1:
+                    sums(b, 2, c)
+                sums(b, 1, c)
         if more:
             weights(o)
-            add_up(o, u)
+            carry(o)
             spare(s)
         else:
             pieces(o)
 
-    order = FIRST + (0, 1, 2)
-    for i, d in enumerate(order):
-        win = (T.RO[:] if d == 0 else T.RW[:, (d - 1) * RWW:(d - 1) * RWW + 97]).indirect(T.GO[:, d * 16:d * 16 + 16])
-        rs, out = ["RV%d" % d, "RZ", "RO", "GO%d" % min(d, 1)], T.GD[:, d * 256:d * 256 + 256]
+    order = ((0, 0, 4), (3, 0, 4), (4, 0, 4), (5, 0, 4), (6, 0, 4), (7, 0, 4), (1, 0, 4), (2, 0, 2), (2, 2, 4))
+    for i, (d, x, y) in enumerate(order):
+        win = (T.RO[:] if d == 0 else T.RW[:, (d - 1) * RWW:(d - 1) * RWW + 97]).indirect(T.GO[:, d * 16 + 4 * x:d * 16 + 4 * y])
+        rs, out = ["RV%d" % d, "RZ", "RO", "GO%d" % min(d, 1)], T.GD[:, d * 256 + 64 * x:d * 256 + 64 * y]
         if i % 2 == 0:
-            vc(rs, ["GD%d" % d], out, win)
+            vc(rs, ["GD%d" % i], out, win)
         else:
-            act(rs, ["GD%d" % d], out, win, COPY)
-        mm(["GD%d" % d, "SY"], ["Q0"], T.Q0[0:8, 0:256], T.SY[:], out, i == 0, i == 7)
-    vc(["Q0"], ["Y"], T.Y[0:8, :], T.Q0[0:8, 0:256])
-    dmas("dY", ["Y"], ["y"], [("S", T.y[:, :], T.Y[0:8, :])])
+            act(rs, ["GD%d" % i], out, win, COPY)
+        for q in range(x, y):
+            mm(["GD%d" % i, "SY"], ["Q0"], T.Q0[0:32, 0:64], T.SY[:, 3 - q:35 - q], T.GD[:, d * 256 + 64 * q:d * 256 + 64 * q + 64],
+               i == 0 and q == 0, i == 8 and q == 3)
+    vc(["Q0"], ["Y"], T.Y[0:32, :], T.Q0[0:32, 0:64])
+    dmas("dY", ["Y"], ["y"], [("S", T.y[:, :], T.Y[0:32, :])])
     for sem in sorted(total):
         if max([seen.get((q, sem), 0) for q in queue]) < total[sem]:
             g.wait_ge(T.sem[sem], total[sem])

@@ -4,11 +4,10 @@ from concourse.mybir import AluOpType, ActivationFunctionType, AxisListType
 N = 8
 M = 2048
 STEPS = 7
-FIRST = (3, 4, 5, 6, 7)
-PAIRS = ((3, 4), (5, 6), (7, 1), (2,))
-BATCH = [(0, 480), (480, 448)]
-CUT, CUTA = 96, 320
-OWN = 480
+PAIRS = ((1, 2), (3, 4), (5, 6), (7,))
+BATCH = [(0, 256), (256, 240), (496, 240), (736, 192)]
+SENDS = {1: ((1, 2), (8, 8)), 2: ((3, 4, 5), (4, 4, 8)), 3: ((6, 7), (8, 8))}
+OWN = 0
 RWW = 112
 ALU = AluOpType
 FN = ActivationFunctionType
@@ -27,7 +26,7 @@ for _n, _w, _t in (
         + [(n, [1], "int32") for n in "IK RI GI R8 P8".split()]
         + [(n, [128], "float32") for n in "IR IDf SEL X0B RU".split()]
         + [(n, [128], "float16") for n in "IDh TRI ONE DG DN DS HB HI LO MK D2 MM0 MM1 MM2 MM3".split()]
-        + [(n, [8], "float32") for n in "G8 G8N G8E".split()] + [("G87", [32], "float32")]
+        + [(n, [8], "float32") for n in "G8 G8N G8E".split()] + [("G87", [16], "float32")]
         + [(n, [16], "float32") for n in "OH LB LS TB TS".split()]
         + [("IDb", [128], "bfloat16"), ("SY", [40], "bfloat16"), ("CM", [16], "bfloat16"), ("CZ", [16], "float32"),
            ("C1", [2, 56], "bfloat16"), ("C2", [2, 56], "bfloat16"), ("IV", [16, 9], "float32"), ("SN", [16], "float16"),
@@ -38,16 +37,14 @@ for _n, _w, _t in (
            ("PL", [928], "float32"), ("F0", [1024], "bfloat16"), ("ZL", [1040], "bfloat16"), ("LM", [14 * 128], "float16"),
            ("HM", [14, 64], "bfloat16"), ("IX", [48], "uint16"), ("GO", [128], "uint16"), ("CP", [672], "float32"),
            ("SA", [672], "bfloat16"), ("RW", [7 * RWW], "bfloat16"), ("RO", [272], "bfloat16"), ("GD", [2048], "bfloat16"),
-           ("Y", [64], "float32"), ("ZS", [512], "bfloat16"), ("Z", [2, 144], "float16")]):
+           ("Y", [64], "float32"), ("ZS", [2, 256], "bfloat16"), ("Z", [4, 144], "float16"),
+           ("D1", [928], "bfloat16"), ("DR", [928], "float16"), ("OF", [4, 16], "uint16"), ("D0", [8, 112], "float32"),
+           ("SP", [4, 112], "float32"), ("WS", [4, 112], "float32"), ("H", [12, 16], "float32"), ("O1", [8], "uint16")]):
     SCRATCH[_n] = ("sbuf", [128] + _w, _t)
-for _b in range(2):
-    for _n, _w, _t in (("D1_", [480], "bfloat16"), ("D2_", [480], "float16"), ("OF", [32], "uint16"), ("D0_", [2, 224], "float32"),
-                       ("SP", [56, 16], "float32"), ("WS", [224], "float32"), ("H", [3, 32], "float32")):
-        SCRATCH["%s%d" % (_n, _b)] = ("sbuf", [128] + _w, _t)
+for _b in range(4):
     SCRATCH["PS%d" % _b] = ("psum", [128, 2, 256], "float32")
-for _b in range(6):
     SCRATCH["Q%d" % _b] = ("psum", [128, 512], "float32")
-PSUM = ["PS0", "PS1"] + ["Q%d" % _b for _b in range(6)]
+PSUM = ["PS%d" % _b for _b in range(4)] + ["Q%d" % _b for _b in range(4)]
 
 DMASEMS = ["dN", "dP", "dB", "dC", "dX", "dL", "dW", "dU", "dV", "dY"]
 SEMAPHORES = (["cV", "cA", "cP", "cG", "box", "ls"] + DMASEMS
@@ -55,7 +52,7 @@ SEMAPHORES = (["cV", "cA", "cP", "cG", "box", "ls"] + DMASEMS
 
 
 def slot(d):
-    return 96 * (d - 3) if d in FIRST else (OWN if d == 0 else OWN + 160 + 96 * d)
+    return 160 + 96 * d
 
 
 def rank_program(g, core, T, topo):
@@ -187,14 +184,13 @@ def rank_program(g, core, T, topo):
                                  ("LB", 0, 1, 1, 1 - SH), ("LB", 9, 10, 1, 2 - SH), ("LB", 14, 15, 1, 1.0)):
         x = T[n][:, lo:hi:step]
         op("G", g.affine_select, ["LS", "LB"], [n + "1"], x, x, [[0, len(range(lo, hi, step))]], ALU.is_gt, c, 0, 0)
-    for b in "01":
-        whole("D0_" + b, T["D0_" + b][:], 448, 0)
-    for b in "01":
-        whole("SPz" + b, T["SP" + b][:, 6::7, :], 128, 0)
+    whole("D0", T.D0[:], 896, 0)
+    whole("ZS", T.ZS[:], 512, 0)
 
     fill("W1e", T.W1[:, M - 8:M + 8], FAR)
     fill("W2e", T.W2[:, M:M + 8], M)
     fill("OSe", T.OS[:, 128:130], M)
+    fill("O1", T.O1[:], 1)
     ts(["IK"], ["R8"], T.R8[:], T.IK[:], 7, None, ALU.bitwise_and)
     ts(["IK"], ["RI"], T.RI[:], T.IK[:], 15, None, ALU.bitwise_and)
     ts(["IK"], ["GI"], T.GI[:], T.IK[:], 4, None, ALU.logical_shift_right)
@@ -215,6 +211,7 @@ def rank_program(g, core, T, topo):
     ts(["RI"], ["XE"], T.XE[:], T.RI[:], 0.5, FAR, ALU.is_lt, ALU.mult)
     ts(["G8", "A0"], ["CM0"], T.CM[:, 0:8], T.G8[:], col("A0"), None, ALU.mult)
     vc(["RI"], ["RF"], T.RF[:], T.RI[:])
+    fill("ZL", T.ZL[:], 0.0)
     ts(["CC"], ["CLz"], T.CL[:, 0:256], T.CC[:, 0:256], 4095, None, ALU.bitwise_and)
     ts(["CC"], ["CLw"], T.CL[:, 256:384], T.CC[:, 256:384], 255, None, ALU.bitwise_and)
     ts(["W2e", "XE"], ["Xe"], T.X[:, M:M + 8], T.W2[:, M:M + 8], col("XE"), 1.0, ALU.add, ALU.add)
@@ -257,7 +254,7 @@ def rank_program(g, core, T, topo):
         for x in (("ZH", 5, 4096 * K, "T0"), ("ZL0", 2, 4096 * K, "T1"), ("V3", 14, -256 * UP16, "V2"),
                   ("U4", 14, 3 * K0 - C - 256 * UP16, "U0"), ("U2", 14, -6 * K6 - 512 * UP16, "U1"), ("ZL1", 14, 2 * K * K, "ZL0")):
             column(*x)
-        for j in range(4):
+        for j in (0, 1):
             act(["G8", "OH"], ["G87"], T.G87[:, 8 * j:8 * j + 8], T.G8[:], COPY, scale=row(7))
         act(["G8", "OH"], ["T3"], T.G8E[:], T.G8[:], COPY, scale=row(14))
         act(["U0", "U2"], ["U5"], col("U5"), col("U0"), IDENT, bias=col("U2"))
@@ -269,9 +266,6 @@ def rank_program(g, core, T, topo):
                           (7, "G8", "ZH"), (8, "G8", "ZL1"), (10, "G8", "V3"), (11, "G8N", "U4"), (12, "G8", "U5")):
             act([n, "OH" if c in range(16) else c], ["C2"], T.C2[:, t // 7, t % 7::7], T[n][:], COPY,
                 scale=row(c) if c in range(16) else col(c))
-        act(["BXa"], ["N0"], T.N0[:], T.BXi[:, 0:1], COPY)
-        act(["IDf"], ["IDh"], T.IDh[:], T.IDf[:], COPY)
-        act(["N0", "IR"], ["X0B"], T.X0B[:], T.IR[:], IDENT, scale=0.0, bias=col("N0"))
 
     tt(["BXa", "BXi"], ["BX"], T.BX[:], T.BXi[:, 0:8:2], T.BXi[:, 8:12], ALU.add)
     for e in (2, 0, 3, 1):
@@ -286,10 +280,9 @@ def rank_program(g, core, T, topo):
                    True, True)
     ts(["RF"], ["R128"], T.R128[:], T.RF[:], 128.0, None, ALU.mult)
     ts(["IK"], ["P8"], T.P8[:], T.IK[:], 3, None, ALU.logical_shift_right)
-    vc(["R8"], ["R8F"], T.R8F[:], T.R8[:])
     fill("RZ", T.RW[:, 96::RWW], 0.0)
-    ts(["IR", "R128"], ["NI"], T.NI[:], T.IR[:], col("R128"), None, ALU.add)
     ts(["Q1"], ["HB"], T.HB[:], T.Q1[:, 0:128], -5.0, None, ALU.is_lt)
+    ts(["IR", "R128"], ["NI"], T.NI[:], T.IR[:], col("R128"), None, ALU.add)
 
     dmas("dL", ["CLz", "CLw"], ["Xb"], [("S", T.X[r::16, 0:M], T.CL[:, 128 * i:128 * i + 128]) for i, r in enumerate((10, 13, 15))])
     X = ["Xa", "Xb", "Xe"]
@@ -311,9 +304,9 @@ def rank_program(g, core, T, topo):
 
     ranks("Q2", True)
     ranks("Q1", False)
-    fill("OF1", T.OF1[:], 1)
-    fill("Z", T.Z[:], 0.0)
+    vc(["R8"], ["R8F"], T.R8F[:], T.R8[:])
     vc(["P8"], ["P8F"], T.P8F[:], T.P8[:])
+    vc(["BXa"], ["N0"], T.N0[:], T.BXi[:, 0:1])
     ts(["Q2"], ["HI"], T.HI[:, 0:112], T.Q2[:, 0:112], 1 / 16, 6 + UP16 - 0.5 + 1 / 32, ALU.mult, ALU.add)
     mm(["HI", "DS"], ["Q1"], T.Q1[:, 0:112], T.DS[:], T.HI[:, 0:112], False, True)
     mm(["HB", "DN"], ["Q2"], T.Q2[:, 112:128], T.DN[:], T.HB[:, 112:128], True, True)
@@ -326,18 +319,21 @@ def rank_program(g, core, T, topo):
             ts(["Q1"], ["LO"], T.LO[:, 0:112], T.Q1[:, 0:112], 96 + 16 * UP16, None, ALU.add)
     for c in range(16):
         ts(["LO"], ["LM"], T.LM[:, c::16], T.LO[:, 0:112], float(c), None, ALU.is_equal)
-    BANK = ("Q3", "Q4", "Q5", "Q0")
+    BANK = ("PS2", "PS3", "Q3", "Q0")
+
+    def part(i, x, y):
+        return T[BANK[i]][x:y, 0, 0:128] if i < 2 else T[BANK[i]][x:y, 0:128]
 
     def product(i):
         for h, d in enumerate(PAIRS[i]):
             for b in (0, 1):
                 k = 7 * b + d - 1
-                mm(["HM", "HM0", "HM1", "LM"], [BANK[i]], T[BANK[i]][64 * h:64 * h + 64, 0:128], T.HM[:, k, :],
+                mm(["HM", "HM0", "HM1", "LM"], [BANK[i]], part(i, 64 * h, 64 * h + 64), T.HM[:, k, :],
                    T.LM[:, 128 * k:128 * k + 128], b == 0, b == 1)
 
     def own_scene(i):
         n, ps, m = 64 * len(PAIRS[i]), "PS%d" % (i % 2), "MM%d" % i
-        tt([BANK[i], "MK"], [m], T[m][0:n, :], T[BANK[i]][0:n, 0:128], T.MK[0:n, :], ALU.mult)
+        tt([BANK[i], "MK"], [m], T[m][0:n, :], part(i, 0, n), T.MK[0:n, :], ALU.mult)
         mm([m, "SN"], [ps], T[ps][:, :, 0:8], T[m][0:n, :], T.SN[0:n, :], True, True)
 
     def list_(i):
@@ -375,27 +371,215 @@ def rank_program(g, core, T, topo):
     list_(3)
     pick(2)
     pick(3)
-    whole("ZL", T.ZL[:], 1040, 0)
-    whole("ZS", T.ZS[:], 512, 0)
-    op("V", v.tensor_reduce, ["OH"], ["E012"], T.E012[:], T.OH[:, 0:3], AxisListType.X, ALU.add)
-    fill("SYz", T.SY[:], 0.0)
-    fill("RO", T.RO[:, 256:272], 0.0)
-    ts(["G8", "E012", "SYz"], ["SY"], T.SY[:, 3:35:4], T.G8[:], col("E012"), -1.0, ALU.mult, ALU.mult)
     vc(W1, ["N1"], T.N1[:], T.W1[:, 1:2])
+
+    def points(b):
+        lo, n = BATCH[b]
+        return ["PL%d" % d for d in range(8) if (d == 0 and b == 0) or (d and slot(d) < lo + n and slot(d) + 96 > lo)]
+
+    def copy(reads, writes, out, in_, n):
+        op("G", g.affine_select, reads, writes, out, in_, [[0, n]], ALU.is_ge, 0.0, 0, 0)
+
+    def depth(b):
+        lo, n = BATCH[b]
+        m, ps = n // 2, "Q%d" % (1 if b % 2 else 3)
+        for j in (0, 1):
+            mm(points(b) + ["CZ0", "CZ"], [ps], T[ps][0:m, 64 + 16 * j:80 + 16 * j], T.PL[:, lo + j:lo + n:2], T.CZ[:], True, True)
+        for c in (0, 1):
+            for i in (0, 1):
+                act([ps, "D0"], ["D0_%d_%d" % (b, c)], T.D0[0:m, 2 * b + c, 1 + i::7], T[ps][0:m, 64 + i:96:2], IDENT, scale=K,
+                    bias=(2 - i) * Z0 * K)
+
+    def rows(b):
+        lo, n = BATCH[b]
+        act(W2 + ["OF%d" % b, "BI", "SC"], ["D2_%d" % b], T.DR[:, lo:lo + n], T.W2[:, 0:M + 2].indirect(T.OF[:, b, 0:n // 16]),
+            IDENT, scale=col("SC"), bias=col("BI"))
+
+    def tests(b, t):
+        lo, n = BATCH[b]
+        out, pt = T.D1[:, lo:lo + n], T.PL[:, lo:lo + n]
+        if t == 0:
+            ts(["N1"] + points(b), ["D1_%d" % b], out, pt, col("N1"), None, ALU.is_lt)
+        else:
+            tt(W1 + points(b) + ["OF%d" % b], ["D1_%d" % b], out, T.W1[:, 0:M + 2].indirect(T.OF[:, b, 0:n // 16]), pt, ALU.is_gt)
+
+    def sums(b, i, t):
+        lo, n = BATCH[b]
+        ps = "PS%d" % b
+        for j in (0, 1):
+            d, x = ("D2", T.D2[:, 0:n // 2]) if (i, t) == (2, 0) else ("D%d_%d" % (i, b), (T.D1 if i == 1 else T.DR)[:, lo + j:lo + n:2])
+            mm([d, "C2" if i == 2 else "C1_12"], [ps], T[ps][0:n // 2, :, 56 * j:56 * j + 56], x, T["C%d" % i][:],
+               i == 2 and j == 0, i == 1 and j == 1)
+
+    def scan(b, c):
+        m, ps, out = BATCH[b][1] // 2, "PS%d" % b, ("SP", "WS")[c]
+        op("V", v.tensor_tensor_scan, [ps, "D0_%d_%d" % (b, c)] + ["D0_%d_s" % b] * c, ["%s%d" % (out, b)], T[out][0:m, b, :],
+           T.D0[0:m, 2 * b + c, :], T[ps][0:m, c, 0:112], 0.0, ALU.subtract, ALU.max)
+
+    def take(b):
+        m = BATCH[b][1] // 2
+        for j in (0, 1):
+            copy(["SP%d" % b, "Z"], ["Z%d" % b], T.Z[0:m, b, 14 + j:142:16], T.SP[0:m, b, 56 * j + 6:56 * j + 56:7], 8)
+
+    def turn(b):
+        m, ex = BATCH[b][1] // 2, "Q%d" % (b % 2)
+        for i in range(8):
+            mm(["Z%d" % b, "IDh"], [ex], T[ex][:, 0:m // 8], T.Z[0:m, b, 14 - 2 * i:142 - 2 * i], T.IDh[0:m, i:m:8], i == 0, i == 7)
+
+    def offsets(b):
+        k, ex = BATCH[b][1] // 16, "Q%d" % (b % 2)
+        act([ex], ["OF%d" % b], T.OF[:, b, 0:k], T[ex][:, 0:k], IDENT, scale=-1.0, bias=SH)
+
+    def carry(b):
+        m = BATCH[b][1] // 2
+        copy(["WS%d" % b], ["D0_%d_s" % b], T.D0[0:m, 2 * b + 1, 6::7], T.WS[0:m, b, 6::7], 16)
+
+    def round_(b):
+        m = BATCH[b][1] // 2
+        for i, e in enumerate((44, 37, 30)):
+            ts(["WS%d" % b], ["H%d" % i], T.H[0:m, 3 * b + i], T.WS[0:m, b, 6::7], 1.5 * 2.0 ** e, 1.5 * 2.0 ** e, ALU.add, ALU.subtract)
+
+    def pieces(b):
+        lo, n = BATCH[b]
+        m, ws, zs, ps = n // 2, "WS%d" % b, "ZS%d" % (b % 2), "Q%d" % (b % 2)
+        for i in (0, 1):
+            tt(["H%d" % i, "H%d" % (i + 1), "ZS"], [zs + "_%d" % i], T.ZS[0:m, b % 2, i::16], T.H[0:m, 3 * b + i + 1], T.H[0:m, 3 * b + i],
+               ALU.subtract)
+        tt([ws, "H2", "ZS"], [zs + "_2"], T.ZS[0:m, b % 2, 2::16], T.WS[0:m, b, 6::7], T.H[0:m, 3 * b + 2], ALU.subtract)
+        for j in (0, 1):
+            mm([zs + "_0", zs + "_1", zs + "_2", "IDb"], [ps], T[ps][:, j:n:2], T.ZS[0:m, b % 2, 128 * j:128 * j + 128], T.IDb[0:m, 0:m],
+               True, True)
+        if b == 0:
+            act([ps], ["RV0"], T.RO[:, 0:256], T[ps][:, 0:256], COPY)
+        else:
+            act([ps], ["SA%d" % b], T.SA[:, lo - 256:lo - 256 + n], T[ps][:, 0:n], COPY)
+            ds, lanes = SENDS[b]
+            remote([(-d, "rt%d" % d, T.SA[:, slot(d) - 256:slot(d) - 160], T.RW[:, (d - 1) * RWW:(d - 1) * RWW + 96], k)
+                    for d, k in zip(ds, lanes)], ["SA%d" % b])
+            for d in ds:
+                note((None, "rt%d" % d, total["rt%d" % d]), [], ["RV%d" % d])
+
+    def spare(k):
+        if k == 0:
+            fill("Z", T.Z[:], 0.0)
+            op("V", v.tensor_reduce, ["OH"], ["E012"], T.E012[:], T.OH[:, 0:3], AxisListType.X, ALU.add)
+            fill("SYz", T.SY[:], 0.0)
+        if k == 1:
+            fill("RO", T.RO[:, 256:272], 0.0)
+            ts(["G8", "E012", "SYz"], ["SY"], T.SY[:, 3:35:4], T.G8[:], col("E012"), -1.0, ALU.mult, ALU.mult)
+            act(["IDf"], ["IDb"], T.IDb[:], T.IDf[:], COPY)
+        if k in (6, 7):
+            b = k - 6
+            act(["Q2", "ZL"], ["ZL%d" % b], T.ZL[:, 142 + b:1030:16], T.Q2[:, 56 * b:56 * b + 56], IDENT, bias=96.0)
+        if k in (8, 9):
+            b = k - 8
+            act(["Q2", "ZL", "KF2", "KF3"], ["ZO%d" % b], T.ZL[:, 14 + b:128:16], T.Q2[:, 112 + 8 * b:120 + 8 * b], IDENT,
+                bias=col("KF3" if b else "KF2"))
+        if 10 <= k < 18:
+            d = k - 10
+            for i in range(8):
+                mm(["ZL0", "ZL1", "ZO0", "ZO1", "IDb"], ["Q3"], T.Q3[:, d * 16:d * 16 + 16],
+                   T.ZL[:, 128 * d + 14 - 2 * i:128 * d + 142 - 2 * i], T.IDb[:, i::8], i == 0, i == 7)
+        if k == 19:
+            act(["Q3"], ["GQ"], T.RU[:], T.Q3[:, 0:128], COPY)
+
+    depth(0)
+    act(["N0", "IR"], ["X0B"], T.X0B[:], T.IR[:], IDENT, scale=0.0, bias=col("N0"))
+    act(W2 + ["O1", "BI", "SC"], ["D2"], T.D2[:], T.W2[:, 0:M + 2].indirect(T.O1[:]), IDENT, scale=col("SC"), bias=col("BI"))
+    mm(["X0B", "G87"], ["Q0"], T.Q0[:, 0:16], T.X0B[:], T.G87[:], True, True)
+    for b in range(4):
+        act(["Q0", "D0"], ["D0_%d_s" % b], T.D0[:, 2 * b + 1, 6::7], T.Q0[:, 0:16], COPY, scale=-1.0)
+    act(["IDf"], ["IDh"], T.IDh[:], T.IDf[:], COPY)
+    tests(0, 0)
+    sums(0, 2, 0)
+    sums(0, 1, 0)
+    for b in (1, 2, 3):
+        sums(b, 2, 0)
+    spare(0)
+    scan(0, 0)
+    take(0)
+    scan(0, 1)
+    carry(0)
+    last = 4 * (STEPS - 1)
+    for k in range(1, 4 * STEPS):
+        b, y, z = k % 4, (k - 1) % 4, (k - 2) % 4
+        if k <= 2:
+            depth(k)
+        if k == 2:
+            turn(0)
+        if 2 <= k < last + 2:
+            offsets(z)
+            if k > 2:
+                rows(z)
+        tests(b, k // 4)
+        sums(b, 1, k // 4)
+        if k == 2:
+            depth(3)
+            rows(0)
+        if 2 <= k <= last:
+            scan(y, 0)
+            take(y)
+        if 4 <= k + 1 < 4 * STEPS:
+            sums((k + 1) % 4, 2, (k + 1) // 4)
+        if 2 <= k <= last:
+            turn(y)
+        if 2 <= k < last + 3:
+            scan(y, 1)
+        if 2 <= k <= last:
+            carry(y)
+        spare(k)
+    round_(1)
+    scan(2, 1)
+    pieces(1)
+    round_(2)
+    pieces(2)
+    scan(3, 1)
+    ts(["GQ"], ["GO1"], T.GO[:, 16:128], T.RU[:, 16:128], 96.0, None, ALU.min)
+    for b in (3, 0):
+        round_(b)
+        pieces(b)
+
+    ts(["GQ"], ["GO0"], T.GO[:, 0:16], T.RU[:, 0:16], 256.0, 256.0, ALU.add, ALU.min)
+    order = ((1, 0, 4), (2, 0, 4), (0, 0, 4), (3, 0, 4), (4, 0, 4), (5, 0, 4), (6, 0, 4), (7, 0, 2), (7, 2, 4))
+    for i, (d, x, y) in enumerate(order):
+        win = (T.RO[:] if d == 0 else T.RW[:, (d - 1) * RWW:(d - 1) * RWW + 97]).indirect(T.GO[:, d * 16 + 4 * x:d * 16 + 4 * y])
+        rs, out = ["RV%d" % d, "RZ", "RO", "GO%d" % min(d, 1)], T.GD[:, d * 256 + 64 * x:d * 256 + 64 * y]
+        if i % 2 == 0:
+            vc(rs, ["GD%d" % i], out, win)
+        else:
+            act(rs, ["GD%d" % i], out, win, COPY)
+        for q in range(x, y):
+            mm(["GD%d" % i, "SY"], ["Q2"], T.Q2[0:32, 0:64], T.SY[:, 3 - q:35 - q], T.GD[:, d * 256 + 64 * q:d * 256 + 64 * q + 64],
+               i == 0 and q == 0, i == 8 and q == 3)
+    vc(["Q2"], ["Y"], T.Y[0:32, :], T.Q2[0:32, 0:64])
+    dmas("dY", ["Y"], ["y"], [("S", T.y[:, :], T.Y[0:32, :])])
+    for sem in sorted(total):
+        if max([seen.get((q, sem), 0) for q in queue]) < total[sem]:
+            g.wait_ge(T.sem[sem], total[sem])
+    return
+    for j in range(4):
+        ts(["G8", "OH"], ["G87"], T.G87[:, 8 * j:8 * j + 8], T.G8[:], row(7), None, ALU.mult)
+    vc(W1, ["N1"], T.N1[:], T.W1[:, 1:2])
+    fill("SYz", T.SY[:], 0.0)
 
     def points(b):
         return ["PL%d" % d for d in (FIRST if b == 0 else (0, 1, 2))]
 
-    def depth(b):
+    def turn_z(b, part):
         lo, n = BATCH[b]
-        ps, d0, m = "Q%d" % b, "D0_%d" % b, n // 4
-        for (x, y) in ((0, 96), (96, m)):
-            for j in range(4):
-                mm(points(b)[:4 if x == 0 else 5] + ["CZ0", "CZ"], [ps], T[ps][x:y, 16 * j:16 * j + 16],
-                   T.PL[:, lo + 4 * x + j:lo + 4 * y:4], T.CZ[:], True, True)
-        for c in (0, 1):
-            for i in (0, 1):
-                act([ps, d0], [d0 + "_%d" % c], T[d0][0:m, c, 1 + i::7], T[ps][0:m, i:64:2], IDENT, scale=K, bias=(2 - i) * Z0 * K)
+        ps, cut = "Q%d" % b, (96, 64)[b]
+        x, y = (cut, n // 4) if part else (0, cut)
+        for j in range(4):
+            mm((points(b) if part else points(b)[:(4, 1)[b]]) + ["CZ0", "CZ"], [ps], T[ps][x:y, 16 * j:16 * j + 16],
+               T.PL[:, lo + 4 * x + j:lo + 4 * y:4], T.CZ[:], True, True)
+
+    def depth(b):
+        ps, d0, m = "Q%d" % b, "D0_%d" % b, BATCH[b][1] // 4
+        for i in (0, 1):
+            act([ps, d0], [d0 + "_0"], T[d0][0:m, 0, 1 + i::7], T[ps][0:m, i:64:2], IDENT, scale=K, bias=(2 - i) * Z0 * K)
+        for i in (0, 1):
+            x = T[d0][0:m, 0, 1 + i::7]
+            op("G", g.affine_select, [d0 + "_0"], [d0 + "_1"], T[d0][0:m, 1, 1 + i::7], x, [[0, 32]], ALU.is_ge, 0.0, 0, 0)
 
     def rows(b, part):
         n, of = BATCH[b][1], "OF%d" % b
@@ -426,13 +610,16 @@ def rank_program(g, core, T, topo):
 
     def nodes(b):
         m, ps, d0, sp = BATCH[b][1] // 4, "PS%d" % b, "D0_%d" % b, "SP%d" % b
-        for j in range(4):
-            op("V", v.tensor_tensor_scan, [ps, d0 + "_0", "SPz%d" % b], [sp], T[sp][0:m, :, j], T[d0][0:m, 0, 56 * j:56 * j + 56],
-               T[ps][0:m, 0, 56 * j:56 * j + 56], 0.0, ALU.subtract, ALU.max)
-        act([sp, "Z"], ["Z%d" % b], T.Z[0:m, b, 12:140], T[sp][0:m, 6::7, :], COPY, scale=-1.0)
+        for h in (0, 1):
+            op("V", v.tensor_tensor_scan, [ps, d0 + "_0", "SPz%d" % b], [sp], T[sp][0:m, :, h], T[d0][0:m, 0, 112 * h:112 * h + 112],
+               T[ps][0:m, 0, 112 * h:112 * h + 112], 0.0, ALU.subtract, ALU.max)
+        for j in (0, 1):
+            act([sp, "Z"], ["Z%d" % b], T.Z[0:m, b, 12 + j:140:2], T[sp][0:m, 56 * j + 6:56 * j + 56:7, :], COPY, scale=-1.0)
 
     def turn(b):
         m, ex = BATCH[b][1] // 4, "Q%d" % b
+        for i in range(2):
+            mm(["Z%d" % b, "IDh"], [ex], T[ex][:, 64:64 + m // 4], T.Z[0:m, b, 12 - 4 * i:140 - 4 * i], T.IDh[0:m, i:m:4], True, True)
         for i in range(4):
             mm(["Z%d" % b, "IDh"], [ex], T[ex][:, 0:m // 4], T.Z[0:m, b, 12 - 4 * i:140 - 4 * i], T.IDh[0:m, i:m:4], i == 0, i == 3)
         act([ex], ["OF%d" % b], T["OF%d" % b][:, 0:m // 4], T[ex][:, 0:m // 4], IDENT, bias=SH)
@@ -472,11 +659,16 @@ def rank_program(g, core, T, topo):
             act([ps], ["RV0"], T.RO[:, 0:256], T[ps][:, 0:256], COPY)
 
     def spare(s):
-        if s in (2, 3):
-            b = s - 2
-            act(["Q2", "ZL"], ["ZL%d" % b], T.ZL[:, 142 + b:1030:16], T.Q2[:, 56 * b:56 * b + 56], IDENT, bias=96.0)
+        if s == 1:
+            fill("RO", T.RO[:, 256:272], 0.0)
+            ts(["G8", "E012", "SYz"], ["SY"], T.SY[:, 3:35:4], T.G8[:], col("E012"), -1.0, ALU.mult, ALU.mult)
+        if s in (1, 2):
+            whole("ZL", T.ZL[:, 520 * (s - 1):520 * s], 520, 0)
+        if s == 3:
+            whole("ZS", T.ZS[:], 512, 0)
         if s in (4, 5):
             b = s - 4
+            act(["Q2", "ZL"], ["ZL%d" % b], T.ZL[:, 142 + b:1030:16], T.Q2[:, 56 * b:56 * b + 56], IDENT, bias=96.0)
             act(["Q2", "ZL", "KF2", "KF3"], ["ZO%d" % b], T.ZL[:, 14 + b:128:16], T.Q2[:, 112 + 8 * b:120 + 8 * b], IDENT,
                 bias=col("KF3" if b else "KF2"))
         if s in (6, 7, 8, 9):
@@ -485,22 +677,29 @@ def rank_program(g, core, T, topo):
                     mm(["ZL0", "ZL1", "ZO0", "ZO1", "IDb"], ["Q4"], T.Q4[:, d * 16:d * 16 + 16],
                        T.ZL[:, 128 * d + 14 - 2 * i:128 * d + 142 - 2 * i], T.IDb[:, i::8], i == 0, i == 7)
         if s == 10:
-            ts(["Q4"], ["GO0"], T.GO[:, 0:16], T.Q4[:, 0:16], 256.0, 256.0, ALU.add, ALU.min)
-        if s == 11:
-            ts(["Q4"], ["GO1"], T.GO[:, 16:128], T.Q4[:, 16:128], 96.0, None, ALU.min)
+            act(["Q4"], ["GQ"], T.RU[:], T.Q4[:, 0:128], COPY)
 
     act(W2 + ["OF1", "BI", "SC"], ["D2"], T.D2[:], T.W2[:, 0:M + 2].indirect(T.OF1[:, 0:8]), IDENT, scale=col("SC"), bias=col("BI"))
+    act(["N0", "IR"], ["X0B"], T.X0B[:], T.IR[:], IDENT, scale=0.0, bias=col("N0"))
+    act(["IDf"], ["IDh"], T.IDh[:], T.IDf[:], COPY)
+    act(["IDf"], ["IDb"], T.IDb[:], T.IDf[:], COPY)
+    turn_z(1, 0)
+    for b in (0, 1):
+        for c in (0, 1):
+            sums(b, 2, c, True)
     mm(["X0B", "G87"], ["Q4"], T.Q4[:, 0:32], T.X0B[:], T.G87[:], True, True)
     for b in (0, 1):
         act(["Q4", "D0_%d" % b], ["D0_%d_s" % b], T["D0_%d" % b][:, 1, 6::7], T.Q4[:, 0:32], COPY, scale=-1.0)
-        for c in (0, 1):
-            sums(b, 2, c, True)
-    act(["IDf"], ["IDb"], T.IDb[:], T.IDf[:], COPY)
+    turn_z(0, 0)
+    turn_z(0, 1)
     depth(0)
     tests(1, 0, 0)
     tests(0, 0, 0)
     tests(0, 0, 1)
+    fill("Z", T.Z[:], 0.0)
+    op("V", v.tensor_reduce, ["OH"], ["E012"], T.E012[:], T.OH[:, 0:3], AxisListType.X, ALU.add)
     sums(0, 1, 0)
+    turn_z(1, 1)
     sums(0, 1, 1)
     for s in range(1, 2 * STEPS + 1):
         b, t = s % 2, s // 2
@@ -532,6 +731,8 @@ def rank_program(g, core, T, topo):
         else:
             pieces(o)
 
+    ts(["GQ"], ["GO0"], T.GO[:, 0:16], T.RU[:, 0:16], 256.0, 256.0, ALU.add, ALU.min)
+    ts(["GQ"], ["GO1"], T.GO[:, 16:128], T.RU[:, 16:128], 96.0, None, ALU.min)
     order = ((0, 0, 4), (3, 0, 4), (4, 0, 4), (5, 0, 4), (6, 0, 4), (7, 0, 4), (1, 0, 4), (2, 0, 2), (2, 2, 4))
     for i, (d, x, y) in enumerate(order):
         win = (T.RO[:] if d == 0 else T.RW[:, (d - 1) * RWW:(d - 1) * RWW + 97]).indirect(T.GO[:, d * 16 + 4 * x:d * 16 + 4 * y])

from concourse.bass import DstId, RemoteDMATransfer
from concourse.mybir import AluOpType, ActivationFunctionType, AxisListType

N = 8
M = 2048
STEPS = 7
PAIRS = ((1, 2), (3, 4), (5, 6), (7,))
BATCH = [(0, 256), (256, 240), (496, 240), (736, 192)]
SENDS = {1: ((1, 2), (8, 8)), 2: ((3, 4, 5), (4, 4, 8)), 3: ((6, 7), (8, 8))}
OWN = 0
RWW = 112
ALU = AluOpType
FN = ActivationFunctionType
COPY, IDENT = FN.Copy, FN.Identity
K, KP, SH = 2.0 ** 22, 4096.0, 1024.0
C, K0, K6 = 2.0 ** 21, 5.0 * 2 ** 20, 9.0 * 2 ** 18
FAR = 2.0 ** 22
UP16 = 1536.0
Z0 = 4096 * UP16 - 2048
COLUMNS = "ZH ZL0 ZL1 V2 V3 U0 U1 U2 U4 U5 P5 P6 T0 T1 E25".split()

SCRATCH = {}
for _n, _w, _t in (
        [(n, [1], "float32") for n in "NK RF GF LO3 MID UP SB A0 A1 A2 NM S2 PB KF2 KF3 R128 BI SC XE E012 N0 N1 R8F P8F".split()]
        + [("CO", [len(COLUMNS)], "float32")]
        + [(n, [1], "int32") for n in "IK RI GI R8 P8".split()]
        + [(n, [128], "float32") for n in "IR IDf SEL X0B RU".split()]
        + [(n, [128], "float16") for n in "IDh TRI ONE DG DN DS HB HI LO MK D2 MM0 MM1 MM2 MM3".split()]
        + [(n, [8], "float32") for n in "G8 G8N G8E".split()] + [("G87", [16], "float32")]
        + [(n, [16], "float32") for n in "OH LB LS TB TS".split()]
        + [("IDb", [128], "bfloat16"), ("SY", [40], "bfloat16"), ("CM", [16], "bfloat16"), ("CZ", [16], "float32"),
           ("C1", [2, 56], "bfloat16"), ("C2", [2, 56], "bfloat16"), ("IV", [16, 9], "float32"), ("SN", [16], "float16"),
           ("BXi", [16], "int32"), ("NB", [4], "int32"), ("BX", [4], "float32"), ("Pi", [256], "int32"), ("Pf", [256], "float32"),
           ("B0", [2, 4, 16], "int32"), ("OT", [128], "int32"), ("OS", [130], "uint16"), ("NI", [128], "int32"),
           ("CC", [384], "int32"), ("CL", [384], "int32"), ("G16", [8, 16], "float32"),
           ("X", [M + 8], "int32"), ("G", [M + 16], "int32"), ("W1", [M + 8], "int32"), ("W2", [M + 8], "int32"),
           ("PL", [928], "float32"), ("F0", [1024], "bfloat16"), ("ZL", [1040], "bfloat16"), ("LM", [14 * 128], "float16"),
           ("HM", [14, 64], "bfloat16"), ("IX", [48], "uint16"), ("GO", [128], "uint16"), ("CP", [672], "float32"),
           ("SA", [672], "bfloat16"), ("RW", [7 * RWW], "bfloat16"), ("RO", [272], "bfloat16"), ("GD", [2048], "bfloat16"),
           ("Y", [64], "float32"), ("ZS", [2, 256], "bfloat16"), ("Z", [4, 144], "float16"),
           ("D1", [928], "bfloat16"), ("DR", [928], "float16"), ("OF", [4, 16], "uint16"), ("D0", [8, 112], "float32"),
           ("SP", [4, 112], "float32"), ("WS", [4, 112], "float32"), ("H", [12, 16], "float32"), ("O1", [8], "uint16")]):
    SCRATCH[_n] = ("sbuf", [128] + _w, _t)
for _b in range(4):
    SCRATCH["PS%d" % _b] = ("psum", [128, 2, 256], "float32")
    SCRATCH["Q%d" % _b] = ("psum", [128, 512], "float32")
PSUM = ["PS%d" % _b for _b in range(4)] + ["Q%d" % _b for _b in range(4)]

DMASEMS = ["dN", "dP", "dB", "dC", "dX", "dL", "dW", "dU", "dV", "dY"]
SEMAPHORES = (["cV", "cA", "cP", "cG", "box", "ls"] + DMASEMS
              + ["pt%d" % d for d in range(1, 8)] + ["rt%d" % d for d in range(1, 8)])


def slot(d):
    return 160 + 96 * d


def rank_program(g, core, T, topo):
    rank = T.rank_of(core)
    if rank is None:
        return
    cores = T.cores
    queue = {"V": g.vector, "A": g.scalar, "P": g.tensor, "G": g, "S": g.sync}
    total = {"ls": 0}
    seen = {}
    wr, rd = {}, {}

    def await_(q, handles):
        need = {}
        for (_, sem, val) in handles:
            if sem in DMASEMS:
                val = total[sem]
            need[sem] = max(need.get(sem, 0), val)
        for sem in sorted(need):
            if seen.get((q, sem), 0) < need[sem]:
                queue[q].wait_ge(T.sem[sem], need[sem])
                seen[(q, sem)] = need[sem]

    def deps(q, reads, writes):
        hs = []
        for t in reads:
            hs += wr[t]
            if t in PSUM:
                hs += [h for h in rd.get(t, []) if h[0] != q]
        for t in writes:
            hs += [h for h in wr.get(t, []) + rd.get(t, []) if h[0] != q]
        await_(q, hs)

    def note(h, reads, writes):
        for t in reads:
            rd.setdefault(t, []).append(h)
        for t in writes:
            wr[t] = [h]
            rd[t] = []

    def op(q, method, reads, writes, *args, **kw):
        deps(q, reads, writes)
        sem = "c" + q
        total[sem] = total.get(sem, 0) + 1
        method(*args, **kw).then_inc(T.sem[sem], 1)
        note((q, sem, total[sem]), reads, writes)

    def dmas(sem, reads, writes, moves):
        for q in sorted(set(m[0] for m in moves)):
            deps(q, reads, writes)
        for (q, out, in_) in moves:
            total[sem] = total.get(sem, 0) + 16
            queue[q].dma_start(out, in_).then_inc(T.sem[sem], 16)
        note((None, sem, total[sem]), reads, writes)

    v, a, p = g.vector, g.scalar, g.tensor

    def ts(reads, writes, out, in0, s1, s2, *ops):
        op("V", v.tensor_scalar, reads, writes, out, in0, s1, s2, *ops)

    def tt(reads, writes, out, in0, in1, o):
        op("V", v.tensor_tensor, reads, writes, out, in0, in1, o)

    def vc(reads, writes, out, in_):
        op("V", v.tensor_copy, reads, writes, out, in_)

    def fill(tag, ap, c, after=()):
        op("V", v.memset, list(after), [tag], ap, c)

    def mm(reads, writes, out, lhsT, rhs, start, stop):
        op("P", p.matmul, reads, writes, out, lhsT, rhs, start, stop)

    def act(reads, writes, out, in_, func, **kw):
        op("A", a.activation, reads, writes, out, in_, func, **kw)

    def col(n):
        return T.CO[:, COLUMNS.index(n):COLUMNS.index(n) + 1] if n in COLUMNS else T[n][:, 0:1]

    def row(r):
        return T.OH[:, r:r + 1]

    def remote(moves, tags):
        deps("G", tags, [])
        trs, at = [], 0
        for (d, sem, src, dst, lanes) in moves:
            other = cores[(rank + d) % N]
            es = topo.engines(core, other)[at:at + lanes]
            at += lanes
            trs.append(RemoteDMATransfer(dst_ids=[DstId(rid=topo.addr(other)[0], pnc=topo.addr(other)[1])], remote_sem=T.sem[sem],
                                         dma_engine_mask=sum(1 << e for e in es), srcs=[src], dsts=[dst]))
            total["ls"] += len(es)
            total[sem] = len(es)
        g.remote_dma_fused(trs, local_sem=T.sem.ls)

    dmas("dN", [], ["BXa", "NB"], [("S", T.BXi[:, 0:2], T.nodes[:, 0:2]), ("A", T.NB[8:128, 0:2], T.nodes[0:120, 0:2]),
                                   ("A", T.NB[0:8, 0:2], T.nodes[8:16, 0:2])])
    dmas("dP", [], ["Pi"], [("S", T.Pi[0:24, :], T.pts[:, :])])
    dmas("dC", [], ["CC"], [("A", T.CC[:, 128 * i:128 * i + 128], T.nodes[r::16, :]) for i, r in enumerate((2, 5, 7))])
    dmas("dB", [], ["B0"], [("S", T.B0[:, i], T.nodes[6 + 16 * i::32, :]) for i in (0, 1)])
    op("G", g.iota, [], ["IK"], T.IK[:], [[1, 1]], 0, 1)
    op("G", g.iota, [], ["IR"], T.IR[:], [[1, 128]], 0, 0, allow_small_or_imprecise_dtypes=True)
    op("G", g.iota, [], ["IV"], T.IV[0:32], [[3, 8], [0, 6], [1, 3]], 0, -1, allow_small_or_imprecise_dtypes=True)
    deps("G", ["BXa", "NB"], [])
    trs = []
    for (src, ds, at) in ((T.BXi[:, 0:1], (2, 4, 6), 0), (T.NB[:, 0:1], (1, 3, 5, 7), 8)):
        others = [cores[(rank - d) % N] for d in ds]
        es = topo.engines(core, others[0])[at:at + 8]
        trs.append(RemoteDMATransfer(
            dst_ids=[DstId(rid=topo.addr(c)[0], pnc=topo.addr(c)[1]) for c in others], dma_engine_mask=sum(1 << e for e in es),
            remote_sem=T.sem.box, srcs=[src],
            dsts=[T.BXi[:, (d if at == 0 else at + d // 2):(d if at == 0 else at + d // 2) + 1] for d in ds]))
        total["ls"] += len(es)
        total["box"] = total.get("box", 0) + len(ds) * len(es)
    g.remote_dma_fused(trs, local_sem=T.sem.ls)
    note((None, "box", total["box"]), [], ["BXi"])
    dmas("dX", [], ["Xa"], [("S", T.X[r::8, 0:M], T.nodes[r::8, :]) for r in (3, 4, 6)]
         + [("S", T.X[r::16, 0:M], T.nodes[x::16, :]) for (r, x) in ((0, 0), (1, 1), (2, 2), (5, 5), (7, 7), (8, 3), (9, 4))])

    def whole(tag, out, n, c):
        op("G", g.iota, [], [tag], out, [[0, n]], c, 0, allow_small_or_imprecise_dtypes=True)

    whole("HM", T.HM[:, :, 48:64], 224, 0)
    op("G", g.iota, [], ["G16"], T.G16[:], [[1, 8], [0, 16]], 0, 0, allow_small_or_imprecise_dtypes=True)
    whole("LS", T.LS[:], 16, 1)
    whole("LB", T.LB[:], 16, 0)
    for (n, lo, hi, step, c) in (("LS", 2, 6, 3, 2.0 ** -12), ("LS", 3, 5, 1, 2.0 ** -8), ("LS", 7, 8, 1, 2.0 ** -8), ("LS", 14, 15, 1, 0.0),
                                 ("LB", 2, 6, 3, UP16 - 0.5 + 2.0 ** -13), ("LB", 3, 5, 1, UP16 - 0.5 + 2.0 ** -9),
                                 ("LB", 7, 8, 1, UP16 - 0.5 + 2.0 ** -9), ("LB", 10, 14, 3, -2048.0), ("LB", 1, 7, 5, -SH),
                                 ("LB", 0, 1, 1, 1 - SH), ("LB", 9, 10, 1, 2 - SH), ("LB", 14, 15, 1, 1.0)):
        x = T[n][:, lo:hi:step]
        op("G", g.affine_select, ["LS", "LB"], [n + "1"], x, x, [[0, len(range(lo, hi, step))]], ALU.is_gt, c, 0, 0)
    whole("D0", T.D0[:], 896, 0)
    whole("ZS", T.ZS[:], 512, 0)

    fill("W1e", T.W1[:, M - 8:M + 8], FAR)
    fill("W2e", T.W2[:, M:M + 8], M)
    fill("OSe", T.OS[:, 128:130], M)
    fill("O1", T.O1[:], 1)
    ts(["IK"], ["R8"], T.R8[:], T.IK[:], 7, None, ALU.bitwise_and)
    ts(["IK"], ["RI"], T.RI[:], T.IK[:], 15, None, ALU.bitwise_and)
    ts(["IK"], ["GI"], T.GI[:], T.IK[:], 4, None, ALU.logical_shift_right)
    ts(["R8"], ["LO3"], T.LO3[:], T.R8[:], 2.5, 2.0, ALU.is_lt, ALU.mult)
    ts(["R8"], ["MID"], T.MID[:], T.R8[:], 5.5, None, ALU.is_lt)
    ts(["RI"], ["UP"], T.UP[:], T.RI[:], 7.5, None, ALU.is_gt)
    ts(["R8"], ["NM"], T.NM[:], T.R8[:], 5.5, None, ALU.is_gt)
    vc(["GI"], ["GF"], T.GF[:], T.GI[:])
    tt(["LO3", "MID"], ["SB"], T.SB[:], T.LO3[:], T.MID[:], ALU.subtract)
    ts(["UP"], ["S2"], T.S2[:], T.UP[:], -2.0, 1.0, ALU.mult, ALU.add)
    ts(["IR", "GF"], ["G8"], T.G8[:], T.IR[:, 0:8], col("GF"), None, ALU.is_equal)
    tt(["SB", "UP"], ["A1"], T.A1[:], T.SB[:], T.UP[:], ALU.mult)
    tt(["NM", "S2"], ["A2"], T.A2[:], T.NM[:], T.S2[:], ALU.mult)
    ts(["IV"], ["SEL"], T.SEL[0:24, :], T.IV[0:24, :, 0:8], 0.0, None, ALU.is_equal)
    tt(["SB", "A1"], ["A0"], T.A0[:], T.SB[:], T.A1[:], ALU.subtract)
    ts(["SB", "A2"], ["PB"], T.PB[:], T.SB[:], col("A2"), 0.5, ALU.add, ALU.mult)
    ts(["G8", "A1"], ["CM1"], T.CM[:, 8:16], T.G8[:], col("A1"), None, ALU.mult)
    ts(["RI"], ["XE"], T.XE[:], T.RI[:], 0.5, FAR, ALU.is_lt, ALU.mult)
    ts(["G8", "A0"], ["CM0"], T.CM[:, 0:8], T.G8[:], col("A0"), None, ALU.mult)
    vc(["RI"], ["RF"], T.RF[:], T.RI[:])
    fill("ZL", T.ZL[:], 0.0)
    ts(["CC"], ["CLz"], T.CL[:, 0:256], T.CC[:, 0:256], 4095, None, ALU.bitwise_and)
    ts(["CC"], ["CLw"], T.CL[:, 256:384], T.CC[:, 256:384], 255, None, ALU.bitwise_and)
    ts(["W2e", "XE"], ["Xe"], T.X[:, M:M + 8], T.W2[:, M:M + 8], col("XE"), 1.0, ALU.add, ALU.add)
    ts(["IR", "RF"], ["OH"], T.OH[:], T.IR[:, 0:16], col("RF"), None, ALU.is_equal)
    for i in range(4):
        op("V", v.transpose, ["B0"], ["OT%d" % i], T.OT[:, i::4], T.B0[:, :, i, :])
    fill("C1", T.C1[:], 0.0)
    vc(["OT%d" % i for i in range(4)], ["OS"], T.OS[:, 0:128], T.OT[:])
    for (t, n, c) in ((1, "A2", K * K), (4, "A0", -KP), (5, "A0", -KP), (6, "SB", -KP), (8, "A2", K * K), (11, "A0", -K0),
                      (12, "SB", -K6)):
        ts(["G8", n, "C1"], ["C1_%d" % t], T.C1[:, t // 7, t % 7::7], T.G8[:], col(n), c, ALU.mult, ALU.mult)
    act(["IK"], ["NK"], T.NK[:], T.IK[:], COPY, scale=-1.0)
    act(["Pi"], ["Pf"], T.Pf[0:24, :], T.Pi[0:24, :], COPY)
    mm(["SEL", "Pf"], ["Q0"], T.Q0[:, 0:256], T.SEL[0:24, :], T.Pf[0:24, :], True, True)
    act(["IR", "NK"], ["X0B"], T.X0B[:], T.IR[:], FN.Abs, bias=col("NK"))
    act(["IR", "NK"], ["RU"], T.RU[:], T.IR[:], FN.Relu, bias=col("NK"))
    act(["IK"], ["KF2"], T.KF2[:], T.IK[:], COPY, scale=2.0)
    act(["X0B"], ["IDf"], T.IDf[:], T.X0B[:], FN.Relu, scale=-1.0, bias=1.0)
    act(["Q0", "PB"], ["PL0"], T.PL[:, OWN:OWN + 256], T.Q0[:, 0:256], IDENT, bias=col("PB"))
    act(["RU"], ["TRI"], T.TRI[:], T.RU[:], FN.Sign)
    act(["IK"], ["KF3"], T.KF3[:], T.IK[:], IDENT, scale=2.0, bias=1.0)
    act(["IR"], ["ONE"], T.ONE[:], T.IR[:], IDENT, scale=0.0, bias=1.0)
    for (n, s) in (("DG", -96.0), ("DS", -16.0), ("DN", -256.0)):
        act(["IDf"], [n], T[n][:], T.IDf[:], COPY, scale=s)

    def column(n, r, c, plus=None):
        if plus is None:
            act(["OH"], [n], col(n), row(r), COPY, scale=c)
        elif plus in range(16):
            act(["OH"], [n], col(n), row(r), IDENT, scale=c, bias=row(plus))
        else:
            act(["OH", plus], [n], col(n), row(r), IDENT, scale=c, bias=col(plus))

    for x in (("T0", 13, K), ("T1", 10, K), ("V2", 7, 256.0, 15), ("U0", 3, 256.0, 11), ("U1", 4, 256.0, 12),
              ("P5", 14, -3 * KP, 1), ("P6", 14, 6 * KP, 9), ("E25", 2, 1.0, 5)):
        column(*x)

    def coefficients():
        act(["G8"], ["G8N"], T.G8N[:], T.G8[:], COPY, scale=-1.0)
        for x in (("ZH", 5, 4096 * K, "T0"), ("ZL0", 2, 4096 * K, "T1"), ("V3", 14, -256 * UP16, "V2"),
                  ("U4", 14, 3 * K0 - C - 256 * UP16, "U0"), ("U2", 14, -6 * K6 - 512 * UP16, "U1"), ("ZL1", 14, 2 * K * K, "ZL0")):
            column(*x)
        for j in (0, 1):
            act(["G8", "OH"], ["G87"], T.G87[:, 8 * j:8 * j + 8], T.G8[:], COPY, scale=row(7))
        act(["G8", "OH"], ["T3"], T.G8E[:], T.G8[:], COPY, scale=row(14))
        act(["U0", "U2"], ["U5"], col("U5"), col("U0"), IDENT, bias=col("U2"))
        act(["G8", "E25"], ["CZ0"], T.CZ[:, 0::2], T.G8[:], COPY, scale=col("E25"))
        act(["G8", "OH"], ["CZ"], T.CZ[:, 1::2], T.G8[:], COPY, scale=row(2))
        for (t, c) in ((4, -2.5 * KP), (9, -C), (13, -2.0 ** 60)):
            act(["T3"], ["C2_%d" % t], T.C2[:, t // 7, t % 7::7], T.G8E[:], COPY, scale=c)
        for (t, n, c) in ((2, "G8N", 6), (3, "G8", 0), (0, "G8", "ZH"), (1, "G8", "ZL1"), (5, "G8", "P5"), (6, "G8N", "P6"),
                          (7, "G8", "ZH"), (8, "G8", "ZL1"), (10, "G8", "V3"), (11, "G8N", "U4"), (12, "G8", "U5")):
            act([n, "OH" if c in range(16) else c], ["C2"], T.C2[:, t // 7, t % 7::7], T[n][:], COPY,
                scale=row(c) if c in range(16) else col(c))

    tt(["BXa", "BXi"], ["BX"], T.BX[:], T.BXi[:, 0:8:2], T.BXi[:, 8:12], ALU.add)
    for e in (2, 0, 3, 1):
        out, pts = T.F0[:, e * 256:e * 256 + 256], T.PL[:, OWN:OWN + 256]
        if e < 2:
            act(["PL0", "BX"], ["F0_%d" % e], out, pts, FN.Sign, scale=-1.0, bias=T.BX[:, e:e + 1])
        else:
            ts(["PL0", "BX"], ["F0_%d" % e], out, pts, T.BX[:, e:e + 1], 2.0, ALU.is_lt, ALU.mult)
        for b in (0, 1):
            for (at, x, y) in (((112 + 8 * b, 0, 8), (56 * b, 8, 16)) if e == 0 else ((56 * b + 16 * e - 8, 0, 16),)):
                mm(["F0_%d" % e, "CM0", "CM1"], ["Q1"], T.Q1[:, at:at + y - x], T.F0[:, e * 256 + b:e * 256 + 256:2], T.CM[:, x:y],
                   True, True)
    ts(["RF"], ["R128"], T.R128[:], T.RF[:], 128.0, None, ALU.mult)
    ts(["IK"], ["P8"], T.P8[:], T.IK[:], 3, None, ALU.logical_shift_right)
    fill("RZ", T.RW[:, 96::RWW], 0.0)
    ts(["Q1"], ["HB"], T.HB[:], T.Q1[:, 0:128], -5.0, None, ALU.is_lt)
    ts(["IR", "R128"], ["NI"], T.NI[:], T.IR[:], col("R128"), None, ALU.add)

    dmas("dL", ["CLz", "CLw"], ["Xb"], [("S", T.X[r::16, 0:M], T.CL[:, 128 * i:128 * i + 128]) for i, r in enumerate((10, 13, 15))])
    X = ["Xa", "Xb", "Xe"]
    act(X + ["OS", "OSe"], ["G"], T.G[:], T.X[:].indirect(T.OS[:, 0:129]), COPY)
    coefficients()
    dmas("dW", ["W1e", "BXi"], ["W1a"], [("S", T.W1[r + 8 * i::16, 0:M - i], T.nodes[r::16, i:M]) for i in (0, 1) for r in range(6)])
    dmas("dU", X + ["NI"], ["W2a"],
         [("S", T.W2[0::8, 0:M], T.X[6::8, 0:M]), ("S", T.W2[3::8, 0:M], T.X[7::8, 0:M]), ("S", T.W2[4::8, 0:M], T.X[7::8, 1:M + 1]),
          ("S", T.W2[1::16, 0:M], T.X[6::16, 1:M + 1]), ("S", T.W2[9::16, 0:M], T.NI[:])])
    dmas("dV", ["G", "W1e", "W2e", "Xe"], ["W1b", "W2b"],
         [("S", T.W1[6 + i::8, 0:M + 2], T.G[i::8, 0:M + 2]) for i in (0, 1)]
         + [("S", T.W2[r::8, 0:M + 2], T.G[r::8, 0:M + 2]) for r in (2, 5, 6, 7)])
    W1, W2 = ["W1a", "W1b"], ["W2a", "W2b"]

    def ranks(ps, last):
        mm(["HB", "TRI"], [ps], T[ps][:, 0:112], T.TRI[:], T.HB[:, 0:112], True, False)
        mm(["HB", "ONE"], [ps], T[ps][:, 56:112], T.ONE[:], T.HB[:, 0:56], False, False)
        mm(["HB", "DG"], [ps], T[ps][:, 0:112], T.DG[:], T.HB[:, 0:112], False, last)

    ranks("Q2", True)
    ranks("Q1", False)
    vc(["R8"], ["R8F"], T.R8F[:], T.R8[:])
    vc(["P8"], ["P8F"], T.P8F[:], T.P8[:])
    vc(["BXa"], ["N0"], T.N0[:], T.BXi[:, 0:1])
    ts(["Q2"], ["HI"], T.HI[:, 0:112], T.Q2[:, 0:112], 1 / 16, 6 + UP16 - 0.5 + 1 / 32, ALU.mult, ALU.add)
    mm(["HI", "DS"], ["Q1"], T.Q1[:, 0:112], T.DS[:], T.HI[:, 0:112], False, True)
    mm(["HB", "DN"], ["Q2"], T.Q2[:, 112:128], T.DN[:], T.HB[:, 112:128], True, True)
    ts(["IR", "P8F"], ["SN"], T.SN[:], T.IR[:, 0:16], col("P8F"), None, ALU.is_equal)
    for n in range(6):
        for b in (0, 1):
            ts(["HI", "KF2", "KF3"], ["HM%d" % b], T.HM[:, 7 * b:7 * b + 7, 8 * n:8 * n + 8], T.HI[:, 56 * b:56 * b + 56], UP16 + n,
               col("KF3" if b else "KF2"), ALU.is_equal, ALU.mult)
        if n == 1:
            ts(["Q1"], ["LO"], T.LO[:, 0:112], T.Q1[:, 0:112], 96 + 16 * UP16, None, ALU.add)
    for c in range(16):
        ts(["LO"], ["LM"], T.LM[:, c::16], T.LO[:, 0:112], float(c), None, ALU.is_equal)
    BANK = ("PS2", "PS3", "Q3", "Q0")

    def part(i, x, y):
        return T[BANK[i]][x:y, 0, 0:128] if i < 2 else T[BANK[i]][x:y, 0:128]

    def product(i):
        for h, d in enumerate(PAIRS[i]):
            for b in (0, 1):
                k = 7 * b + d - 1
                mm(["HM", "HM0", "HM1", "LM"], [BANK[i]], part(i, 64 * h, 64 * h + 64), T.HM[:, k, :],
                   T.LM[:, 128 * k:128 * k + 128], b == 0, b == 1)

    def own_scene(i):
        n, ps, m = 64 * len(PAIRS[i]), "PS%d" % (i % 2), "MM%d" % i
        tt([BANK[i], "MK"], [m], T[m][0:n, :], part(i, 0, n), T.MK[0:n, :], ALU.mult)
        mm([m, "SN"], [ps], T[ps][:, :, 0:8], T[m][0:n, :], T.SN[0:n, :], True, True)

    def list_(i):
        ps = "PS%d" % (i % 2)
        vc([ps], ["IX%d" % i], T.IX[:, 12 * i:12 * i + 12], T[ps][:, :, 0:6])

    def pick(i):
        ds = PAIRS[i]
        n = 96 * len(ds)
        vc(["PL0", "IX%d" % i], ["CP%d" % i], T.CP[:, 192 * i:192 * i + n],
           T.PL[:, OWN:OWN + 256].indirect(T.IX[:, 12 * i:12 * i + n // 16]))
        remote([(d, "pt%d" % d, T.CP[:, 192 * i + 96 * h:192 * i + 96 * h + 96], T.PL[:, slot(d):slot(d) + 96], 16 // len(ds))
                for h, d in enumerate(ds)], ["CP%d" % i, "RZ"])
        for d in ds:
            note((None, "pt%d" % d, total["pt%d" % d]), [], ["PL%d" % d])

    product(0)
    product(1)
    ts(["G16", "R8F"], ["MK"], T.MK[:], T.G16[:], col("R8F"), None, ALU.is_equal)
    tt(["OH", "LS1"], ["TS"], T.TS[:], T.OH[:], T.LS[:], ALU.mult)
    tt(["OH", "LB1"], ["TB"], T.TB[:], T.OH[:], T.LB[:], ALU.mult)
    op("V", v.tensor_reduce, ["TS"], ["SC"], T.SC[:], T.TS[:], AxisListType.X, ALU.add)
    own_scene(0)
    product(2)
    op("V", v.tensor_reduce, ["TB"], ["BI"], T.BI[:], T.TB[:], AxisListType.X, ALU.add)
    own_scene(1)
    product(3)
    list_(0)
    own_scene(2)
    list_(1)
    pick(0)
    own_scene(3)
    list_(2)
    pick(1)
    list_(3)
    pick(2)
    pick(3)
    vc(W1, ["N1"], T.N1[:], T.W1[:, 1:2])

    def points(b):
        lo, n = BATCH[b]
        return ["PL%d" % d for d in range(8) if (d == 0 and b == 0) or (d and slot(d) < lo + n and slot(d) + 96 > lo)]

    def copy(reads, writes, out, in_, n):
        op("G", g.affine_select, reads, writes, out, in_, [[0, n]], ALU.is_ge, 0.0, 0, 0)

    def depth(b):
        lo, n = BATCH[b]
        m, ps = n // 2, "Q%d" % (1 if b % 2 else 3)
        for j in (0, 1):
            mm(points(b) + ["CZ0", "CZ"], [ps], T[ps][0:m, 64 + 16 * j:80 + 16 * j], T.PL[:, lo + j:lo + n:2], T.CZ[:], True, True)
        for c in (0, 1):
            for i in (0, 1):
                act([ps, "D0"], ["D0_%d_%d" % (b, c)], T.D0[0:m, 2 * b + c, 1 + i::7], T[ps][0:m, 64 + i:96:2], IDENT, scale=K,
                    bias=(2 - i) * Z0 * K)

    def rows(b):
        lo, n = BATCH[b]
        act(W2 + ["OF%d" % b, "BI", "SC"], ["D2_%d" % b], T.DR[:, lo:lo + n], T.W2[:, 0:M + 2].indirect(T.OF[:, b, 0:n // 16]),
            IDENT, scale=col("SC"), bias=col("BI"))

    def tests(b, t):
        lo, n = BATCH[b]
        out, pt = T.D1[:, lo:lo + n], T.PL[:, lo:lo + n]
        if t == 0:
            ts(["N1"] + points(b), ["D1_%d" % b], out, pt, col("N1"), None, ALU.is_lt)
        else:
            tt(W1 + points(b) + ["OF%d" % b], ["D1_%d" % b], out, T.W1[:, 0:M + 2].indirect(T.OF[:, b, 0:n // 16]), pt, ALU.is_gt)

    def sums(b, i, t):
        lo, n = BATCH[b]
        ps = "PS%d" % b
        for j in (0, 1):
            d, x = ("D2", T.D2[:, 0:n // 2]) if (i, t) == (2, 0) else ("D%d_%d" % (i, b), (T.D1 if i == 1 else T.DR)[:, lo + j:lo + n:2])
            mm([d, "C2" if i == 2 else "C1_12"], [ps], T[ps][0:n // 2, :, 56 * j:56 * j + 56], x, T["C%d" % i][:],
               i == 2 and j == 0, i == 1 and j == 1)

    def scan(b, c):
        m, ps, out = BATCH[b][1] // 2, "PS%d" % b, ("SP", "WS")[c]
        op("V", v.tensor_tensor_scan, [ps, "D0_%d_%d" % (b, c)] + ["D0_%d_s" % b] * c, ["%s%d" % (out, b)], T[out][0:m, b, :],
           T.D0[0:m, 2 * b + c, :], T[ps][0:m, c, 0:112], 0.0, ALU.subtract, ALU.max)

    def take(b):
        m = BATCH[b][1] // 2
        for j in (0, 1):
            copy(["SP%d" % b, "Z"], ["Z%d" % b], T.Z[0:m, b, 14 + j:142:16], T.SP[0:m, b, 56 * j + 6:56 * j + 56:7], 8)

    def turn(b):
        m, ex = BATCH[b][1] // 2, "Q%d" % (b % 2)
        for i in range(8):
            mm(["Z%d" % b, "IDh"], [ex], T[ex][:, 0:m // 8], T.Z[0:m, b, 14 - 2 * i:142 - 2 * i], T.IDh[0:m, i:m:8], i == 0, i == 7)

    def offsets(b):
        k, ex = BATCH[b][1] // 16, "Q%d" % (b % 2)
        act([ex], ["OF%d" % b], T.OF[:, b, 0:k], T[ex][:, 0:k], IDENT, scale=-1.0, bias=SH)

    def carry(b):
        m = BATCH[b][1] // 2
        copy(["WS%d" % b], ["D0_%d_s" % b], T.D0[0:m, 2 * b + 1, 6::7], T.WS[0:m, b, 6::7], 16)

    def round_(b):
        m = BATCH[b][1] // 2
        for i, e in enumerate((44, 37, 30)):
            ts(["WS%d" % b], ["H%d" % i], T.H[0:m, 3 * b + i], T.WS[0:m, b, 6::7], 1.5 * 2.0 ** e, 1.5 * 2.0 ** e, ALU.add, ALU.subtract)

    def pieces(b):
        lo, n = BATCH[b]
        m, ws, zs, ps = n // 2, "WS%d" % b, "ZS%d" % (b % 2), "Q%d" % (b % 2)
        for i in (0, 1):
            tt(["H%d" % i, "H%d" % (i + 1), "ZS"], [zs + "_%d" % i], T.ZS[0:m, b % 2, i::16], T.H[0:m, 3 * b + i + 1], T.H[0:m, 3 * b + i],
               ALU.subtract)
        tt([ws, "H2", "ZS"], [zs + "_2"], T.ZS[0:m, b % 2, 2::16], T.WS[0:m, b, 6::7], T.H[0:m, 3 * b + 2], ALU.subtract)
        for j in (0, 1):
            mm([zs + "_0", zs + "_1", zs + "_2", "IDb"], [ps], T[ps][:, j:n:2], T.ZS[0:m, b % 2, 128 * j:128 * j + 128], T.IDb[0:m, 0:m],
               True, True)
        if b == 0:
            act([ps], ["RV0"], T.RO[:, 0:256], T[ps][:, 0:256], COPY)
        else:
            act([ps], ["SA%d" % b], T.SA[:, lo - 256:lo - 256 + n], T[ps][:, 0:n], COPY)
            ds, lanes = SENDS[b]
            remote([(-d, "rt%d" % d, T.SA[:, slot(d) - 256:slot(d) - 160], T.RW[:, (d - 1) * RWW:(d - 1) * RWW + 96], k)
                    for d, k in zip(ds, lanes)], ["SA%d" % b])
            for d in ds:
                note((None, "rt%d" % d, total["rt%d" % d]), [], ["RV%d" % d])

    def spare(k):
        if k == 0:
            fill("Z", T.Z[:], 0.0)
            op("V", v.tensor_reduce, ["OH"], ["E012"], T.E012[:], T.OH[:, 0:3], AxisListType.X, ALU.add)
            fill("SYz", T.SY[:], 0.0)
        if k == 1:
            fill("RO", T.RO[:, 256:272], 0.0)
            ts(["G8", "E012", "SYz"], ["SY"], T.SY[:, 3:35:4], T.G8[:], col("E012"), -1.0, ALU.mult, ALU.mult)
            act(["IDf"], ["IDb"], T.IDb[:], T.IDf[:], COPY)
        if k in (6, 7):
            b = k - 6
            act(["Q2", "ZL"], ["ZL%d" % b], T.ZL[:, 142 + b:1030:16], T.Q2[:, 56 * b:56 * b + 56], IDENT, bias=96.0)
        if k in (8, 9):
            b = k - 8
            act(["Q2", "ZL", "KF2", "KF3"], ["ZO%d" % b], T.ZL[:, 14 + b:128:16], T.Q2[:, 112 + 8 * b:120 + 8 * b], IDENT,
                bias=col("KF3" if b else "KF2"))
        if 10 <= k < 18:
            d = k - 10
            for i in range(8):
                mm(["ZL0", "ZL1", "ZO0", "ZO1", "IDb"], ["Q3"], T.Q3[:, d * 16:d * 16 + 16],
                   T.ZL[:, 128 * d + 14 - 2 * i:128 * d + 142 - 2 * i], T.IDb[:, i::8], i == 0, i == 7)
        if k == 19:
            act(["Q3"], ["GQ"], T.RU[:], T.Q3[:, 0:128], COPY)

    depth(0)
    act(["N0", "IR"], ["X0B"], T.X0B[:], T.IR[:], IDENT, scale=0.0, bias=col("N0"))
    act(W2 + ["O1", "BI", "SC"], ["D2"], T.D2[:], T.W2[:, 0:M + 2].indirect(T.O1[:]), IDENT, scale=col("SC"), bias=col("BI"))
    mm(["X0B", "G87"], ["Q0"], T.Q0[:, 0:16], T.X0B[:], T.G87[:], True, True)
    for b in range(4):
        act(["Q0", "D0"], ["D0_%d_s" % b], T.D0[:, 2 * b + 1, 6::7], T.Q0[:, 0:16], COPY, scale=-1.0)
    act(["IDf"], ["IDh"], T.IDh[:], T.IDf[:], COPY)
    tests(0, 0)
    sums(0, 2, 0)
    sums(0, 1, 0)
    for b in (1, 2, 3):
        sums(b, 2, 0)
    spare(0)
    scan(0, 0)
    take(0)
    scan(0, 1)
    carry(0)
    last = 4 * (STEPS - 1)
    for k in range(1, 4 * STEPS):
        b, y, z = k % 4, (k - 1) % 4, (k - 2) % 4
        if k <= 2:
            depth(k)
        if k == 2:
            turn(0)
        if 2 <= k < last + 2:
            offsets(z)
            if k > 2:
                rows(z)
        tests(b, k // 4)
        sums(b, 1, k // 4)
        if k == 2:
            depth(3)
            rows(0)
        if 2 <= k <= last:
            scan(y, 0)
            take(y)
        if 4 <= k + 1 < 4 * STEPS:
            sums((k + 1) % 4, 2, (k + 1) // 4)
        if 2 <= k <= last:
            turn(y)
        if 2 <= k < last + 3:
            scan(y, 1)
        if 2 <= k <= last:
            carry(y)
        spare(k)
    round_(1)
    scan(2, 1)
    pieces(1)
    round_(2)
    pieces(2)
    scan(3, 1)
    ts(["GQ"], ["GO1"], T.GO[:, 16:128], T.RU[:, 16:128], 96.0, None, ALU.min)
    for b in (3, 0):
        round_(b)
        pieces(b)

    ts(["GQ"], ["GO0"], T.GO[:, 0:16], T.RU[:, 0:16], 256.0, 256.0, ALU.add, ALU.min)
    order = ((1, 0, 4), (2, 0, 4), (0, 0, 4), (3, 0, 4), (4, 0, 4), (5, 0, 4), (6, 0, 4), (7, 0, 2), (7, 2, 4))
    for i, (d, x, y) in enumerate(order):
        win = (T.RO[:] if d == 0 else T.RW[:, (d - 1) * RWW:(d - 1) * RWW + 97]).indirect(T.GO[:, d * 16 + 4 * x:d * 16 + 4 * y])
        rs, out = ["RV%d" % d, "RZ", "RO", "GO%d" % min(d, 1)], T.GD[:, d * 256 + 64 * x:d * 256 + 64 * y]
        if i % 2 == 0:
            vc(rs, ["GD%d" % i], out, win)
        else:
            act(rs, ["GD%d" % i], out, win, COPY)
        for q in range(x, y):
            mm(["GD%d" % i, "SY"], ["Q2"], T.Q2[0:32, 0:64], T.SY[:, 3 - q:35 - q], T.GD[:, d * 256 + 64 * q:d * 256 + 64 * q + 64],
               i == 0 and q == 0, i == 8 and q == 3)
    vc(["Q2"], ["Y"], T.Y[0:32, :], T.Q2[0:32, 0:64])
    dmas("dY", ["Y"], ["y"], [("S", T.y[:, :], T.Y[0:32, :])])
    for sem in sorted(total):
        if max([seen.get((q, sem), 0) for q in queue]) < total[sem]:
            g.wait_ge(T.sem[sem], total[sem])
    return
    for j in range(4):
        ts(["G8", "OH"], ["G87"], T.G87[:, 8 * j:8 * j + 8], T.G8[:], row(7), None, ALU.mult)
    vc(W1, ["N1"], T.N1[:], T.W1[:, 1:2])
    fill("SYz", T.SY[:], 0.0)

    def points(b):
        return ["PL%d" % d for d in (FIRST if b == 0 else (0, 1, 2))]

    def turn_z(b, part):
        lo, n = BATCH[b]
        ps, cut = "Q%d" % b, (96, 64)[b]
        x, y = (cut, n // 4) if part else (0, cut)
        for j in range(4):
            mm((points(b) if part else points(b)[:(4, 1)[b]]) + ["CZ0", "CZ"], [ps], T[ps][x:y, 16 * j:16 * j + 16],
               T.PL[:, lo + 4 * x + j:lo + 4 * y:4], T.CZ[:], True, True)

    def depth(b):
        ps, d0, m = "Q%d" % b, "D0_%d" % b, BATCH[b][1] // 4
        for i in (0, 1):
            act([ps, d0], [d0 + "_0"], T[d0][0:m, 0, 1 + i::7], T[ps][0:m, i:64:2], IDENT, scale=K, bias=(2 - i) * Z0 * K)
        for i in (0, 1):
            x = T[d0][0:m, 0, 1 + i::7]
            op("G", g.affine_select, [d0 + "_0"], [d0 + "_1"], T[d0][0:m, 1, 1 + i::7], x, [[0, 32]], ALU.is_ge, 0.0, 0, 0)

    def rows(b, part):
        n, of = BATCH[b][1], "OF%d" % b
        x, y = (0, CUTA) if part == 0 else (CUTA, n)
        act(W2 + [of, "BI", "SC"], ["D2_%d_%d" % (b, part)], T["D2_%d" % b][:, x:y], T.W2[:, 0:M + 2].indirect(T[of][:, x // 16:y // 16]),
            IDENT, scale=col("SC"), bias=col("BI"))

    def tests(b, t, part):
        lo, n = BATCH[b]
        cut = CUT if t else (384, 256)[b]
        x, y = (0, cut) if part == 0 else (cut, n)
        of, d1, out, pt = "OF%d" % b, "D1_%d_%d" % (b, part), T["D1_%d" % b][:, x:y], T.PL[:, lo + x:lo + y]
        if t == 0:
            ts(["N1"] + (points(b) if part else points(b)[:(4, 1)[b]]), [d1], out, pt, col("N1"), None, ALU.is_lt)
        else:
            tt(W1 + points(b) + [of], [d1], out, T.W1[:, 0:M + 2].indirect(T[of][:, x // 16:y // 16]), pt, ALU.is_gt)

    def bank(b, c, x, y):
        m = BATCH[b][1] // 4
        return ("PS%d" % b, T["PS%d" % b][0:m, 0, x:y]) if c == 0 else ("Q%d" % (3 + 2 * b), T["Q%d" % (3 + 2 * b)][0:m, x:y])

    def sums(b, i, c, first=False):
        n, d = BATCH[b][1], "D%d_%d" % (i, b)
        for j in range(4):
            ps, out = bank(b, c, 56 * j, 56 * j + 56)
            mm((["D2"] if first else [d + "_0", d + "_1"]) + ["C2" if i == 2 else "C1_12"], [ps], out,
               T.D2[:, 0:n // 4] if first else T[d][:, j:n:4], T["C%d" % i][:, c], i == 2 and j == 0, i == 1 and j == 3)

    def nodes(b):
        m, ps, d0, sp = BATCH[b][1] // 4, "PS%d" % b, "D0_%d" % b, "SP%d" % b
        for h in (0, 1):
            op("V", v.tensor_tensor_scan, [ps, d0 + "_0", "SPz%d" % b], [sp], T[sp][0:m, :, h], T[d0][0:m, 0, 112 * h:112 * h + 112],
               T[ps][0:m, 0, 112 * h:112 * h + 112], 0.0, ALU.subtract, ALU.max)
        for j in (0, 1):
            act([sp, "Z"], ["Z%d" % b], T.Z[0:m, b, 12 + j:140:2], T[sp][0:m, 56 * j + 6:56 * j + 56:7, :], COPY, scale=-1.0)

    def turn(b):
        m, ex = BATCH[b][1] // 4, "Q%d" % b
        for i in range(2):
            mm(["Z%d" % b, "IDh"], [ex], T[ex][:, 64:64 + m // 4], T.Z[0:m, b, 12 - 4 * i:140 - 4 * i], T.IDh[0:m, i:m:4], True, True)
        for i in range(4):
            mm(["Z%d" % b, "IDh"], [ex], T[ex][:, 0:m // 4], T.Z[0:m, b, 12 - 4 * i:140 - 4 * i], T.IDh[0:m, i:m:4], i == 0, i == 3)
        act([ex], ["OF%d" % b], T["OF%d" % b][:, 0:m // 4], T[ex][:, 0:m // 4], IDENT, bias=SH)

    def weights(b):
        m, d0, ws = BATCH[b][1] // 4, "D0_%d" % b, "WS%d" % b
        ps, x = bank(b, 1, 0, 224)
        op("V", v.tensor_tensor_scan, [ps, d0 + "_1", d0 + "_s"], [ws], T[ws][0:m, :], T[d0][0:m, 1, :], x, 0.0, ALU.subtract, ALU.max)

    def carry(b):
        m, d0, ws = BATCH[b][1] // 4, "D0_%d" % b, "WS%d" % b
        op("G", g.affine_select, [ws], [d0 + "_s"], T[d0][0:m, 1, 6::7], T[ws][0:m, 6::7], [[0, 32]], ALU.is_ge, 0.0, 0, 0)

    def send(ds, tag, lanes):
        at = [slot(d) if d in FIRST else slot(d) - 256 for d in ds]
        remote([(-d, "rt%d" % d, T.SA[:, x:x + 96], T.RW[:, (d - 1) * RWW:(d - 1) * RWW + 96], n) for d, x, n in zip(ds, at, lanes)], [tag])
        for d in ds:
            note((None, "rt%d" % d, total["rt%d" % d]), [], ["RV%d" % d])

    def pieces(b):
        n = BATCH[b][1]
        m, ws, h, ps = n // 4, "WS%d" % b, T["H%d" % b], "Q%d" % (4 - 2 * b)
        for i, e in enumerate((44, 37, 30)):
            ts([ws], ["H%d_%d" % (b, i)], h[0:m, i], T[ws][0:m, 6::7], 1.5 * 2.0 ** e, 1.5 * 2.0 ** e, ALU.add, ALU.subtract)
        for i in (0, 1):
            tt(["H%d_%d" % (b, i), "H%d_%d" % (b, i + 1), "ZS"], ["ZS_%d" % i], T.ZS[0:m, i::16], h[0:m, i + 1], h[0:m, i], ALU.subtract)
        tt([ws, "H%d_2" % b, "ZS"], ["ZS_2"], T.ZS[0:m, 2::16], T[ws][0:m, 6::7], h[0:m, 2], ALU.subtract)
        for j in range(4):
            mm(["ZS_0", "ZS_1", "ZS_2", "IDb"], [ps], T[ps][:, j:n:4], T.ZS[0:m, 128 * j:128 * j + 128], T.IDb[0:m, 0:m], True, True)
        if b == 0:
            act([ps], ["SA0"], T.SA[:, 0:384], T[ps][:, 0:384], COPY)
            send(FIRST[:4], "SA0", (4, 4, 4, 4))
            act([ps], ["SA2"], T.SA[:, 384:480], T[ps][:, 384:480], COPY)
        else:
            act([ps], ["SA1"], T.SA[:, 480:672], T[ps][:, 256:448], COPY)
            send((1, 2, 7), "SA1", (4, 4, 8))
            act([ps], ["RV0"], T.RO[:, 0:256], T[ps][:, 0:256], COPY)

    def spare(s):
        if s == 1:
            fill("RO", T.RO[:, 256:272], 0.0)
            ts(["G8", "E012", "SYz"], ["SY"], T.SY[:, 3:35:4], T.G8[:], col("E012"), -1.0, ALU.mult, ALU.mult)
        if s in (1, 2):
            whole("ZL", T.ZL[:, 520 * (s - 1):520 * s], 520, 0)
        if s == 3:
            whole("ZS", T.ZS[:], 512, 0)
        if s in (4, 5):
            b = s - 4
            act(["Q2", "ZL"], ["ZL%d" % b], T.ZL[:, 142 + b:1030:16], T.Q2[:, 56 * b:56 * b + 56], IDENT, bias=96.0)
            act(["Q2", "ZL", "KF2", "KF3"], ["ZO%d" % b], T.ZL[:, 14 + b:128:16], T.Q2[:, 112 + 8 * b:120 + 8 * b], IDENT,
                bias=col("KF3" if b else "KF2"))
        if s in (6, 7, 8, 9):
            for d in (2 * s - 12, 2 * s - 11):
                for i in range(8):
                    mm(["ZL0", "ZL1", "ZO0", "ZO1", "IDb"], ["Q4"], T.Q4[:, d * 16:d * 16 + 16],
                       T.ZL[:, 128 * d + 14 - 2 * i:128 * d + 142 - 2 * i], T.IDb[:, i::8], i == 0, i == 7)
        if s == 10:
            act(["Q4"], ["GQ"], T.RU[:], T.Q4[:, 0:128], COPY)

    act(W2 + ["OF1", "BI", "SC"], ["D2"], T.D2[:], T.W2[:, 0:M + 2].indirect(T.OF1[:, 0:8]), IDENT, scale=col("SC"), bias=col("BI"))
    act(["N0", "IR"], ["X0B"], T.X0B[:], T.IR[:], IDENT, scale=0.0, bias=col("N0"))
    act(["IDf"], ["IDh"], T.IDh[:], T.IDf[:], COPY)
    act(["IDf"], ["IDb"], T.IDb[:], T.IDf[:], COPY)
    turn_z(1, 0)
    for b in (0, 1):
        for c in (0, 1):
            sums(b, 2, c, True)
    mm(["X0B", "G87"], ["Q4"], T.Q4[:, 0:32], T.X0B[:], T.G87[:], True, True)
    for b in (0, 1):
        act(["Q4", "D0_%d" % b], ["D0_%d_s" % b], T["D0_%d" % b][:, 1, 6::7], T.Q4[:, 0:32], COPY, scale=-1.0)
    turn_z(0, 0)
    turn_z(0, 1)
    depth(0)
    tests(1, 0, 0)
    tests(0, 0, 0)
    tests(0, 0, 1)
    fill("Z", T.Z[:], 0.0)
    op("V", v.tensor_reduce, ["OH"], ["E012"], T.E012[:], T.OH[:, 0:3], AxisListType.X, ALU.add)
    sums(0, 1, 0)
    turn_z(1, 1)
    sums(0, 1, 1)
    for s in range(1, 2 * STEPS + 1):
        b, t = s % 2, s // 2
        o, u = 1 - b, (s - 1) // 2
        more = u < STEPS - 1
        if 1 < s < 2 * STEPS:
            tests(b, t, 0)
        if more:
            nodes(o)
            if s == 1:
                depth(1)
        else:
            weights(o)
        if 1 < s < 2 * STEPS:
            rows(b, 1)
        if more:
            turn(o)
            rows(o, 0)
        if s < 2 * STEPS:
            tests(b, t, 1)
            for c in (0, 1) if t < STEPS - 1 else (1,):
                if s > 1:
                    sums(b, 2, c)
                sums(b, 1, c)
        if more:
            weights(o)
            carry(o)
            spare(s)
        else:
            pieces(o)

    ts(["GQ"], ["GO0"], T.GO[:, 0:16], T.RU[:, 0:16], 256.0, 256.0, ALU.add, ALU.min)
    ts(["GQ"], ["GO1"], T.GO[:, 16:128], T.RU[:, 16:128], 96.0, None, ALU.min)
    order = ((0, 0, 4), (3, 0, 4), (4, 0, 4), (5, 0, 4), (6, 0, 4), (7, 0, 4), (1, 0, 4), (2, 0, 2), (2, 2, 4))
    for i, (d, x, y) in enumerate(order):
        win = (T.RO[:] if d == 0 else T.RW[:, (d - 1) * RWW:(d - 1) * RWW + 97]).indirect(T.GO[:, d * 16 + 4 * x:d * 16 + 4 * y])
        rs, out = ["RV%d" % d, "RZ", "RO", "GO%d" % min(d, 1)], T.GD[:, d * 256 + 64 * x:d * 256 + 64 * y]
        if i % 2 == 0:
            vc(rs, ["GD%d" % i], out, win)
        else:
            act(rs, ["GD%d" % i], out, win, COPY)
        for q in range(x, y):
            mm(["GD%d" % i, "SY"], ["Q0"], T.Q0[0:32, 0:64], T.SY[:, 3 - q:35 - q], T.GD[:, d * 256 + 64 * q:d * 256 + 64 * q + 64],
               i == 0 and q == 0, i == 8 and q == 3)
    vc(["Q0"], ["Y"], T.Y[0:32, :], T.Q0[0:32, 0:64])
    dmas("dY", ["Y"], ["y"], [("S", T.y[:, :], T.Y[0:32, :])])
    for sem in sorted(total):
        if max([seen.get((q, sem), 0) for q in queue]) < total[sem]:
            g.wait_ge(T.sem[sem], total[sem])
